import numpy as np, ml_dtypes
CORES = [66,74,82,90,194,202,210,218]
N = 8
BF = ml_dtypes.bfloat16
def gentries(a):
    return np.ascontiguousarray(a.reshape(8, 16, -1).transpose(0, 2, 1)).reshape(8, -1)
def gtable(e):
    e = np.asarray(e); return np.ascontiguousarray(e.reshape(8, -1, 16).transpose(0, 2, 1)).reshape(128, -1).astype(np.int32)
V, L, RO, LAM, MU, STEP = 1024, 4, 2, 9, 4, 4
def perms(rng):
    return np.argsort(rng.random((N, 8, V)), axis=-1)
def parts(rng):
    sh = (N, 8, 16, V)
    return rng.integers(0, 32, sh, dtype=np.int32), rng.integers(2, 62, sh, dtype=np.int32), rng.integers(0, 100, sh, dtype=np.int32), perms(rng), perms(rng)
def pick(t, ix):
    return np.stack([np.stack([np.take(t[q, g], ix[q, g], axis=-1) for g in range(8)]) for q in range(N)])
def edges(h, a, b):
    hp = np.roll(h, 1, axis=0)
    return np.abs(h - pick(hp, a)), np.abs(h - pick(hp, b))
def forest(f, p, a, b, da, db):
    won = []
    for t in range(L):
        if t: p = np.roll(p, 1, axis=0)
        c0 = pick(p, a) + da; c1 = pick(p, b) + db
        w = np.add.reduce(c1 < c0, axis=2, dtype=np.int32) >= 9
        p = np.where(w[:, :, None, :], c1, c0) + f
        won.append(w)
    return p, won
def entered(wrong, won, a, b):
    m = wrong; u = np.zeros_like(m)
    for t in range(L - 1, 0, -1):
        x = np.zeros_like(m); y = np.zeros_like(m)
        np.put_along_axis(x, a, m & ~won[t], 2); np.put_along_axis(y, b, m & won[t], 2)
        m = np.roll(x | y, -1, axis=0); u = u | m
    return u
def bar(h, e, p, a, b):
    da, db = edges(h, a, b); c, won = forest(e, p, a, b, da, db)
    return np.ascontiguousarray(np.sort(c, axis=2)[:, :, 7, :]).astype(np.int64)
def pack(h, e, p, z, a, b):
    w = lambda x: np.ascontiguousarray(x.reshape(N, 128, V)).astype(np.float32).astype(BF)
    return {"hf": w(h), "toll": w(e), "p0": w(p), "lim": np.clip(z, 0, 1023).astype(np.int32), "sa": np.stack([gtable(x) for x in a]), "sb": np.stack([gtable(x) for x in b])}
def near(rng, q, share, under, over):
    return np.where(rng.random(q.shape) < share, q - 1 - rng.integers(0, under, q.shape), q + rng.integers(0, over, q.shape))
def classes(rng, to):
    x = np.zeros(V, np.int64)
    for c in range(8): x[c::8] = 8 * rng.permutation(V >> 3) + to[c]
    return x
def setup_inputs(rng):
    h, e, p, a, b = parts(rng)
    return pack(h, e, p, near(rng, bar(h, e, p, a, b), 0.2, 12, 24), a, b)
def setup_inputs_spread(rng):
    h, e, p, a, b = parts(rng); col = (N, 8, 1, V)
    h = np.minimum(np.exp2(2 + 3 * rng.random(col)) * rng.random(h.shape), 31).astype(np.int32)
    e = np.minimum(64 * rng.random(col) ** 2 * rng.random(e.shape) + rng.integers(0, 8, e.shape), 63).astype(np.int32)
    p = np.minimum(np.exp2(3 + 5 * rng.random(col)) * rng.random(p.shape), 255).astype(np.int32)
    h[:, :, :, ::5] = rng.integers(0, 32, h[:, :, :, ::5].shape); e[:, :, :, ::3] = rng.integers(0, 64, e[:, :, :, ::3].shape); p[:, :, :, ::7] = rng.integers(0, 256, p[:, :, :, ::7].shape)
    return pack(h, e, p, near(rng, bar(h, e, p, a, b), 0.3, 60, 90), a, b)
def setup_inputs_ends(rng):
    sh = (N, 8, 16, V)
    h = 31 * rng.integers(0, 2, sh, dtype=np.int32); e = 63 * rng.integers(0, 2, sh, dtype=np.int32); p = 255 * rng.integers(0, 2, sh, dtype=np.int32)
    z = 1023 * (rng.random((N, 8, V)) >= 0.25).astype(np.int64)
    a = np.zeros((N, 8, V), np.int64); b = np.zeros((N, 8, V), np.int64)
    hi = np.concatenate([np.arange(16), np.arange(V - 16, V)]); lo = np.arange(16, 48); mid = np.arange(48, V - 16)
    for q in range(N):
        for g in range(8):
            for s in (a, b):
                for x in (hi, lo, mid): s[q, g, x] = x[rng.permutation(len(x))]
            if g % 2: a[q, g, hi] = hi[::-1]; b[q, g, hi] = hi
            if g == 5: a[q, g, lo] = lo[::-1]; b[q, g, lo] = lo
    h[:, :, :, hi] = 31 * (np.arange(N) % 2)[:, None, None, None]; e[:, :, :, hi] = 63; p[:, :, :, hi] = 255
    h[:, :, :, lo] = 0; e[:, :, :, lo] = 0; p[:, :, :, lo] = 0
    z[:, :, V - 1] = 0
    p[:, 5, :, lo] = 1
    z[:, 5, lo] = 1023; z[:, 7, hi[1:31]] = 1023
    for i in range(16):
        x, y = rng.integers(0, 2, 2)
        z[i % N, 5, lo[31 - i if x else i]] = 0
        if i: z[i % N, 7, hi[31 - i if y else i]] = 254 + 94 * L
    return pack(h, e, p, z, a, b)
def setup_inputs_corners(rng):
    h, e, p, a, b = parts(rng); w = rng.permutation(8); k = np.arange(V)
    b[:, w[2]] = a[:, w[2]]
    b[:, w[3]] = a[:, w[3]] ^ 1; e[:, w[3]] = 63 * (k % 2)
    a[:, w[4]] = k; b[:, w[4]] = V - 1 - k
    p[:, w[5]] = rng.integers(0, 256, (N, 1, 1)); e[:, w[5]] = rng.integers(0, 64, (N, 1, 1)); h[:, w[5]] = rng.integers(0, 32, (N, 16, 1))
    lev = rng.integers(0, 2, (N, 1, V)); cut = 7 + rng.integers(0, 3, (N, 1, V))
    p[:, w[6]] = np.where(np.arange(16)[None, :, None] < cut, 10 * lev, 10 - 10 * lev); e[:, w[6]] = 20; h[:, w[6]] = rng.integers(0, 32, (N, 16, 1))
    e[:, w[7]] = 63 * rng.integers(0, 2, (N, 16, V))
    q = bar(h, e, p, a, b); z = q + rng.integers(-1, 2, q.shape)
    odd = (np.arange(N) % 2)[:, None]
    z[:, w[0]] = np.where(odd == 0, 1023, 0); z[:, w[1]] = np.where(odd == 0, 0, 1023)
    return pack(h, e, p, z, a, b)
def setup_inputs_calm(rng):
    h, e, p, a, b = parts(rng); sh = h.shape
    low = (rng.random(sh) < 0.25).astype(np.int64); low[:, 6, ::2] = rng.integers(0, 5, low[:, 6, ::2].shape)
    i = rng.permutation(16)
    for j, (x, y) in enumerate(((3, 0), (5, 5), (5, 4))): low[::2, 3, i[j]] = x; low[1::2, 3, i[j]] = y
    h = np.where((np.arange(N) % 2 == 1)[:, None, None, None], 31 - low, low).astype(np.int32); p = rng.integers(0, 4, sh, dtype=np.int32)
    base = 60 * ((np.arange(N)[:, None] + np.arange(8)[None, :]) % 2)
    base[:, 5] = 60; base[:, 7] = 60; p[:, 5] += 252; p[:, 7] += 128
    e = (base[:, :, None, None] + rng.integers(0, 4, sh)).astype(np.int32)
    z = bar(h, e, p, a, b)
    for q in range(N):
        for g in range(4): z[q, g, rng.permutation(V)[:g]] -= 1
    z[:, 4:] -= (rng.random((N, 4, V)) < 0.15)
    return pack(h, e, p, z, a, b)
def setup_inputs_crowd(rng):
    h, e, p, a, b = parts(rng); k = np.arange(V); first = k[(k & 2) == 0]; k8 = k & 7
    gap = np.array([3, LAM + MU, LAM + MU + 1, 30, 60, 60, 60, 60])[None, :, None, None]; odd = (k % 2)[None, None, None, :]
    h[:, :4] = rng.integers(0, 32, (N, 4, 16, 1)); h[:, 4:] = rng.integers(0, 11, (N, 4, 16, V))
    e = (rng.integers(0, 4, (N, 8, 16, 1)) + gap * odd).astype(np.int32); p = (rng.integers(20, 100, (N, 8, 16, 1)) + gap * odd).astype(np.int32)
    z = np.zeros((N, 8, V), np.int64)
    for q in range(N):
        for g in range(6):
            c = 2 * rng.permutation(V // 2); o = rng.integers(0, 2, V // 2)
            a[q, g, first] = c + o; a[q, g, first + 2] = c + 1 - o
            if g % 2:
                i = 2 * int(rng.integers(0, V // 2)); x = e[q, g]; x[:, [i, i + 1]] = x[:, [i + 1, i]]
                z[q, g, int(rng.integers(0, V))] = 1023
    b[:, :6] = a[:, :6] ^ 1
    step = np.array([0, 0, 0, 25, 25, 25, 25, 55])[k8]
    h[:, 6] = rng.integers(0, 30, (1, 16, 1)) + 2 * (k8 == 4)
    e[:, 6] = rng.integers(0, 4, (N, 16, 1)) + step; p[:, 6] = rng.integers(20, 100, (N, 16, 1)) + step
    h[:, 7] = rng.integers(0, 28, (1, 16, 1)) + (k8 >> 1)
    e[:, 7] = rng.integers(10, 51, (N, 16, 1)); p[:, 7] = rng.integers(20, 100, (N, 16, 1))
    h[:, 4] = rng.integers(0, 11, (N, 16, 1)); p[:, 4] = rng.integers(20, 100, (N, 16, 1))
    e[:, 4] = rng.integers(20, 41, (N, 16, 1)) + np.where(k8 < 6, k8 & 1, 0)
    for q in range(N):
        a[q, 4] = classes(rng, (2, 4, 6, 1, 3, 5, 0, 7)); b[q, 4] = classes(rng, (3, 5, 1, 7, 0, 2, 4, 6))
        a[q, 6] = classes(rng, (2, 0, 4, 1, 6, 7, 5, 3)); b[q, 6] = classes(rng, (7, 3, 0, 5, 1, 2, 6, 4))
        a[q, 7] = classes(rng, (0, 1, 2, 3, 4, 5, 6, 7)); b[q, 7] = classes(rng, (2, 3, 4, 5, 6, 7, 0, 1))
    z[:, 4] = np.where(k8 < 6, bar(h, e, p, a, b)[:, 4] - 1, 1023)
    return pack(h, e, p, z, a, b)
def check_ranges(d):
    bad = []
    for k, lo, hi in (("hf", 0, 31), ("toll", 0, 63), ("p0", 0, 255), ("lim", 0, 1023), ("sa", 0, V - 1), ("sb", 0, V - 1)):
        x = np.asarray(d[k]).astype(np.float64)
        if not np.all((x >= lo) & (x <= hi) & (x == np.floor(x))): bad.append("range of " + k)
    for k in ("sa", "sb"):
        if any(np.any(np.sort(gentries(np.asarray(d[k])[q]), axis=1) != np.arange(V)) for q in range(N)): bad.append("numbers of " + k + " not each once")
    return bad
def reference(hf, toll, p0, lim, sa, sb):
    whole_ = lambda x: x.astype(np.float32).astype(np.int32).reshape(N, 8, 16, V)
    h = whole_(hf); e = whole_(toll); p = whole_(p0); z = lim.astype(np.int32)[:, :, None, :]
    a = np.stack([gentries(x) for x in sa]).astype(np.int64); b = np.stack([gentries(x) for x in sb]).astype(np.int64)
    da, db = edges(h, a, b); tab = np.exp(-0.125 * np.arange(32)); gain = np.zeros((N, 8, 16, V))
    ident = np.broadcast_to(np.arange(V), (N, 8, V))
    for rnd in range(RO):
        last, w1 = forest(e, p, a, b, da, db)
        wrong = np.add.reduce(last > z, axis=2, dtype=np.int32) >= 9
        m1 = entered(wrong, w1, a, b).astype(np.int32)
        f = e + (LAM * m1 + MU * np.roll(m1, -1, axis=1))[:, :, None, :]
        unused, w2 = forest(f, p, a, b, da, db)
        m2 = entered(wrong, w2, a, b).astype(np.int32)
        na = ident; nb = ident; fa = h; fb = h; acc = np.zeros((N, 8, 16, V))
        for t in range(L - 1, 0, -1):
            na = np.roll(pick(np.where(w1[t], b, a), na), -1, axis=0); nb = np.roll(pick(np.where(w2[t], b, a), nb), -1, axis=0)
            oa = np.roll(fa, -1, axis=0); ob = np.roll(fb, -1, axis=0)
            fa = pick(h, na); fb = pick(h, nb)
            acc = np.roll(acc, -1, axis=0) + tab[np.abs(fa - ob)] + 0.5 * tab[np.abs(fb - oa)]
        gain = gain + acc
        e = np.clip(e + STEP * (m1 - m2)[:, :, None, :], 0, 63)
    return {"gain": gain.reshape(N, 128, V).astype(np.float32), "tollout": e.reshape(N, 128, V).astype(np.float32)}

def check_inputs(d):
    bad = list(check_ranges(d))
    if not bad:
        for name, y in reference(**d).items():
            for q in range(N):
                v = np.abs(np.asarray(y[q], np.float64)); s = np.sqrt(np.mean(v * v))
                if v.max() > 4 * s or s < 2.0 ** -4: bad.append('%s of rank %d is uneven or too small' % (name, q))
    return bad

@@ -1,0 +1,682 @@
+import math
+from concourse.bass import DstId, RemoteDMATransfer
+from concourse.mybir import AluOpType as ALU, ActivationFunctionType as AF
+
+N = 8
+V = 1024
+H = 512
+F32, BF, F16, I32, U16 = "float32", "bfloat16", "float16", "int32", "uint16"
+
+
+def sb(n, d):
+    return ("sbuf", [128, n], d)
+
+
+SCRATCH = {
+    "s_i": ("dram", [8, 128, 32], I32), "l_i": ("dram", [8, 128, 32], I32),
+    "s_h": ("dram", [8, 128, 128], BF), "l_h": ("dram", [8, 128, 128], BF),
+    "s_pe": ("dram", [8, 128, 256], BF), "l_pe": ("dram", [8, 128, 256], BF),
+    "s_v": ("dram", [8, 128, 16], I32), "l_v": ("dram", [8, 128, 16], I32),
+    "s_t": ("dram", [8, 128, 128], BF), "l_t": ("dram", [8, 128, 128], BF),
+    "iot": sb(V, F32), "g16": sb(256, F32), "pci": sb(8, I32), "pcf": sb(8, F32), "v16": sb(64, F32),
+    "idp": sb(256, BF), "idn": sb(256, BF), "id13": sb(256, BF), "id8": sb(128, BF), "id32": sb(128, BF),
+    "idf": sb(256, F32), "ihp": sb(128, F16), "ihn": sb(128, F16), "ih1": sb(128, F16), "ct": sb(768, BF),
+    "x0": sb(V, F32), "x1": sb(V, F32), "rm": sb(H, F32),
+    "t2a": sb(144, BF), "t2b": sb(144, BF), "t2f": sb(144, F32), "bo": sb(176, BF), "m16": sb(16, F32),
+    "xt": sb(16 * 176, BF), "ones": sb(H, BF), "m85": sb(128, BF),
+    "zi": sb(64, F32), "cc": sb(64, F32), "off": sb(64, F32),
+    "oi": sb(128, I32), "ou": sb(128, U16), "ov": sb(128, I32), "li": sb(192, I32), "lf": sb(192, F32),
+    "lu": sb(512, U16), "asx": sb(256, F32), "vi": sb(128, I32), "vf": sb(128, F32), "lv": sb(384, U16),
+    "zh": sb(64, BF), "zt": sb(64, F32), "zl": sb(64, BF),
+    "t1": sb(128, F32), "t2": sb(128, F32), "t3": sb(64, F32), "ix": sb(128, U16), "adq": sb(256, F32), "gz": sb(H, F32), "eb": sb(2 * V, F32), "wc": sb(2 * V, F32), "ixa": sb(64, U16), "ixb": sb(64, U16),
+    "hl": sb(V, BF), "hp": sb(V, BF), "ha": sb(V, BF), "hb": sb(V, BF), "da": sb(V, BF),
+    "dd": sb(4 * V, BF), "hab": sb(2 * V, BF), "e0": sb(V, BF), "e1": sb(V, BF), "e2": sb(V, BF),
+    "wa": sb(2 * V, F32), "wb": sb(2 * V, F32), "qh": sb(V, F16), "nn": sb(V, F32), "na": sb(V, F32), "nb": sb(V, F32),
+    "lt": sb(4 * V, BF), "sw": sb(2 * V, BF), "wt": sb(V, BF), "wr": sb(V, BF),
+    "sa1": sb(V, BF), "sa2": sb(V, BF), "g0": sb(3 * V, BF), "g1": sb(3 * V, BF),
+    "u4": sb(256, BF), "u9": sb(64, BF), "un": sb(128, BF), "mk": sb(64, BF), "dl": sb(64, BF),
+    "la": sb(V, F16), "lb": sb(V, F16), "ta": sb(V, BF), "tb": sb(V, BF), "fa": sb(V, BF), "fb": sb(V, BF),
+    "acc": sb(V, F32),
+}
+for _k in range(8):
+    SCRATCH["b%d" % _k] = ("psum", [128, H], F32)
+PIECES = ((0, 512), (512, 768), (768, 1024))
+for _k, (_lo, _hi) in enumerate(PIECES):
+    SCRATCH["s_g%d" % _k] = ("dram", [8, 128, (_hi - _lo) // 8], F32)
+    SCRATCH["l_g%d" % _k] = ("dram", [8, 128, (_hi - _lo) // 8], F32)
+NDS = 80
+SEMAPHORES = ["cv", "cs", "cp", "cg"] + ["d%d" % k for k in range(NDS)]
+
+CY, PEC, GAM, FIX, LAT = 1.0, 0.5, 1.55, 60.0, 90.0
+OPT = dict(dma_add=True, wm=("pp", "pp", "pp"), wl=("ps", "ps", "ps"), both=True, zs=True, tail_dma=0, seed=10, noise=400.0, split=True, wch=((0, 512), (512, 1024)), strip_s=False, look=0.5, margin=1500.0, pieces=((0, 512), (512, 768), (768, 1024)))
+
+
+def price(v, fix=FIX, cy=CY, gam=GAM, pec=PEC):
+    if isinstance(v, tuple):
+        return fix * v[0] + cy * (v[1] + gam * v[2]) + pec * v[3]
+    return v
+
+
+def build():
+    ops = []
+    last = {}
+    nsem = [0]
+
+    def add(eng, fn, rd, wr, cost, kind="c", after=(), lat=0.0):
+        i = len(ops)
+        deps = {}
+        for j in after:
+            deps[j] = True
+        for (rs, w) in ((rd, False), (wr, True)):
+            for r in rs:
+                nm, lo, hi = r[0], r[1], r[2]
+                bank = SCRATCH.get(nm, ("x",))[0] == "psum"
+                if bank:
+                    lo, hi = 0, H
+                for (l2, h2, j, w2) in last.get(nm, ()):
+                    if l2 < hi and lo < h2 and j != i:
+                        same = ops[j]["eng"] == eng and kind == "c" and ops[j]["kind"] == "c"
+                        if w2 and not w:
+                            deps[j] = True
+                        elif w or w2 or (bank and not same):
+                            deps[j] = deps.get(j, False) or not (same and eng == "p")
+        for (rs, w) in ((rd, False), (wr, True)):
+            for r in rs:
+                nm, lo, hi = r[0], r[1], r[2]
+                bank = SCRATCH.get(nm, ("x",))[0] == "psum"
+                if bank:
+                    lo, hi = 0, H
+                lst = last.setdefault(nm, [])
+                if w:
+                    lst[:] = [e for e in lst if not (lo <= e[0] and e[1] <= hi)]
+                lst.append((lo, hi, i, w))
+        o = dict(eng=eng, fn=fn, deps=deps, vec=cost, cost=price(cost), kind=kind, lat=lat, nm=(wr or rd)[0][0] if (wr or rd) else "")
+        if kind != "c":
+            o["sem"] = "d%d" % nsem[0]
+            nsem[0] += 1
+        ops.append(o)
+        return i
+
+    def A(T, r):
+        if isinstance(r, (int, float)):
+            return r
+        nm, lo, hi = r[0], r[1], r[2]
+        st = r[3] if len(r) > 3 else 1
+        p = r[4] if len(r) > 4 else 128
+        return T[nm][0:p, lo:hi:st] if st != 1 else T[nm][0:p, lo:hi]
+
+    def n_(r):
+        st = r[3] if len(r) > 3 else 1
+        return (r[2] - r[1] + st - 1) // st
+
+    def two(r):
+        return SCRATCH[r[0]][2] in (BF, F16, U16)
+
+    def ps(r):
+        return SCRATCH[r[0]][0] == "psum"
+
+    def src(T, x, idx):
+        return A(T, x) if idx is None else A(T, x).indirect(A(T, idx))
+
+    def aps(*xs):
+        return [x for x in xs if isinstance(x, tuple)]
+
+    def vcost(out, x, idx, base):
+        if idx is not None:
+            return (1, 0.0, n_(out), 0.0)
+        return (1, max(64.0, n_(out) * base), 0.0, 0.0)
+
+    def tt(out, x, y, op, idx=None):
+        return add("v", lambda g, T, c: g.vector.tensor_tensor(A(T, out), src(T, x, idx), A(T, y), op),
+                   aps(x, y, idx), [out], vcost(out, x, idx, 1.0 if ps(x) or ps(y) else 2.0))
+
+    def ts(out, x, s1, op0, s2=None, op1=None, idx=None):
+        def fn(g, T, c):
+            if op1 is None:
+                return g.vector.tensor_scalar(A(T, out), src(T, x, idx), A(T, s1), None, op0)
+            return g.vector.tensor_scalar(A(T, out), src(T, x, idx), A(T, s1), A(T, s2), op0, op1)
+        return add("v", fn, aps(x, s1, s2, idx), [out], vcost(out, x, idx, 0.5 if two(out) and two(x) else 1.0))
+
+    def cp(out, x, idx=None):
+        return add("v", lambda g, T, c: g.vector.tensor_copy(A(T, out), src(T, x, idx)),
+                   aps(x, idx), [out], vcost(out, x, idx, 0.5 if two(out) and two(x) else 1.0))
+
+    def act(out, x, f, bias=0.0, scale=1.0, idx=None):
+        return add("s", lambda g, T, c: g.scalar.activation(A(T, out), src(T, x, idx), f, bias=A(T, bias), scale=A(T, scale)),
+                   aps(x, idx, bias, scale), [out], vcost(out, x, idx, 1.0))
+
+    def mm(items):
+        def fn(g, T, c):
+            ins = None
+            for (o, l, r, s0, s1) in items:
+                ins = g.tensor.matmul(A(T, o), A(T, l), A(T, r), s0, s1)
+            return ins
+        cost = (0.5, 0.0, 0.0, sum(max(64, n_(r)) * (1 if two(r) else 4) for (o, l, r, s0, s1) in items))
+        rd = []
+        for (o, l, r, s0, s1) in items:
+            rd += [l, r]
+        return add("p", fn, rd, [items[0][0]], cost)
+
+    def dma(q, fn, rd, wr, nbytes):
+        return add(q, fn, rd, wr, 60.0 if q != "g" else 400.0, kind="d", lat=1900.0 + nbytes / 180.0)
+
+    def gop(fn, wr, n):
+        return add("g", fn, [], wr, 130.0 + 2 * CY * n)
+
+    def send(pairs, rd, land, nbytes, one=False):
+        k = len(ops)
+
+        def fn(g, T, c):
+            topo, core = c["topo"], c["core"]
+            trs = []
+            tot = 0
+            for n, (d, s, t) in enumerate(pairs(T, c["q"])):
+                dc = T.cores[d]
+                rid, pid = topo.addr(dc, core)
+                en = topo.engines(core, dc)
+                m = topo.mask(core, dc) if one else 1 << en[n]
+                tot += len(en) if one else 1
+                trs.append(RemoteDMATransfer(dst_ids=[DstId(rid=rid, pnc=pid)], dma_engine_mask=m,
+                                             remote_sem=T.sem[ops[k + 1]["sem"]], src=s, dst=t))
+            g.remote_dma_fused(trs, local_sem=T.sem[ops[k]["sem"]])
+            return tot
+        i = add("g", fn, rd, [], 500.0, kind="r", lat=2000.0 + nbytes / 20.0)
+        j = add(None, None, [], land, 0.0, kind="a")
+        ops[j]["from"] = i
+        ops[j]["one"] = one
+        return j
+
+    def D(nm, k=0):
+        return (nm, k, k + 1)
+
+    def a2a(s, l, nbytes, base=0):
+        k = base // 8
+        send(lambda T, q: [(d % N, T[s][base + d % N], T[l][base + q]) for d in range(q + 1, q + N)],
+             [D(s, k)], [D(l, 2 * k)], nbytes)
+
+    def own(qn, s, l, nbytes):
+        dma(qn, lambda e, T, c: [e.dma_start(T[l][c["q"]], T[s][c["q"]])], [D(s)], [D(l, 1)], nbytes)
+
+    HS = ((0, H), (H, V))
+
+    def ch(nm, h, base=0):
+        return (nm, base + h * H, base + h * H + H)
+
+    def bk(k, n=H, lo=0):
+        return ("b%d" % k, lo, lo + n)
+
+    def rot(nm, t):
+        return (nm, 16 * t, 16 * t + 128)
+
+    dma("y", lambda e, T, c: [e.dma_start(T.s_i[:, 0:32, :], T.sa[:]), e.dma_start(T.s_i[:, 64:96, :], T.lim[:])], [], [("s_i", 0, 1)], 8e4)
+    dma("a", lambda e, T, c: [e.dma_start(T.s_i[:, 32:64, :], T.sb[:]), e.dma_start(T.s_i[:, 96:128, :], T.lim[:])], [], [("s_i", 1, 2)], 8e4)
+    dma("y", lambda e, T, c: [e.dma_start(T.s_h[:], T.hf[:])], [], [D("s_h")], 26e4)
+    dma("a", lambda e, T, c: [e.dma_start(T.oi[:, 0:64], T.sa[:]), e.dma_start(T.oi[:, 64:128], T.sb[:])], [], [("oi", 0, 128)], 8e4)
+    dma("y", lambda e, T, c: [e.dma_start(T.s_pe[:, 0:64, :], T.p0[:])], [], [("s_pe", 0, 1)], 26e4)
+    dma("a", lambda e, T, c: [e.dma_start(T.s_pe[:, 64:128, :], T.toll[:])], [], [("s_pe", 1, 2)], 26e4)
+    gop(lambda g, T, c: g.iota(T.pci[:, 0:1], [[0, 1]], 0, 1), [("pci", 0, 1)], 1)
+    gop(lambda g, T, c: g.iota(T.iot[:, 0:144], [[1, 144]], 0, 0, allow_small_or_imprecise_dtypes=True), [("iot", 0, 144)], 144)
+    gop(lambda g, T, c: g.iota(T.g16[:, 0:176], [[1, 11], [0, 16]], 0, 0, allow_small_or_imprecise_dtypes=True), [("g16", 0, 176)], 176)
+    for k in range(144, V, 144):
+        w = min(144, V - k)
+        act(("iot", k, k + w), ("iot", 0, w), AF.Identity, bias=float(k))
+    send(lambda T, q: [(d % N, T.s_i[d % N], T.l_i[q]) for d in range(q + 1, q + N)], [("s_i", 0, 2)], [D("l_i")], 16e3)
+    dma("y", lambda e, T, c: [e.dma_start(T.l_i[c["q"]], T.s_i[c["q"]])], [("s_i", 0, 2)], [D("l_i", 1)], 16e3)
+    a2a("s_h", "l_h", 32e3)
+    own("y", "s_h", "l_h", 32e3)
+    send(lambda T, q: [(d % N, T.s_pe[d % N], T.l_pe[q]) for d in range(q + 1, q + N)], [("s_pe", 0, 2)], [D("l_pe")], 64e3)
+    dma("y", lambda e, T, c: [e.dma_start(T.l_pe[c["q"]], T.s_pe[c["q"]])], [("s_pe", 0, 2)], [D("l_pe", 1)], 64e3)
+
+    P, PD, PM, PT, P0, PQ = [("pcf", k, k + 1) for k in range(6)]
+    ts(("pci", 1, 2), ("pci", 0, 1), 4, ALU.arith_shift_right)
+    ts(("pci", 2, 3), ("pci", 0, 1), 15, ALU.bitwise_and)
+    cp(("pcf", 0, 3), ("pci", 0, 3))
+    ts(PT, PD, 16.0, ALU.mult, 15.0, ALU.add)
+    ts(P0, PM, 0.0, ALU.is_equal)
+    cp(("ou", 0, 128), ("oi", 0, 128))
+    I128, I144 = ("iot", 0, 128), ("iot", 0, 144)
+    ts(("t2f", 0, 144), I144, PT, ALU.is_equal, P0, ALU.mult)
+    for k in range(2):
+        if k == 0:
+            add("v", lambda g, T, c: g.vector.tensor_copy(T.wa[:, 0:V].indirect(T.ou[:, 0:64]), T.iot[:]),
+                [("iot", 0, V), ("ou", 0, 64)], [("wa", 0, V)], (1, V * 3.8, 0, 0))
+        else:
+            add("s", lambda g, T, c: g.scalar.activation(T.wa[:, V:2 * V].indirect(T.ou[:, 64:128]), T.iot[:], AF.Silu),
+                [("iot", 0, V), ("ou", 64, 128)], [("wa", V, 2 * V)], (22, V * 3.8, 0, 0))
+        mm([(bk(7, 64, 64 * k), ("t2f", 15 - i, 143 - i), ("wa", k * V + i, k * V + V, 16), i == 0, i == 15) for i in range(16)])
+    cp(("ov", 0, 128), bk(7, 128))
+    dma("y", lambda e, T, c: [e.dma_start(T.s_v[:], T.ov[:])], [("ov", 0, 128)], [D("s_v")], 64e3)
+    a2a("s_v", "l_v", 8e3)
+    own("y", "s_v", "l_v", 8e3)
+    for k in range(2):
+        ts(("idf", 128 * k, 128 * k + 128), I128, P, ALU.is_equal)
+    for (nm, n, s) in (("idp", 256, 1.0), ("idn", 256, -1.0), ("id13", 256, 2.0 ** -13), ("id8", 128, 2.0 ** -8), ("id32", 128, 1.0 / 32)):
+        act((nm, 0, n), ("idf", 0, n), AF.Identity, scale=s)
+    for k in range(3):
+        ts(("ct", 256 * k, 256 * k + 256), ("idf", 0, 256), P0, ALU.mult, 4096.0 ** (2 - k), ALU.mult)
+    ts(("ih1", 0, 128), ("idf", 0, 128), 1.0, ALU.mult)
+    ts(("ihp", 0, 128), ("idf", 0, 128), 8192.0, ALU.mult)
+    ts(("ihn", 0, 128), ("idf", 0, 128), -8192.0, ALU.mult)
+    ts(("t2a", 0, 144), I144, PT, ALU.is_equal, -2048.0, ALU.mult)
+    ts(("t2b", 0, 144), I144, PT, ALU.is_equal, 2048.0, ALU.mult)
+    ts(("bo", 0, 128), ("g16", 0, 128), PD, ALU.is_equal)
+    ts(("bo", 128, 176), ("g16", 0, 48), PD, ALU.is_equal)
+    ts(("m16", 0, 16), ("iot", 0, 16), PM, ALU.is_equal)
+    for i in range(16):
+        act(("xt", 176 * i, 176 * i + 176), ("bo", 0, 176), AF.Identity, scale=("m16", i, i + 1))
+    add("v", lambda g, T, c: g.vector.memset(T.ones[:], 1.0), [], [("ones", 0, H)], 350.0)
+    add("v", lambda g, T, c: g.vector.memset(T.m85[:], -8.5), [], [("m85", 0, 128)], 150.0)
+    ts(("v16", 0, 64), ("iot", 0, 64), 16.0, ALU.mult, PM, ALU.add)
+    OA, OB = -18432.0, 16384.0
+    ts(("zi", 0, 32), ("v16", 0, 32), OA, ALU.add)
+    ts(("zi", 32, 64), ("v16", 32, 64), OB + H, ALU.add)
+    ts(("cc", 0, 32), ("v16", 0, 32), OA + H, ALU.add)
+    ts(("cc", 32, 64), ("v16", 32, 64), OB, ALU.add)
+    add("v", lambda g, T, c: g.vector.memset(T.off[:, 0:32], OA + H), [], [("off", 0, 32)], 130.0)
+    add("v", lambda g, T, c: g.vector.memset(T.off[:, 32:64], OB), [], [("off", 32, 64)], 130.0)
+
+    LI, LH, LPE = ("l_i", 0, 2), ("l_h", 0, 2), ("l_pe", 0, 2)
+    dma("y", lambda e, T, c: [e.dma_start(T.li[:, 0:64], T.l_i[:, 0:32, :])], [LI], [("li", 0, 64)], 32e3)
+    dma("y", lambda e, T, c: [e.dma_start(T.li[:, 64:128], T.l_i[:, 32:64, :])], [LI], [("li", 64, 128)], 32e3)
+    dma("y", lambda e, T, c: [e.dma_start(T.hp[16:128, :], T.l_h[0:7]), e.dma_start(T.hp[0:16, :], T.l_h[7])], [LH], [("hp", 0, V)], 26e4)
+    dma("y", lambda e, T, c: [e.dma_start(T.hl[:], T.l_h[:])], [LH], [("hl", 0, V)], 26e4)
+    dma("g", lambda e, T, c: [e.dma_start(T.wb[:, H:H + V], T.l_pe[:, 0:64, :])], [LPE], [("wb", H, H + V)], 52e4)
+    dma("y", lambda e, T, c: [e.dma_start(T.e0[:], T.l_pe[:, 64:128, :])], [LPE], [("e0", 0, V)], 26e4)
+    dma("y", lambda e, T, c: [e.dma_start(T.li[:, 128:192], T.l_i[:, 64:96, :])], [LI], [("li", 128, 192)], 32e3)
+    dma("y", lambda e, T, c: [e.dma_start(T.vi[:], T.l_v[:])], [("l_v", 0, 2)], [("vi", 0, 128)], 64e3)
+    cp(("lu", 0, 128), ("li", 0, 128))
+    cp(("lf", 0, 128), ("li", 0, 128))
+    tt(("asx", 0, 64), ("lf", 0, 64), ("off", 0, 64), ALU.add)
+    mm([(bk(6, 128, 128 * (t - 1)), rot("idf", t), ("lf", 0, 128), True, True) for t in (1, 2, 3)])
+    cp(("lu", 128, 512), bk(6, 384))
+    for t in (1, 2, 3):
+        tt(("asx", 64 * t, 64 * t + 64), bk(6, 64, 128 * (t - 1)), ("off", 0, 64), ALU.add)
+    cp(("lf", 128, 192), ("li", 128, 192))
+    cp(("zh", 0, 64), ("lf", 128, 192))
+    tt(("zt", 0, 64), ("lf", 128, 192), ("zh", 0, 64), ALU.subtract)
+    ts(("zl", 0, 64), ("zt", 0, 64), 0.9375, ALU.add)
+    cp(("vf", 0, 128), ("vi", 0, 128))
+    mm([(bk(7, 128, 128 * (t - 1)), rot("idf", t), ("vf", 0, 128), True, True) for t in (1, 2, 3)])
+    cp(("lv", 0, 384), bk(7, 384))
+
+    def lst(nm, t, k, h):
+        lo = 128 * t + 64 * k + 32 * h
+        return (nm, lo, lo + 32)
+
+    def passes(bank, items):
+        for n, it in enumerate(items):
+            s0, s1 = n == 0, n == len(items) - 1
+            if it[0] == "x":
+                t, u, h = it[1], it[2], it[3]
+                mm([(bk(bank, 64, 64 * j), ("xt", 176 * (8 * h + j) + 16 * t, 176 * (8 * h + j) + 16 * t + 128), u, False, s1 and j == 7)
+                    for j in range(8)])
+            else:
+                mm([(bk(bank), it[0], it[1], s0, s1)])
+
+    for h in (0, 1):
+        if h == 0:
+            act(ch("ha", h), ("hp", 0, V), AF.Identity, idx=lst("lu", 0, 0, h))
+        else:
+            cp(ch("ha", h), ("hp", 0, V), idx=lst("lu", 0, 0, h))
+        cp(ch("hb", h), ("hp", 0, V), idx=lst("lu", 0, 1, h))
+        passes(0 + h, [(rot("idp", 0), ch("hl", h)), (rot("idn", 0), ch("ha", h))])
+        act(ch("da", h), bk(0 + h), AF.Abs)
+        passes(2 + h, [(rot("idp", 0), ch("hl", h)), (rot("idn", 0), ch("hb", h))])
+        act(bk(2 + h), bk(2 + h), AF.Abs)
+        tt(ch("dd", h), bk(2 + h), ch("da", h), ALU.subtract)
+
+    def mkdd(t):
+        for h in ((0,) if OPT["zs"] else (0, 1)):
+            passes(4 + h, [(rot("idp", t), ch("dd", h))])
+            act(ch("dd", h, V * t), bk(4 + h), AF.Identity, bias=DEL[t])
+
+    DEL = (0.0, 0.125, 0.25, 0.5)
+    Q3 = H + H // 2
+
+    def step(t, w, sel, dst=None, adq=None, ix2=None, late=False, ab=0):
+        zs = ((w, 0, H), (w, 3 * H, 4 * H))
+        pw = (w, H, 3 * H)
+        tb0 = 64 if late else 0
+        for h in (0, 1):
+            if h == 1 and t and OPT["zs"]:
+                passes(5, [(rot("idp", t), ch("dd", h))])
+                act(("gz", 0, H), pw, AF.Identity, bias=DEL[t], idx=lst("lu", t, 1, h))
+                tt(zs[h], bk(5), ("gz", 0, H), ALU.add)
+            else:
+                tt(zs[h], pw, ch("dd", h, V * t), ALU.add, idx=lst("lu", t, 1, h))
+            tt(ch("lt", h, V * t), pw, zs[h], ALU.is_gt, idx=lst("lu", t, 0, h))
+            tb = ("t2a", "t2b")[h]
+            mm([(bk(2 + h, 32), (tb, 15 - i, 143 - i), ("lt", V * t + H * h + i, V * t + H * h + H, 16), i == 0, i == 15) for i in range(16)])
+            c32 = lambda nm, b=0: (nm, b + 32 * h, b + 32 * h + 32)
+            tt(c32("t1", tb0), bk(2 + h, 32), c32("zi"), (ALU.max, ALU.min)[h])
+            tt(c32("t2", tb0), c32("t1", tb0), c32("asx", 64 * t), (ALU.min, ALU.max)[h])
+            ts(c32("ix", tb0), c32("t2", tb0), (-OA, -OB)[h], ALU.add)
+            win = (w, H * h, H * h + 3 * H)
+            if h == 0 or late or not OPT["split"]:
+                act(ch(sel, h), win, AF.Identity, idx=c32("ix", tb0))
+                if dst:
+                    tt(ch(dst[0], h, dst[1]), bk(ab + h), ch(sel, h), ALU.add)
+            else:
+                act((sel, H, Q3), win, AF.Identity, idx=("ix", 32, 48))
+                if dst:
+                    tt((dst[0], dst[1] + Q3, dst[1] + V), win, adq, ALU.add, idx=("ix", 48, 64))
+                    tt((dst[0], dst[1] + H, dst[1] + Q3), bk(ab + 1, H // 2), (sel, H, Q3), ALU.add)
+                else:
+                    cp((sel, Q3, V), win, idx=("ix", 48, 64))
+            if ix2:
+                tt(c32("t3"), c32("t1", tb0), c32("cc"), (ALU.min, ALU.max)[h])
+                ts(c32(ix2), c32("t3"), (-OA, -OB - H)[h], ALU.add)
+
+    for h in (0, 1):
+        passes(4 + h, [(rot("idp", 0), ch("da", h))])
+    step(0, "wb", "nn", dst=("qh", 0), adq=("da", Q3, V), ab=4)
+    for t in (1, 2, 3):
+        mkdd(t)
+    for (k, nm, h) in ((0, "hb", 0), (1, "ha", 0), (2, "ha", 1), (3, "hb", 1)):
+        passes(6 + k % 2, [(rot("idp", 3), ch(nm, h))])
+        act(("hab", H * k, H * k + H), bk(6 + k % 2), AF.Identity)
+
+    MK = ("mk", 0, 64)
+
+    def forest(e, second):
+        mk = (lambda t, h: [("x", t, MK, h)]) if second else (lambda t, h: [])
+        for h in (0, 1):
+            passes(h, [(rot("id8", 0), ch("hl", h))] + [(rot("ih1", 0), ch("qh", h)), (rot("idp", 0), ch(e, h))][::-1 if e == "e0" else 1] + mk(0, h))
+            if h == 0:
+                act(ch("wa", h, H), bk(h), AF.Identity, bias=-511.5 / 8192)
+            else:
+                ts(ch("wa", h, H), bk(h), -511.5 / 8192, ALU.add)
+        w3 = "wc" if second else "wa"
+        for (t, w, w2) in ((1, "wa", "wb"), (2, "wb", w3)):
+            for h in (1, 0):
+                passes(h, [(rot("idp", t), ch("da", h)), (rot("idp", t), ch(e, h))]
+                       + ([(rot("id13", 1), ch("hl", h))] if t == 1 else []) + mk(t, h))
+            if OPT["split"]:
+                act(("adq", 0, H // 2), bk(1, H // 2, H // 2), AF.Identity)
+            step(t, w, "nn", dst=(w2, H), adq=("adq", 0, H // 2))
+            for h, (lo, hi) in enumerate(OPT["wch"]):
+                if OPT["wm"][2 - t][h] != "f":
+                    mm([(bk(4, hi - lo), ("bo", 0, 128), ("lt", V * t + lo, V * t + hi), True, True)])
+                    act(("sw", V * (t - 1) + lo, V * (t - 1) + hi), bk(4, hi - lo), AF.Sign, bias=-8.5)
+        n = "nb" if second else "na"
+        step(3, w3, n, ix2="ixb" if second else "ixa", late=second)
+        if not second:
+            for h in (0, 1):
+                passes(h, [(rot("idn", 3), ch("da", h)), (rot("idn", 3), ch(e, h)), ("x", 3, ("zh", 0, 64), h), ("x", 3, ("zl", 0, 64), h)])
+                tt(ch("wt", h), bk(h), ch(n, h), ALU.is_lt)
+                passes(4 + h, [(("bo", 0, 128), ch("wt", h))])
+                act(ch("wr", h), bk(4 + h), AF.Relu, bias=-8.5)
+
+    def walk(u4, u9, wm):
+        for h in (0, 1):
+            passes(h, [(("m85", 0, 128, 1, 1), ("ones", 0, H, 1, 1)), (("bo", 0, 128), ch("lt", h, 3 * V))])
+            tt(ch("sa1", h), bk(h), ch("wr", h), ALU.mult)
+        for (t, s, s2) in ((3, "sa1", "sa2"), (2, "sa2", "sa1"), (1, "sa1", None)):
+            for h, (lo, hi) in enumerate(OPT["wch"]):
+                b0, l0 = V * (t - 1), 128 * (t - 1)
+                a0, a1 = ("g0", b0 + lo, b0 + hi), ("g1", b0 + lo, b0 + hi)
+                md = wm[3 - t][h]
+                ib = ("lv", l0 + 64 + lo // 16, l0 + 64 + hi // 16)
+                bb = bk((0, 1, 3)[h], hi - lo)
+                act(a0, (s, 0, V), AF.Relu, scale=-1.0, idx=("lv", l0 + lo // 16, l0 + hi // 16))
+                if md == "s":
+                    act(a1, (s, 0, V), AF.Relu, idx=ib)
+                elif md == "p":
+                    ts(a1, (s, 0, V), 0.0, ALU.max, idx=ib)
+                else:
+                    tt(a1, (s, 0, V), a0, ALU.max, idx=ib)
+                if s2 and md == "f":
+                    mm([(bb, ("m85", 0, 128, 1, 1), ("ones", 0, hi - lo, 1, 1), True, False)])
+                    mm([(bb, ("bo", 0, 128), ("lt", V * (t - 1) + lo, V * (t - 1) + hi), False, True)])
+                    tt((s2, lo, hi), bb, a1, ALU.mult)
+                elif s2:
+                    mm([(bb, rot("idp", 0), a1, True, False)])
+                    mm([(bb, rot("idp", 0), a0, False, True)])
+                    tt((s2, lo, hi), bb, ("sw", V * (t - 2) + lo, V * (t - 2) + hi), ALU.mult)
+                nms = (s2,) if s2 else (("g1",) if md == "f" else ("g1", "g0"))
+                for nm in nms:
+                    its = []
+                    for i in range(lo // 64, hi // 64):
+                        s0 = 256 * (t - 1) + 128 - (16 * (t - 1) + i)
+                        its.append((bk(2, 64), ("ct", s0, s0 + 128), (nm, 64 * i, 64 * i + 64),
+                                    t == 3 and i == 0, t == 1 and i == 15 and nm == nms[-1]))
+                    mm(its)
+        ts(u4, bk(2, 64), 0.0, ALU.not_equal, 4.0, ALU.mult)
+        if u9:
+            ts(u9, bk(2, 64), 0.0, ALU.not_equal, 9.0, ALU.mult)
+
+    pool = [[6, 7], 0]
+
+    def nb_():
+        pool[1] += 1
+        return pool[0][pool[1] % len(pool[0])]
+
+    M8 = 1.5 * 2 ** 20
+
+    def strip(n, l, tp, f, ix2):
+        for h in (0, 1):
+            b = nb_()
+            if OPT["strip_s"]:
+                act(("rm", 0, H), ch(n, h), AF.Identity, bias=M8)
+                act(bk(b), ("rm", 0, H), AF.Identity, bias=-M8)
+            else:
+                ts(bk(b), ch(n, h), M8, ALU.add, M8, ALU.subtract)
+            tt(ch(l, h), ch(n, h), bk(b), ALU.subtract)
+            ts(ch(tp, h), ch(l, h), 8192.0, ALU.mult, 6160.0, ALU.add)
+            if f:
+                act(ch(f, h), ("hab", V * h, V * h + V), AF.Identity, idx=(ix2, 32 * h, 32 * h + 32))
+
+    first = [True, True]
+    by_dma = [0, 0]
+
+    def term(items, bias, half, lo, hi, dm):
+        b = bk(nb_(), hi - lo)
+        h = lo // H
+        for n, (tb, x) in enumerate(items):
+            mm([(b, tb, (x, lo, hi), n == 0, n == len(items) - 1)])
+        act(b, b, AF.Abs, bias=bias)
+        lb = math.log(0.5) if half else 0.0
+        ac = ("acc", lo, hi)
+        if first[h]:
+            act(ac, b, AF.Exp, bias=lb, scale=-0.125)
+            first[h] = False
+        elif dm:
+            by_dma[h] += 1
+            x = ("x%d" % (by_dma[h] % 2), lo, hi)
+            act(x, b, AF.Exp, bias=lb, scale=-0.125)
+            dma("g", lambda e, T, c: [e.dma_start(A(T, ac), A(T, x), accum_op=ALU.add)], [x, ac], [ac], 1024.0 * (hi - lo))
+        else:
+            act(b, b, AF.Exp, bias=lb, scale=-0.125)
+            tt(ac, b, ac, ALU.add)
+
+    IP, IN = rot("idp", 0), rot("idn", 0)
+
+    def gain_a():
+        strip("na", "la", "ta", "fa", "ixa")
+        for (lo, hi) in HS:
+            term([(IP, "fa"), (rot("idn", 3), "hl")], 0.0, False, lo, hi, OPT["dma_add"])
+
+    def both_ways(second):
+        for k in range(4):
+            h, b, src_k, dst_k = k // 2, bk(nb_()), ("hab", H * k, H * k + H), ("eb", H * k, H * k + H)
+            if not second:
+                passes(int(b[0][1]), [(rot("idn", 3), ch("hl", h)), (IP, src_k)])
+                act(b, b, AF.Abs)
+                act(dst_k, b, AF.Exp, bias=math.log(0.5), scale=-0.125)
+            else:
+                passes(int(b[0][1]), [(IN, src_k), (rot("ihp", 0), ch("la", h)), (IN, ch("ta", h))])
+                act(b, b, AF.Abs, bias=6175.5)
+                x = ch("x%d" % (k % 2), h)
+                act(x, b, AF.Exp, scale=-0.125)
+                dma("g", lambda e, T, c, x=x, d=dst_k: [e.dma_start(A(T, d), A(T, x), accum_op=ALU.add)], [x, dst_k], [dst_k], 52e4)
+
+    def gain_b(parts, nd, both=False):
+        strip("nb", "lb", "tb", None if both else "fb", "ixb")
+        for (lo, hi) in parts:
+            if both:
+                h = lo // H
+                tt(("acc", lo, hi), ("eb", V * h, V * h + V), ("acc", lo, hi), ALU.add, idx=("ixb", lo // 16, hi // 16))
+            else:
+                term([(IP, "fb"), (rot("idn", 3), "hl")], 0.0, True, lo, hi, nd > 0)
+                term([(rot("ihp", 0), "la"), (IN, "ta"), (IN, "fb")], 6175.5, False, lo, hi, nd > 1)
+            term([(rot("ihp", 0), "lb"), (IN, "tb"), (IN, "fa")], 6175.5, True, lo, hi, nd > 2)
+            term([(rot("id32", 0), "ta"), (rot("ihn", 0), "lb"), (IP, "tb")], -6352.5, False, lo, hi, nd > 3)
+            term([(rot("id32", 0), "tb"), (rot("ihn", 0), "la"), (IP, "ta")], -6352.5, True, lo, hi, nd > 4)
+
+    for rnd in (0, 1):
+        e, e2 = ("e0", "e1", "e2")[rnd], ("e0", "e1", "e2")[rnd + 1]
+        ua, ub, un = ("u4", 128 * rnd, 128 * rnd + 64), ("u4", 128 * rnd + 64, 128 * rnd + 128), ("un", 64 * rnd, 64 * rnd + 64)
+        forest(e, False)
+        walk(ua, ("u9", 0, 64), OPT["wm"])
+        send(lambda T, q, ua=ua, un=un: [((q - 1) % N, A(T, ua), A(T, un))], [ua], [un], 2e3, one=True)
+        gain_a()
+        if OPT["both"]:
+            both_ways(rnd == 1)
+        tt(MK, ("u9", 0, 64), un, ALU.add)
+        forest(e, True)
+        walk(ub, None, OPT["wl"] if rnd else OPT["wm"])
+        tt(("dl", 0, 64), ua, ub, ALU.subtract)
+        for h in (0, 1):
+            eb = h if rnd else 4 + h
+            passes(eb, [(IP, ch(e, h)), ("x", 0, ("dl", 0, 64), h)])
+            ts(ch(e2, h), bk(eb), 0.0, ALU.max, 63.0, ALU.min)
+        if rnd == 1:
+            pool[0] = [4, 5, 6, 7]
+            gain_b(PIECES, OPT["tail_dma"], OPT["both"])
+        else:
+            gain_b(HS, 5 if OPT["dma_add"] else 0)
+
+    def home(e, T, q, out, s, l, base, cols):
+        r = [e.dma_start(out[16 * q:16 * q + 16, cols], T[s][base + q])]
+        if q > 0:
+            r.append(e.dma_start(out[0:16 * q, cols], T[l][base:base + q]))
+        if q < N - 1:
+            r.append(e.dma_start(out[16 * q + 16:128, cols], T[l][base + q + 1:base + N]))
+        return r
+    dma("y", lambda e, T, c: [e.dma_start(T.s_t[:], T.e2[:])], [("e2", 0, V)], [D("s_t")], 26e4)
+    a2a("s_t", "l_t", 32e3)
+    dma("g", lambda e, T, c: home(e, T, c["q"], T.tollout, "s_t", "l_t", 0, slice(0, V)), [D("s_t"), D("l_t")], [], 52e4)
+    for k, (lo, hi) in enumerate(PIECES):
+        sg, lg, nby = "s_g%d" % k, "l_g%d" % k, 512.0 * (hi - lo)
+        dma("y", lambda e, T, c, sg=sg, lo=lo, hi=hi: [e.dma_start(T[sg][:], T.acc[:, lo:hi])], [("acc", lo, hi)], [D(sg)], nby)
+        a2a(sg, lg, nby / 8)
+        dma("y", lambda e, T, c, sg=sg, lg=lg, lo=lo, hi=hi: home(e, T, c["q"], T.gain, sg, lg, 0, slice(lo, hi)), [D(sg), D(lg)], [], nby)
+    return ops
+
+
+def queue_of(o):
+    return "s" if o["eng"] == "a" else o["eng"]
+
+
+def schedule(ops):
+    n = len(ops)
+    pre = [dict(o["deps"]) for o in ops]
+    for i, o in enumerate(ops):
+        if o["kind"] == "a":
+            pre[i][o["from"]] = True
+    succ = [[] for _ in range(n)]
+    for i in range(n):
+        for j in pre[i]:
+            succ[j].append(i)
+    pr = [0.0] * n
+    for i in range(n - 1, -1, -1):
+        pr[i] = ops[i]["cost"] + ops[i]["lat"] + max([pr[k] + (LAT if pre[k][i] else 0.0) for k in succ[i]] + [0.0])
+    x = OPT["seed"]
+    for i in range(n):
+        x = (x * 1103515245 + 12345) % 2147483648
+        if ops[i]["kind"] == "c":
+            pr[i] += OPT["noise"] * x / 2147483648.0
+    left = [len(p) for p in pre]
+    rdy = [0.0] * n
+    fin = [0.0] * n
+    start = [0.0] * n
+    free = {}
+    avail = [i for i in range(n) if left[i] == 0]
+    order = []
+    while avail:
+        best = None
+        for i in avail:
+            q = queue_of(ops[i])
+            s = rdy[i] if q is None else max(rdy[i], free.get(q, 0.0))
+            if best is None or s < best[0] - 1e-9 or (abs(s - best[0]) <= 1e-9 and pr[i] > pr[best[1]]):
+                best = (s, i)
+        s, i = best
+        q = queue_of(ops[i])
+        if q is not None:
+            for k in avail:
+                if queue_of(ops[k]) == q and pr[k] > pr[i] + OPT["margin"] and rdy[k] < s + OPT["look"] * ops[i]["cost"]:
+                    i = k
+            s = max(rdy[i], free.get(q, 0.0))
+            free[q] = s + ops[i]["cost"]
+        avail.remove(i)
+        start[i] = s
+        fin[i] = s + ops[i]["cost"] + ops[i]["lat"]
+        order.append(i)
+        for k in succ[i]:
+            rdy[k] = max(rdy[k], fin[i] + LAT if pre[k][i] else s)
+            left[k] -= 1
+            if left[k] == 0:
+                avail.append(k)
+    return order, start, fin
+
+
+PLAN = {}
+
+
+def rank_program(g, core, T, topo):
+    q = T.rank_of(core)
+    if q is None:
+        return
+    if not PLAN:
+        PLAN["ops"] = build()
+        PLAN["order"] = schedule(PLAN["ops"])[0]
+    ops, order = PLAN["ops"], PLAN["order"]
+    c = dict(q=q, core=core, topo=topo)
+    qs = {"v": g.vector, "s": g.scalar, "p": g.tensor, "g": g, "y": g.sync}
+    csem = {"v": "cv", "s": "cs", "p": "cp", "g": "cg"}
+    cnt = {}
+    tok = {}
+    seen = {k: {} for k in qs}
+    know = {}
+
+    def wait(qn, j):
+        s, v = tok[j]
+        if seen[qn].get(s, 0) < v:
+            qs[qn].wait_ge(T.sem[s], v)
+            seen[qn][s] = v
+            for (s2, v2) in know[j].items():
+                if seen[qn].get(s2, 0) < v2:
+                    seen[qn][s2] = v2
+
+    for i in order:
+        o = ops[i]
+        if o["kind"] == "a":
+            nb = T.cores[(q + 1) % N]
+            tok[i] = (o["sem"], len(topo.engines(nb, core)) if o["one"] else N - 1)
+            know[i] = {}
+            continue
+        qn = queue_of(o)
+        for j in sorted((j for j, w in o["deps"].items() if w), reverse=True):
+            wait(qn, j)
+        know[i] = dict(seen[qn])
+        if o["kind"] == "c":
+            s = csem[qn]
+            cnt[s] = cnt.get(s, 0) + 1
+            o["fn"](g, T, c).then_inc(T.sem[s], 1)
+            tok[i] = (s, cnt[s])
+        elif o["kind"] == "d":
+            ins = o["fn"](qs[qn], T, c)
+            for x in ins:
+                x.then_inc(T.sem[o["sem"]], 16)
+            tok[i] = (o["sem"], 16 * len(ins))
+        else:
+            tok[i] = (o["sem"], o["fn"](g, T, c))
+    fin = {}
+    for i in order:
+        s, v = tok[i]
+        if v >= fin.get(s, (0, 0))[0]:
+            fin[s] = (v, i)
+    for i in order:
+        s, v = tok[i]
+        if fin[s][1] == i and all(seen[k].get(s, 0) < v for k in seen):
+            wait("g", i)

@@ -12,43 +12,45 @@ def sb(n, d):
     return ("sbuf", [128, n], d)
 
 
-SCRATCH = {
-    "s_i": ("dram", [8, 128, 32], I32), "l_i": ("dram", [8, 128, 32], I32),
-    "s_h": ("dram", [8, 128, 128], BF), "l_h": ("dram", [8, 128, 128], BF),
-    "s_pe": ("dram", [8, 128, 256], BF), "l_pe": ("dram", [8, 128, 256], BF),
-    "s_v": ("dram", [8, 128, 16], I32), "l_v": ("dram", [8, 128, 16], I32),
-    "s_t": ("dram", [8, 128, 128], BF), "l_t": ("dram", [8, 128, 128], BF),
-    "iot": sb(V, F32), "g16": sb(256, F32), "pci": sb(8, I32), "pcf": sb(8, F32), "v16": sb(64, F32),
-    "idp": sb(256, BF), "idn": sb(256, BF), "id13": sb(256, BF), "id8": sb(128, BF), "id32": sb(128, BF),
-    "idf": sb(256, F32), "ihp": sb(128, F16), "ihn": sb(128, F16), "ih1": sb(128, F16), "ct": sb(768, BF),
-    "x0": sb(V, F32), "x1": sb(V, F32), "rm": sb(H, F32),
-    "t2a": sb(144, BF), "t2b": sb(144, BF), "t2f": sb(144, F32), "bo": sb(176, BF), "m16": sb(16, F32),
-    "xt": sb(16 * 176, BF), "ones": sb(H, BF), "m85": sb(128, BF),
-    "zi": sb(64, F32), "cc": sb(64, F32), "off": sb(64, F32),
-    "oi": sb(128, I32), "ou": sb(128, U16), "ov": sb(128, I32), "li": sb(192, I32), "lf": sb(192, F32),
-    "lu": sb(512, U16), "asx": sb(256, F32), "vi": sb(128, I32), "vf": sb(128, F32), "lv": sb(384, U16),
-    "zh": sb(64, BF), "zt": sb(64, F32), "zl": sb(64, BF),
-    "t1": sb(128, F32), "t2": sb(128, F32), "t3": sb(64, F32), "ix": sb(128, U16), "adq": sb(256, F32), "gz": sb(H, F32), "eb": sb(2 * V, F32), "wc": sb(2 * V, F32), "ixa": sb(64, U16), "ixb": sb(64, U16),
-    "hl": sb(V, BF), "hp": sb(V, BF), "ha": sb(V, BF), "hb": sb(V, BF), "da": sb(V, BF),
-    "dd": sb(4 * V, BF), "hab": sb(2 * V, BF), "e0": sb(V, BF), "e1": sb(V, BF), "e2": sb(V, BF),
-    "wa": sb(2 * V, F32), "wb": sb(2 * V, F32), "qh": sb(V, F16), "nn": sb(V, F32), "na": sb(V, F32), "nb": sb(V, F32),
-    "lt": sb(4 * V, BF), "sw": sb(2 * V, BF), "wt": sb(V, BF), "wr": sb(V, BF),
-    "sa1": sb(V, BF), "sa2": sb(V, BF), "g0": sb(3 * V, BF), "g1": sb(3 * V, BF),
-    "u4": sb(256, BF), "u9": sb(64, BF), "un": sb(128, BF), "mk": sb(64, BF), "dl": sb(64, BF),
-    "la": sb(V, F16), "lb": sb(V, F16), "ta": sb(V, BF), "tb": sb(V, BF), "fa": sb(V, BF), "fb": sb(V, BF),
-    "acc": sb(V, F32),
-}
-for _k in range(8):
-    SCRATCH["b%d" % _k] = ("psum", [128, H], F32)
+def slots(n, d):
+    return ("dram", [N, 128, n], d)
+
+
 PIECES = ((0, 512), (512, 768), (768, 1024))
+SCRATCH = {
+    "iot": sb(V, F32), "g16": sb(176, F32), "jj": sb(128, F32), "s2": sb(128, F32), "pci": sb(8, I32), "pcf": sb(16, F32),
+    "idf": sb(256, F32), "idp": sb(256, BF), "idn": sb(256, BF), "id13": sb(256, BF), "id8": sb(256, BF), "id32": sb(128, BF),
+    "ihp": sb(128, F16), "ihn": sb(128, F16), "t2f": sb(144, F32), "t2v": sb(144, BF), "ca": sb(144, BF), "cb": sb(144, BF),
+    "cl": sb(256, BF), "bo": sb(176, BF), "bs": sb(128, BF), "cv": sb(256, BF), "mf": sb(128, BF), "ma": sb(128, BF), "mb": sb(128, BF),
+    "xt": sb(16 * 128, BF), "k16": sb(128, F32), "ih1": sb(128, F16), "cx": sb(64, F16), "zq": sb(240, BF),
+    "oi": sb(128, I32), "ou": sb(128, U16), "ov": sb(192, I32), "li": sb(128, I32), "lf": sb(192, F32), "lu": sb(512, U16),
+    "vi": sb(192, I32), "vf": sb(192, F32), "lv": sb(384, U16), "zh": sb(64, BF), "zt": sb(64, F32), "zl": sb(64, BF),
+    "ix": sb(64, U16), "ixa": sb(128, U16), "ixb": sb(128, U16),
+    "hp": sb(V, BF), "hi": sb(2 * V, BF), "hab": sb(2 * V, BF), "da": sb(V, BF), "db": sb(V, BF), "dd": sb(4 * V, BF), "pz": sb(V, BF), "q16": sb(V, BF),
+    "e0": sb(V, BF), "e1": sb(V, BF), "en": sb(V, BF), "tf": sb(V, F32),
+    "pa": sb(V, F32), "pb": sb(V, F32), "pc": sb(V, F32), "w1": sb(2 * V, F32), "w2": sb(2 * V, F32),
+    "gz": sb(V, F32), "uq": sb(V, F32), "nn": sb(V, F32), "na": sb(V, F32), "nb": sb(V, F32), "rm": sb(H, F32),
+    "lt": sb(4 * V, BF), "wt": sb(V, BF), "wr": sb(V, BF), "ms": sb(3 * V, BF), "g0": sb(3 * V, BF), "g1": sb(3 * V, BF),
+    "u4": sb(256, BF), "u9": sb(64, BF), "un": sb(128, BF), "mk": sb(128, BF), "dl": sb(64, BF), "dr": sb(N * 64, BF), "dq": sb(64, BF),
+    "la": sb(2 * V, F16), "lb": sb(V, F16), "ta": sb(2 * V, BF), "tb": sb(V, BF), "fa": sb(2 * V, BF), "fb": sb(V, BF),
+    "eb": sb(2 * V, F32), "xe": sb(2 * V, F32), "xx": sb(4 * V, F32), "acc": sb(V, F32),
+}
+for _k, _n, _d in (("l", 16, I32), ("h", 128, BF), ("p", 128, BF), ("e", 128, BF), ("v", 24, I32), ("t", 128, BF)):
+    SCRATCH["s_" + _k] = slots(_n, _d)
+    SCRATCH["l_" + _k] = slots(_n, _d)
 for _k, (_lo, _hi) in enumerate(PIECES):
-    SCRATCH["s_g%d" % _k] = ("dram", [8, 128, (_hi - _lo) // 8], F32)
-    SCRATCH["l_g%d" % _k] = ("dram", [8, 128, (_hi - _lo) // 8], F32)
-NDS = 80
+    SCRATCH["s_g%d" % _k] = slots((_hi - _lo) // 8, F32)
+    SCRATCH["l_g%d" % _k] = slots((_hi - _lo) // 8, F32)
+PS = ("bA", "bB", "bC", "bD")
+for _k in PS:
+    SCRATCH[_k] = ("psum", [128, V], F32)
+NDS = 100
 SEMAPHORES = ["cv", "cs", "cp", "cg"] + ["d%d" % k for k in range(NDS)]
 
 CY, PEC, GAM, FIX, LAT = 1.0, 0.5, 1.55, 60.0, 90.0
-OPT = dict(dma_add=True, wm=("pp", "pp", "pp"), wl=("ps", "ps", "ps"), both=True, zs=True, tail_dma=0, seed=10, noise=400.0, split=True, wch=((0, 512), (512, 1024)), strip_s=False, look=0.5, margin=1500.0, pieces=((0, 512), (512, 768), (768, 1024)))
+FIGURES = ((60.0, 0.95, 1.55, 0.48, 100.0, 1.0), (50.0, 0.85, 1.2, 0.43, 150.0, 1.3), (70.0, 1.2, 2.0, 0.6, 70.0, 0.9))
+OPT = dict(c=512, s=(768, 768, 768, 768), z=(512, 512, 1024, 1024), turns=6000, dde="v", wp=(1, 1, 1, 1), wg="sv", both=True, pe=(0, 0, 0), sumb=(4, 5, 4), pool=(6, 7, 4, 5),
+           lean=0.0, a0=True, early=110e3, due=(0.0, 0.0, 45e3, 0.0, 0.0), strip="vvvv")
 
 
 def price(v, fix=FIX, cy=CY, gam=GAM, pec=PEC):
@@ -61,36 +63,35 @@ def build():
     ops = []
     last = {}
     nsem = [0]
+    boost = [0.0]
 
-    def add(eng, fn, rd, wr, cost, kind="c", after=(), lat=0.0):
+    def span(r):
+        nm, lo, hi = r[0], r[1], r[2]
+        if nm in PS:
+            return nm, lo // H * H, (hi + H - 1) // H * H, None, True
+        return nm, lo, hi, (lo % 2 if len(r) > 3 and r[3] == 2 else None), False
+
+    def add(eng, fn, rd, wr, cost, kind="c", lat=0.0):
         i = len(ops)
         deps = {}
-        for j in after:
-            deps[j] = True
         for (rs, w) in ((rd, False), (wr, True)):
             for r in rs:
-                nm, lo, hi = r[0], r[1], r[2]
-                bank = SCRATCH.get(nm, ("x",))[0] == "psum"
-                if bank:
-                    lo, hi = 0, H
-                for (l2, h2, j, w2) in last.get(nm, ()):
-                    if l2 < hi and lo < h2 and j != i:
-                        same = ops[j]["eng"] == eng and kind == "c" and ops[j]["kind"] == "c"
+                nm, lo, hi, lane, bank = span(r)
+                for (l2, h2, j, w2, lane2) in last.get(nm, ()):
+                    if l2 < hi and lo < h2 and (lane is None or lane2 is None or lane == lane2):
+                        same = ops[j]["eng"] == eng != "f" and kind == "c" and ops[j]["kind"] == "c"
                         if w2 and not w:
                             deps[j] = True
                         elif w or w2 or (bank and not same):
                             deps[j] = deps.get(j, False) or not (same and eng == "p")
         for (rs, w) in ((rd, False), (wr, True)):
             for r in rs:
-                nm, lo, hi = r[0], r[1], r[2]
-                bank = SCRATCH.get(nm, ("x",))[0] == "psum"
-                if bank:
-                    lo, hi = 0, H
+                nm, lo, hi, lane, bank = span(r)
                 lst = last.setdefault(nm, [])
                 if w:
-                    lst[:] = [e for e in lst if not (lo <= e[0] and e[1] <= hi)]
-                lst.append((lo, hi, i, w))
-        o = dict(eng=eng, fn=fn, deps=deps, vec=cost, cost=price(cost), kind=kind, lat=lat, nm=(wr or rd)[0][0] if (wr or rd) else "")
+                    lst[:] = [e for e in lst if not (lo - (lane or 0) <= e[0] and e[1] <= hi and (lane is None or lane == e[4]))]
+                lst.append((lo, hi, i, w, lane))
+        o = dict(eng=eng, fn=fn, deps=deps, boost=boost[0], vec=cost, cost=price(cost), kind=kind, lat=lat, nm=(wr or rd)[0][0] if (wr or rd) else "")
         if kind != "c":
             o["sem"] = "d%d" % nsem[0]
             nsem[0] += 1
@@ -112,38 +113,51 @@ def build():
     def two(r):
         return SCRATCH[r[0]][2] in (BF, F16, U16)
 
-    def ps(r):
-        return SCRATCH[r[0]][0] == "psum"
-
     def src(T, x, idx):
         return A(T, x) if idx is None else A(T, x).indirect(A(T, idx))
 
     def aps(*xs):
         return [x for x in xs if isinstance(x, tuple)]
 
-    def vcost(out, x, idx, base):
+    def vcost(out, idx, base):
         if idx is not None:
             return (1, 0.0, n_(out), 0.0)
         return (1, max(64.0, n_(out) * base), 0.0, 0.0)
 
     def tt(out, x, y, op, idx=None):
         return add("v", lambda g, T, c: g.vector.tensor_tensor(A(T, out), src(T, x, idx), A(T, y), op),
-                   aps(x, y, idx), [out], vcost(out, x, idx, 1.0 if ps(x) or ps(y) else 2.0))
+                   aps(x, y, idx), [out], vcost(out, idx, 1.0 if x[0] in PS or y[0] in PS else 2.0))
 
     def ts(out, x, s1, op0, s2=None, op1=None, idx=None):
         def fn(g, T, c):
+            a = s1[0](c["q"]) if isinstance(s1, list) else A(T, s1)
             if op1 is None:
-                return g.vector.tensor_scalar(A(T, out), src(T, x, idx), A(T, s1), None, op0)
-            return g.vector.tensor_scalar(A(T, out), src(T, x, idx), A(T, s1), A(T, s2), op0, op1)
-        return add("v", fn, aps(x, s1, s2, idx), [out], vcost(out, x, idx, 0.5 if two(out) and two(x) else 1.0))
+                return g.vector.tensor_scalar(A(T, out), src(T, x, idx), a, None, op0)
+            return g.vector.tensor_scalar(A(T, out), src(T, x, idx), a, A(T, s2), op0, op1)
+        return add("v", fn, aps(x, s1, s2, idx), [out], vcost(out, idx, 0.5 if two(out) and two(x) else 1.0))
 
     def cp(out, x, idx=None):
         return add("v", lambda g, T, c: g.vector.tensor_copy(A(T, out), src(T, x, idx)),
-                   aps(x, idx), [out], vcost(out, x, idx, 0.5 if two(out) and two(x) else 1.0))
+                   aps(x, idx), [out], vcost(out, idx, 0.5 if two(out) and two(x) else 1.0))
 
     def act(out, x, f, bias=0.0, scale=1.0, idx=None):
         return add("s", lambda g, T, c: g.scalar.activation(A(T, out), src(T, x, idx), f, bias=A(T, bias), scale=A(T, scale)),
-                   aps(x, idx, bias, scale), [out], vcost(out, x, idx, 1.0))
+                   aps(x, idx, bias, scale), [out], vcost(out, idx, 1.0))
+
+    def either(eng, on_s, on_v, rd, out, cost):
+        i = add(eng, on_v if eng == "v" else on_s, rd, [out], cost)
+        if eng == "f":
+            ops[i]["ways"] = [("s", on_s, cost), ("v", on_v, cost)]
+        return i
+
+    def mov(eng, out, x, bias=0.0, scale=1.0, idx=None):
+        return either(eng, lambda g, T, c: g.scalar.activation(A(T, out), src(T, x, idx), AF.Identity, bias=bias, scale=scale),
+                      lambda g, T, c: g.vector.tensor_scalar(A(T, out), src(T, x, idx), scale, bias, ALU.mult, ALU.add),
+                      aps(x, idx), out, vcost(out, idx, 1.0))
+
+    def sign(eng, out, x):
+        return either(eng, lambda g, T, c: g.scalar.activation(A(T, out), A(T, x), AF.Sign),
+                      lambda g, T, c: g.vector.tensor_scalar(A(T, out), A(T, x), -1.0, 1.0, ALU.max, ALU.min), [x], out, vcost(out, None, 1.0))
 
     def mm(items):
         def fn(g, T, c):
@@ -158,12 +172,20 @@ def build():
         return add("p", fn, rd, [items[0][0]], cost)
 
     def dma(q, fn, rd, wr, nbytes):
-        return add(q, fn, rd, wr, 60.0 if q != "g" else 400.0, kind="d", lat=1900.0 + nbytes / 180.0)
+        return add(q, fn, rd, wr, 60.0 if q != "g" else 500.0, kind="d", lat=2000.0 + nbytes / 400.0)
 
-    def gop(fn, wr, n):
-        return add("g", fn, [], wr, 130.0 + 2 * CY * n)
+    def dma_add(out, x):
+        dma("g", lambda e, T, c: [e.dma_start(A(T, out), A(T, x), accum_op=ALU.add)], [x, out], [out], 1024.0 * n_(out))
 
-    def send(pairs, rd, land, nbytes, one=False):
+    def iota(out, pattern, base=0, step=0):
+        small = SCRATCH[out[0]][2] != I32
+        def fn(g, T, c):
+            if small:
+                return g.iota(A(T, out), pattern, base, step, allow_small_or_imprecise_dtypes=True)
+            return g.iota(A(T, out), pattern, base, step)
+        return add("g", fn, [], [out], 130.0 + 2 * CY * n_(out))
+
+    def send(pairs, rd, land, lat, one=False):
         k = len(ops)
 
         def fn(g, T, c):
@@ -180,54 +202,60 @@ def build():
                                              remote_sem=T.sem[ops[k + 1]["sem"]], src=s, dst=t))
             g.remote_dma_fused(trs, local_sem=T.sem[ops[k]["sem"]])
             return tot
-        i = add("g", fn, rd, [], 500.0, kind="r", lat=2000.0 + nbytes / 20.0)
+        i = add("g", fn, rd, [], 500.0, kind="r", lat=lat)
         j = add(None, None, [], land, 0.0, kind="a")
         ops[j]["from"] = i
         ops[j]["one"] = one
         return j
 
-    def D(nm, k=0):
-        return (nm, k, k + 1)
+    def others(q):
+        return [d % N for d in range(q + 1, q + N)]
 
-    def a2a(s, l, nbytes, base=0):
-        k = base // 8
-        send(lambda T, q: [(d % N, T[s][base + d % N], T[l][base + q]) for d in range(q + 1, q + N)],
-             [D(s, k)], [D(l, 2 * k)], nbytes)
-
-    def own(qn, s, l, nbytes):
-        dma(qn, lambda e, T, c: [e.dma_start(T[l][c["q"]], T[s][c["q"]])], [D(s)], [D(l, 1)], nbytes)
+    def a2a(k, own=True):
+        s, l = "s_" + k, "l_" + k
+        nby = 128 * SCRATCH[s][1][2] * (2 if SCRATCH[s][2] == BF else 4)
+        send(lambda T, q: [(d, T[s][d], T[l][q]) for d in others(q)], [(s, 0, 2)], [(l, 0, 1)], 2200.0 + nby / 25.0)
+        if own:
+            dma("y", lambda e, T, c: [e.dma_start(T[l][c["q"]], T[s][c["q"]])], [(s, 0, 2)], [(l, 1, 2)], nby)
 
     HS = ((0, H), (H, V))
 
-    def ch(nm, h, base=0):
-        return (nm, base + h * H, base + h * H + H)
-
     def bk(k, n=H, lo=0):
-        return ("b%d" % k, lo, lo + n)
+        return (PS[k // 2], H * (k % 2) + lo, H * (k % 2) + lo + n)
 
     def rot(nm, t):
         return (nm, 16 * t, 16 * t + 128)
 
-    dma("y", lambda e, T, c: [e.dma_start(T.s_i[:, 0:32, :], T.sa[:]), e.dma_start(T.s_i[:, 64:96, :], T.lim[:])], [], [("s_i", 0, 1)], 8e4)
-    dma("a", lambda e, T, c: [e.dma_start(T.s_i[:, 32:64, :], T.sb[:]), e.dma_start(T.s_i[:, 96:128, :], T.lim[:])], [], [("s_i", 1, 2)], 8e4)
-    dma("y", lambda e, T, c: [e.dma_start(T.s_h[:], T.hf[:])], [], [D("s_h")], 26e4)
-    dma("a", lambda e, T, c: [e.dma_start(T.oi[:, 0:64], T.sa[:]), e.dma_start(T.oi[:, 64:128], T.sb[:])], [], [("oi", 0, 128)], 8e4)
-    dma("y", lambda e, T, c: [e.dma_start(T.s_pe[:, 0:64, :], T.p0[:])], [], [("s_pe", 0, 1)], 26e4)
-    dma("a", lambda e, T, c: [e.dma_start(T.s_pe[:, 64:128, :], T.toll[:])], [], [("s_pe", 1, 2)], 26e4)
-    gop(lambda g, T, c: g.iota(T.pci[:, 0:1], [[0, 1]], 0, 1), [("pci", 0, 1)], 1)
-    gop(lambda g, T, c: g.iota(T.iot[:, 0:144], [[1, 144]], 0, 0, allow_small_or_imprecise_dtypes=True), [("iot", 0, 144)], 144)
-    gop(lambda g, T, c: g.iota(T.g16[:, 0:176], [[1, 11], [0, 16]], 0, 0, allow_small_or_imprecise_dtypes=True), [("g16", 0, 176)], 176)
-    for k in range(144, V, 144):
-        w = min(144, V - k)
-        act(("iot", k, k + w), ("iot", 0, w), AF.Identity, bias=float(k))
-    send(lambda T, q: [(d % N, T.s_i[d % N], T.l_i[q]) for d in range(q + 1, q + N)], [("s_i", 0, 2)], [D("l_i")], 16e3)
-    dma("y", lambda e, T, c: [e.dma_start(T.l_i[c["q"]], T.s_i[c["q"]])], [("s_i", 0, 2)], [D("l_i", 1)], 16e3)
-    a2a("s_h", "l_h", 32e3)
-    own("y", "s_h", "l_h", 32e3)
-    send(lambda T, q: [(d % N, T.s_pe[d % N], T.l_pe[q]) for d in range(q + 1, q + N)], [("s_pe", 0, 2)], [D("l_pe")], 64e3)
-    dma("y", lambda e, T, c: [e.dma_start(T.l_pe[c["q"]], T.s_pe[c["q"]])], [("s_pe", 0, 2)], [D("l_pe", 1)], 64e3)
+    def passes(bank, lo, hi, items):
+        for n, it in enumerate(items):
+            s0, s1 = n == 0, n == len(items) - 1
+            if it[0] == "x":
+                js = range(lo // 64, hi // 64)
+                mm([(bk(bank, 64, 64 * j - lo), ("xt", 128 * j, 128 * j + 128), it[1], False, s1 and j == js[-1]) for j in js])
+            else:
+                st = it[3] if len(it) > 3 else 1
+                mm([(bk(bank, hi - lo), it[0], (it[1], it[2] + st * lo, it[2] - it[2] % st + st * hi, st), s0, s1)])
 
-    P, PD, PM, PT, P0, PQ = [("pcf", k, k + 1) for k in range(6)]
+    dma("y", lambda e, T, c: [e.dma_start(T.s_l[:, 0:64, :], T.sa[:])], [], [("s_l", 0, 1)], 4e4)
+    dma("a", lambda e, T, c: [e.dma_start(T.s_l[:, 64:128, :], T.sb[:])], [], [("s_l", 1, 2)], 4e4)
+    dma("y", lambda e, T, c: [e.dma_start(T.s_h[:], T.hf[:])], [], [("s_h", 0, 2)], 26e4)
+    dma("a", lambda e, T, c: [e.dma_start(T.oi[:, 0:64], T.sa[:]), e.dma_start(T.oi[:, 64:128], T.sb[:])], [], [("oi", 0, 128)], 8e4)
+    dma("y", lambda e, T, c: [e.dma_start(T.s_p[:], T.p0[:])], [], [("s_p", 0, 2)], 40e4)
+    dma("a", lambda e, T, c: [e.dma_start(T.ov[:, 128:192], T.lim[:])], [], [("ov", 128, 192)], 4e4)
+    dma("y", lambda e, T, c: [e.dma_start(T.s_e[:], T.toll[:])], [], [("s_e", 0, 2)], 60e4)
+    iota(("pci", 0, 1), [[0, 1]], 0, 1)
+    iota(("iot", 0, 256), [[1, 256]])
+    iota(("g16", 0, 128), [[1, 8], [0, 16]])
+    for k in (1, 2, 3):
+        act(("iot", 256 * k, 256 * k + 256), ("iot", 0, 256), AF.Identity, bias=256.0 * k)
+    for k in "lhpe":
+        a2a(k)
+    iota(("jj", 0, 128), [[8, 8], [0, 2], [1, 8]])
+    iota(("s2", 0, 128), [[0, 8], [4, 2], [0, 8]], -2)
+    iota(("k16", 0, 128), [[0, 8], [1, 16]])
+
+    boost[0] = OPT["early"]
+    P, PD, PM, PT, P0, PH, LA, LB, P16, RA, RB, PZ, MQ, PX, P7, WB = [("pcf", k, k + 1) for k in range(16)]
     ts(("pci", 1, 2), ("pci", 0, 1), 4, ALU.arith_shift_right)
     ts(("pci", 2, 3), ("pci", 0, 1), 15, ALU.bitwise_and)
     cp(("pcf", 0, 3), ("pci", 0, 3))
@@ -236,214 +264,220 @@ def build():
     cp(("ou", 0, 128), ("oi", 0, 128))
     I128, I144 = ("iot", 0, 128), ("iot", 0, 144)
     ts(("t2f", 0, 144), I144, PT, ALU.is_equal, P0, ALU.mult)
+    add("v", lambda g, T, c: g.vector.tensor_copy(T.w2[:, 0:V].indirect(T.ou[:, 0:64]), T.iot[:]),
+        [("iot", 0, V), ("ou", 0, 64)], [("w2", 0, V)], (1, V * 3.8, 0, 0))
+    add("s", lambda g, T, c: g.scalar.activation(T.w2[:, V:2 * V].indirect(T.ou[:, 64:128]), T.iot[:], AF.Silu),
+        [("iot", 0, V), ("ou", 64, 128)], [("w2", V, 2 * V)], (22, V * 3.8, 0, 0))
     for k in range(2):
-        if k == 0:
-            add("v", lambda g, T, c: g.vector.tensor_copy(T.wa[:, 0:V].indirect(T.ou[:, 0:64]), T.iot[:]),
-                [("iot", 0, V), ("ou", 0, 64)], [("wa", 0, V)], (1, V * 3.8, 0, 0))
-        else:
-            add("s", lambda g, T, c: g.scalar.activation(T.wa[:, V:2 * V].indirect(T.ou[:, 64:128]), T.iot[:], AF.Silu),
-                [("iot", 0, V), ("ou", 64, 128)], [("wa", V, 2 * V)], (22, V * 3.8, 0, 0))
-        mm([(bk(7, 64, 64 * k), ("t2f", 15 - i, 143 - i), ("wa", k * V + i, k * V + V, 16), i == 0, i == 15) for i in range(16)])
+        for j in range(0, 16, 4):
+            mm([(bk(7, 64, 64 * k), ("t2f", 15 - i, 143 - i), ("w2", k * V + i, k * V + V, 16), i == 0, i == 15) for i in range(j, j + 4)])
     cp(("ov", 0, 128), bk(7, 128))
-    dma("y", lambda e, T, c: [e.dma_start(T.s_v[:], T.ov[:])], [("ov", 0, 128)], [D("s_v")], 64e3)
-    a2a("s_v", "l_v", 8e3)
-    own("y", "s_v", "l_v", 8e3)
+    dma("y", lambda e, T, c: [e.dma_start(T.s_v[:], T.ov[:])], [("ov", 0, 192)], [("s_v", 0, 2)], 1e5)
+    a2a("v")
     for k in range(2):
         ts(("idf", 128 * k, 128 * k + 128), I128, P, ALU.is_equal)
-    for (nm, n, s) in (("idp", 256, 1.0), ("idn", 256, -1.0), ("id13", 256, 2.0 ** -13), ("id8", 128, 2.0 ** -8), ("id32", 128, 1.0 / 32)):
-        act((nm, 0, n), ("idf", 0, n), AF.Identity, scale=s)
-    for k in range(3):
-        ts(("ct", 256 * k, 256 * k + 256), ("idf", 0, 256), P0, ALU.mult, 4096.0 ** (2 - k), ALU.mult)
-    ts(("ih1", 0, 128), ("idf", 0, 128), 1.0, ALU.mult)
-    ts(("ihp", 0, 128), ("idf", 0, 128), 8192.0, ALU.mult)
-    ts(("ihn", 0, 128), ("idf", 0, 128), -8192.0, ALU.mult)
-    ts(("t2a", 0, 144), I144, PT, ALU.is_equal, -2048.0, ALU.mult)
-    ts(("t2b", 0, 144), I144, PT, ALU.is_equal, 2048.0, ALU.mult)
+    for (nm, n, s) in (("idp", 192, 1.0), ("idn", 192, -1.0), ("id13", 160, 2.0 ** -13), ("id8", 144, 2.0 ** -8), ("id32", 128, 1.0 / 32)):
+        mov("f", (nm, 0, n), ("idf", 0, n), scale=s)
+    ts(("ihp", 0, 128), ("idp", 0, 128), 8192.0, ALU.mult)
+    ts(("ihn", 0, 128), ("idp", 0, 128), -8192.0, ALU.mult)
+    ts(("ih1", 0, 128), ("idp", 0, 128), 1.0, ALU.mult)
+    ts(("t2v", 0, 144), I144, PT, ALU.is_equal, 1.0 / 17, ALU.mult)
+    ts(PX, PM, 2.0, ALU.mult)
+    ts(("cx", 0, 64), ("iot", 0, 64), 32.0, ALU.mult, PX, ALU.add)
     ts(("bo", 0, 128), ("g16", 0, 128), PD, ALU.is_equal)
-    ts(("bo", 128, 176), ("g16", 0, 48), PD, ALU.is_equal)
-    ts(("m16", 0, 16), ("iot", 0, 16), PM, ALU.is_equal)
-    for i in range(16):
-        act(("xt", 176 * i, 176 * i + 176), ("bo", 0, 176), AF.Identity, scale=("m16", i, i + 1))
-    add("v", lambda g, T, c: g.vector.memset(T.ones[:], 1.0), [], [("ones", 0, H)], 350.0)
-    add("v", lambda g, T, c: g.vector.memset(T.m85[:], -8.5), [], [("m85", 0, 128)], 150.0)
-    ts(("v16", 0, 64), ("iot", 0, 64), 16.0, ALU.mult, PM, ALU.add)
-    OA, OB = -18432.0, 16384.0
-    ts(("zi", 0, 32), ("v16", 0, 32), OA, ALU.add)
-    ts(("zi", 32, 64), ("v16", 32, 64), OB + H, ALU.add)
-    ts(("cc", 0, 32), ("v16", 0, 32), OA + H, ALU.add)
-    ts(("cc", 32, 64), ("v16", 32, 64), OB, ALU.add)
-    add("v", lambda g, T, c: g.vector.memset(T.off[:, 0:32], OA + H), [], [("off", 0, 32)], 130.0)
-    add("v", lambda g, T, c: g.vector.memset(T.off[:, 32:64], OB), [], [("off", 32, 64)], 130.0)
+    for k in range(4):
+        x = ("xt", H * k, H * k + H)
+        iota(x, [[0, H]], 1)
+        add("g", lambda g, T, c, x=x, k=k: g.affine_select(A(T, x), A(T, x), [[-1, 4], [-16, 8], [0, 16]], ALU.is_equal, 0.0, -4 * k, 1),
+            [x], [x], 170.0 + 2 * CY * H)
+    ts(RA, PM, 7.5, ALU.is_lt)
+    ts(RB, PM, 7.5, ALU.is_gt)
+    ts(("pcf", 6, 8), ("pcf", 9, 11), 16.0, ALU.mult)
+    ts(PH, P, 0.5, ALU.mult)
+    ts(P16, PD, 16.0, ALU.mult)
+    ts(("ca", 0, 144), I144, PT, ALU.is_equal, RA, ALU.mult)
+    ts(("cb", 0, 144), I144, PT, ALU.is_equal, RB, ALU.mult)
+    for k in range(2):
+        ts(("cl", 128 * k, 128 * k + 128), I128, P16, ALU.is_equal)
+    ts(("mf", 0, 128), ("jj", 0, 128), PH, ALU.is_equal, 16.0, ALU.mult)
+    ts(("ma", 0, 128), ("jj", 0, 128), PH, ALU.is_equal, LA, ALU.mult)
+    ts(("mb", 0, 128), ("jj", 0, 128), PH, ALU.is_equal, LB, ALU.mult)
+    tt(("bs", 0, 128), ("bo", 0, 128), ("s2", 0, 128), ALU.mult)
+    ts(P7, PM, 7.0, ALU.is_equal)
+    ts(WB, P7, 100.0, ALU.mult, -8.5, ALU.add)
+    ts(("cv", 0, 128), ("s2", 0, 128), -8.5, ALU.mult, -16.0, ALU.add)
+    ts(("cv", 128, 256), ("k16", 0, 128), 7.0, ALU.is_equal, 63.0, ALU.mult)
+    tt(("cv", 0, 128), ("cv", 0, 128), ("cv", 128, 256), ALU.add)
+    ts(("cv", 128, 256), ("bo", 0, 128), P7, ALU.mult)
+    tt(("cv", 0, 128), ("cv", 0, 128), ("cv", 128, 256), ALU.mult)
+    for nm in ("mf", "ma"):
+        tt((nm, 0, 128), (nm, 0, 128), ("cv", 0, 128), ALU.add)
+    ts(PZ, PM, 112.0, ALU.add)
+    ts(MQ, PD, [float], ALU.is_equal)
+    ts(("zq", 0, 240), ("iot", 0, 240), PZ, ALU.is_equal, MQ, ALU.mult)
 
-    LI, LH, LPE = ("l_i", 0, 2), ("l_h", 0, 2), ("l_pe", 0, 2)
-    dma("y", lambda e, T, c: [e.dma_start(T.li[:, 0:64], T.l_i[:, 0:32, :])], [LI], [("li", 0, 64)], 32e3)
-    dma("y", lambda e, T, c: [e.dma_start(T.li[:, 64:128], T.l_i[:, 32:64, :])], [LI], [("li", 64, 128)], 32e3)
-    dma("y", lambda e, T, c: [e.dma_start(T.hp[16:128, :], T.l_h[0:7]), e.dma_start(T.hp[0:16, :], T.l_h[7])], [LH], [("hp", 0, V)], 26e4)
-    dma("y", lambda e, T, c: [e.dma_start(T.hl[:], T.l_h[:])], [LH], [("hl", 0, V)], 26e4)
-    dma("g", lambda e, T, c: [e.dma_start(T.wb[:, H:H + V], T.l_pe[:, 0:64, :])], [LPE], [("wb", H, H + V)], 52e4)
-    dma("y", lambda e, T, c: [e.dma_start(T.e0[:], T.l_pe[:, 64:128, :])], [LPE], [("e0", 0, V)], 26e4)
-    dma("y", lambda e, T, c: [e.dma_start(T.li[:, 128:192], T.l_i[:, 64:96, :])], [LI], [("li", 128, 192)], 32e3)
-    dma("y", lambda e, T, c: [e.dma_start(T.vi[:], T.l_v[:])], [("l_v", 0, 2)], [("vi", 0, 128)], 64e3)
+    boost[0] = 0.0
+    dma("y", lambda e, T, c: [e.dma_start(T.li[:, 0:64], T.l_l[:, 0:64, :])], [("l_l", 0, 2)], [("li", 0, 64)], 32e3)
+    dma("y", lambda e, T, c: [e.dma_start(T.li[:, 64:128], T.l_l[:, 64:128, :])], [("l_l", 0, 2)], [("li", 64, 128)], 32e3)
+    dma("y", lambda e, T, c: [e.dma_start(T.hp[16:128, :], T.l_h[0:7]), e.dma_start(T.hp[0:16, :], T.l_h[7])], [("l_h", 0, 2)], [("hp", 0, V)], 26e4)
+    dma("y", lambda e, T, c: [e.dma_start(T.pz[:], T.l_p[:])], [("l_p", 0, 2)], [("pz", 0, V)], 26e4)
+    dma("y", lambda e, T, c: [e.dma_start(T.e0[:], T.l_e[:])], [("l_e", 0, 2)], [("e0", 0, V)], 26e4)
+    dma("y", lambda e, T, c: [e.dma_start(T.vi[:], T.l_v[:])], [("l_v", 0, 2)], [("vi", 0, 192)], 1e5)
     cp(("lu", 0, 128), ("li", 0, 128))
     cp(("lf", 0, 128), ("li", 0, 128))
-    tt(("asx", 0, 64), ("lf", 0, 64), ("off", 0, 64), ALU.add)
     mm([(bk(6, 128, 128 * (t - 1)), rot("idf", t), ("lf", 0, 128), True, True) for t in (1, 2, 3)])
     cp(("lu", 128, 512), bk(6, 384))
+
+    def lst(nm, t, k, lo, hi):
+        return (nm, 128 * t + 64 * k + lo // 16, 128 * t + 64 * k + hi // 16)
+
+    def lane(nm, k, lo, hi):
+        return (nm, 2 * lo + k, 2 * hi, 2)
+
+    IP, IN = rot("idp", 0), rot("idn", 0)
+    DEL = 0.125
+    for h, (lo, hi) in enumerate(HS):
+        mov("s", lane("hi", 0, lo, hi), ("hp", 0, V), idx=lst("lu", 0, 0, lo, hi))
+        mov("v", lane("hi", 1, lo, hi), ("hp", 0, V), idx=lst("lu", 0, 1, lo, hi))
+        passes(h, lo, hi, [(rot("idp", 1), "hp", 0), (IN, "hi", 0, 2)])
+        act(("da", lo, hi), bk(h), AF.Abs)
+        passes(4 + h, lo, hi, [(rot("idp", 1), "hp", 0), (IN, "hi", 1, 2)])
+        act(("db", lo, hi), bk(4 + h), AF.Abs)
+        passes(4 + h, lo, hi, [(IN, "da", 0), (IP, "db", 0)])
+        mov(OPT["dde"], ("dd", lo, hi), bk(4 + h), bias=DEL)
+
+    def turn(out, x, t):
+        (o, a, b), (i, c_, d) = out, x
+        dma("y", lambda e, T, c: [e.dma_start(T[o][0:128 - 16 * t, a:b], T[i][16 * t:128, c_:d]),
+                                  e.dma_start(T[o][128 - 16 * t:128, a:b], T[i][0:16 * t, c_:d])], [x], [out], 256.0 * (b - a))
     for t in (1, 2, 3):
-        tt(("asx", 64 * t, 64 * t + 64), bk(6, 64, 128 * (t - 1)), ("off", 0, 64), ALU.add)
-    cp(("lf", 128, 192), ("li", 128, 192))
-    cp(("zh", 0, 64), ("lf", 128, 192))
-    tt(("zt", 0, 64), ("lf", 128, 192), ("zh", 0, 64), ALU.subtract)
-    ts(("zl", 0, 64), ("zt", 0, 64), 0.9375, ALU.add)
-    cp(("vf", 0, 128), ("vi", 0, 128))
-    mm([(bk(7, 128, 128 * (t - 1)), rot("idf", t), ("vf", 0, 128), True, True) for t in (1, 2, 3)])
-    cp(("lv", 0, 384), bk(7, 384))
+        for (lo, hi) in (HS if t == 1 else ((0, V),)):
+            turn(("dd", V * t + lo, V * t + hi), ("dd", lo, hi), t)
+    turn(("hab", 0, 2 * V), ("hi", 0, 2 * V), 3)
 
-    def lst(nm, t, k, h):
-        lo = 128 * t + 64 * k + 32 * h
-        return (nm, lo, lo + 32)
+    C = OPT["c"]
+    CH = ((0, C), (C, V))
 
-    def passes(bank, items):
-        for n, it in enumerate(items):
-            s0, s1 = n == 0, n == len(items) - 1
-            if it[0] == "x":
-                t, u, h = it[1], it[2], it[3]
-                mm([(bk(bank, 64, 64 * j), ("xt", 176 * (8 * h + j) + 16 * t, 176 * (8 * h + j) + 16 * t + 128), u, False, s1 and j == 7)
-                    for j in range(8)])
-            else:
-                mm([(bk(bank), it[0], it[1], s0, s1)])
+    def halves(lo, hi):
+        return [(max(lo, a), min(hi, b)) for (a, b) in HS if max(lo, a) < min(hi, b)]
 
-    for h in (0, 1):
-        if h == 0:
-            act(ch("ha", h), ("hp", 0, V), AF.Identity, idx=lst("lu", 0, 0, h))
+    def behind(i, js):
+        for j in js:
+            ops[i]["deps"].setdefault(j, False)
+        return i
+
+    def votes(t, p, w, ix, z, late=False, mid=None):
+        pw = (p, 0, V)
+        for (lo, hi) in halves(z, V):
+            passes(4 + lo // H, lo, hi, [(rot("idp", t), "dd", 0)])
+            act(("gz", lo, hi), pw, AF.Identity, idx=lst("lu", t, 1, lo, hi))
+        row = []
+        for k, (lo, hi) in enumerate(CH):
+            act(lane(w, 0, lo, hi), pw, AF.Identity, bias=DEL, idx=lst("lu", t, 0, lo, hi))
+            if lo < z:
+                m = min(hi, z)
+                behind(tt(lane(w, 1, lo, m), pw, ("dd", V * t + lo, V * t + m), ALU.add, idx=lst("lu", t, 1, lo, m)), row[:1])
+            for (a, b) in halves(max(lo, z), hi):
+                behind(tt(lane(w, 1, a, b), bk(4 + a // H, b - a, a - max(z, a // H * H)), ("gz", a, b), ALU.add), row[:1])
+            row.append(behind(tt(("lt", V * t + lo, V * t + hi), pw, lane(w, 1, lo, hi), ALU.is_gt, idx=lst("lu", t, 0, lo, hi)), row[1:]))
+            n = (hi - lo) // 16
+            mm([(bk(2 + k, n), ("ih1", 0, 128), ("cx", 0, n), True, False)]
+               + [(bk(2 + k, n), ("t2v", 15 - i, 143 - i), ("lt", V * t + lo + i, V * t + hi, 16), False, i == 15) for i in range(16)])
+            js = mid() if mid and k else []
+            row.append(behind(ts((ix[0], ix[1] + lo // 16, ix[1] + hi // 16), bk(2 + k, n), 1.5 * 2 ** 23, ALU.add, 1.5 * 2 ** 23, ALU.subtract),
+                              js if OPT["a0"] else []))
+            if late:
+                row.pop()
+
+    def pick(w, ix, lo, hi):
+        clo, chi = CH[0] if lo < C else CH[1]
+        return (w, 2 * clo, 2 * chi), (ix[0], ix[1] + lo // 16, ix[1] + hi // 16)
+
+    def step(t, p, w, ix, sel, out, op, op_r, S, Z):
+        def part(lo, hi):
+            win, i = pick(w, ix, lo, hi)
+            act((sel, lo, hi), win, AF.Identity, idx=i)
+            return [tt((out, lo, hi), (PS[0], lo, hi), (sel, lo, hi), op_r)]
+        if S < V:
+            mov("s", ("uq", S, V), (PS[0], S, V))
+        votes(t, p, w, ix, Z, mid=lambda: part(0, C))
+        if S < V:
+            win, i = pick(w, ix, S, V)
+            tt((out, S, V), win, ("uq", S, V), op, idx=i)
+            part(C, S)
         else:
-            cp(ch("ha", h), ("hp", 0, V), idx=lst("lu", 0, 0, h))
-        cp(ch("hb", h), ("hp", 0, V), idx=lst("lu", 0, 1, h))
-        passes(0 + h, [(rot("idp", 0), ch("hl", h)), (rot("idn", 0), ch("ha", h))])
-        act(ch("da", h), bk(0 + h), AF.Abs)
-        passes(2 + h, [(rot("idp", 0), ch("hl", h)), (rot("idn", 0), ch("hb", h))])
-        act(bk(2 + h), bk(2 + h), AF.Abs)
-        tt(ch("dd", h), bk(2 + h), ch("da", h), ALU.subtract)
+            part(C, 768)
+            part(768, V)
 
-    def mkdd(t):
-        for h in ((0,) if OPT["zs"] else (0, 1)):
-            passes(4 + h, [(rot("idp", t), ch("dd", h))])
-            act(ch("dd", h, V * t), bk(4 + h), AF.Identity, bias=DEL[t])
+    IX = ("ix", 0)
+    votes(0, "pz", "w1", IX, V)
+    for (lo, hi, e) in ((0, C, "s"), (C, 768, "s"), (768, V, "v")):
+        win, i = pick("w1", IX, lo, hi)
+        mov(e, ("q16", lo, hi), win, bias=-128.0 - DEL, idx=i)
 
-    DEL = (0.0, 0.125, 0.25, 0.5)
-    Q3 = H + H // 2
+    cp(("vf", 0, 192), ("vi", 0, 192))
+    mm([(bk(7, 128, 128 * (t - 1)), rot("idf", t), ("vf", 0, 128), True, True) for t in (1, 2, 3)]
+       + [(bk(7, 64, 384), rot("idf", 3), ("vf", 128, 192), True, True)])
+    cp(("zh", 0, 64), bk(7, 64, 384))
+    tt(("zt", 0, 64), bk(7, 64, 384), ("zh", 0, 64), ALU.subtract)
+    ts(("zl", 0, 64), ("zt", 0, 64), 0.9375, ALU.add)
+    cp(("lv", 0, 384), bk(7, 384))
+    U9 = ("u9", 0, 64)
 
-    def step(t, w, sel, dst=None, adq=None, ix2=None, late=False, ab=0):
-        zs = ((w, 0, H), (w, 3 * H, 4 * H))
-        pw = (w, H, 3 * H)
-        tb0 = 64 if late else 0
-        for h in (0, 1):
-            if h == 1 and t and OPT["zs"]:
-                passes(5, [(rot("idp", t), ch("dd", h))])
-                act(("gz", 0, H), pw, AF.Identity, bias=DEL[t], idx=lst("lu", t, 1, h))
-                tt(zs[h], bk(5), ("gz", 0, H), ALU.add)
-            else:
-                tt(zs[h], pw, ch("dd", h, V * t), ALU.add, idx=lst("lu", t, 1, h))
-            tt(ch("lt", h, V * t), pw, zs[h], ALU.is_gt, idx=lst("lu", t, 0, h))
-            tb = ("t2a", "t2b")[h]
-            mm([(bk(2 + h, 32), (tb, 15 - i, 143 - i), ("lt", V * t + H * h + i, V * t + H * h + H, 16), i == 0, i == 15) for i in range(16)])
-            c32 = lambda nm, b=0: (nm, b + 32 * h, b + 32 * h + 32)
-            tt(c32("t1", tb0), bk(2 + h, 32), c32("zi"), (ALU.max, ALU.min)[h])
-            tt(c32("t2", tb0), c32("t1", tb0), c32("asx", 64 * t), (ALU.min, ALU.max)[h])
-            ts(c32("ix", tb0), c32("t2", tb0), (-OA, -OB)[h], ALU.add)
-            win = (w, H * h, H * h + 3 * H)
-            if h == 0 or late or not OPT["split"]:
-                act(ch(sel, h), win, AF.Identity, idx=c32("ix", tb0))
-                if dst:
-                    tt(ch(dst[0], h, dst[1]), bk(ab + h), ch(sel, h), ALU.add)
-            else:
-                act((sel, H, Q3), win, AF.Identity, idx=("ix", 32, 48))
-                if dst:
-                    tt((dst[0], dst[1] + Q3, dst[1] + V), win, adq, ALU.add, idx=("ix", 48, 64))
-                    tt((dst[0], dst[1] + H, dst[1] + Q3), bk(ab + 1, H // 2), (sel, H, Q3), ALU.add)
-                else:
-                    cp((sel, Q3, V), win, idx=("ix", 48, 64))
-            if ix2:
-                tt(c32("t3"), c32("t1", tb0), c32("cc"), (ALU.min, ALU.max)[h])
-                ts(c32(ix2), c32("t3"), (-OA, -OB - H)[h], ALU.add)
-
-    for h in (0, 1):
-        passes(4 + h, [(rot("idp", 0), ch("da", h))])
-    step(0, "wb", "nn", dst=("qh", 0), adq=("da", Q3, V), ab=4)
-    for t in (1, 2, 3):
-        mkdd(t)
-    for (k, nm, h) in ((0, "hb", 0), (1, "ha", 0), (2, "ha", 1), (3, "hb", 1)):
-        passes(6 + k % 2, [(rot("idp", 3), ch(nm, h))])
-        act(("hab", H * k, H * k + H), bk(6 + k % 2), AF.Identity)
-
-    MK = ("mk", 0, 64)
-
-    def forest(e, second):
-        mk = (lambda t, h: [("x", t, MK, h)]) if second else (lambda t, h: [])
-        for h in (0, 1):
-            passes(h, [(rot("id8", 0), ch("hl", h))] + [(rot("ih1", 0), ch("qh", h)), (rot("idp", 0), ch(e, h))][::-1 if e == "e0" else 1] + mk(0, h))
-            if h == 0:
-                act(ch("wa", h, H), bk(h), AF.Identity, bias=-511.5 / 8192)
-            else:
-                ts(ch("wa", h, H), bk(h), -511.5 / 8192, ALU.add)
-        w3 = "wc" if second else "wa"
-        for (t, w, w2) in ((1, "wa", "wb"), (2, "wb", w3)):
+    def forest(e, rnd, second, un):
+        Z, S = OPT["z"][2 * rnd + second], OPT["s"][2 * rnd + second]
+        for h, (lo, hi) in enumerate(HS):
+            its = [(IP, "q16", 0), (IP, e, 0)][::-1 if rnd == 0 else 1]
+            passes(h, lo, hi, [(rot("id8", 1), "hp", 0), (IP, "da", 0)] + its + ([("x", U9), ("x", un)] if second else []))
+            mov("sv"[h], ("pa", lo, hi), bk(h), bias=128.0 - 511.5 / 8192)
+        for (t, p, p2) in ((1, "pa", "pb"), (2, "pb", "pc")):
             for h in (1, 0):
-                passes(h, [(rot("idp", t), ch("da", h)), (rot("idp", t), ch(e, h))]
-                       + ([(rot("id13", 1), ch("hl", h))] if t == 1 else []) + mk(t, h))
-            if OPT["split"]:
-                act(("adq", 0, H // 2), bk(1, H // 2, H // 2), AF.Identity)
-            step(t, w, "nn", dst=(w2, H), adq=("adq", 0, H // 2))
-            for h, (lo, hi) in enumerate(OPT["wch"]):
-                if OPT["wm"][2 - t][h] != "f":
-                    mm([(bk(4, hi - lo), ("bo", 0, 128), ("lt", V * t + lo, V * t + hi), True, True)])
-                    act(("sw", V * (t - 1) + lo, V * (t - 1) + hi), bk(4, hi - lo), AF.Sign, bias=-8.5)
-        n = "nb" if second else "na"
-        step(3, w3, n, ix2="ixb" if second else "ixa", late=second)
-        if not second:
-            for h in (0, 1):
-                passes(h, [(rot("idn", 3), ch("da", h)), (rot("idn", 3), ch(e, h)), ("x", 3, ("zh", 0, 64), h), ("x", 3, ("zl", 0, 64), h)])
-                tt(ch("wt", h), bk(h), ch(n, h), ALU.is_lt)
-                passes(4 + h, [(("bo", 0, 128), ch("wt", h))])
-                act(ch("wr", h), bk(4 + h), AF.Relu, bias=-8.5)
+                passes(h, H * h, H * h + H, [(rot("idp", t), "da", 0), (rot("idp", t), e, 0)]
+                       + ([(rot("id13", 2), "hp", 0)] if t == 1 else []) + ([("x", ("mk", 64 * t - 64, 64 * t))] if second else []))
+            step(t, p, "w1", IX, "nn", p2, ALU.add, ALU.add, S, Z)
+        ix = ("ixb" if second else "ixa", 64 * rnd)
+        if second:
+            votes(3, "pc", "w2", ix, Z, rnd == 0)
+            boost[0] = OPT["due"][0] * (1 - rnd)
+            for (lo, hi) in (PIECES if rnd else CH):
+                win, i = pick("w2", ix, lo, hi)
+                mov("f", ("nb", lo, hi), win, idx=i)
+            boost[0] = 0.0
+            return ix
+        for h in (1, 0):
+            passes(h, H * h, H * h + H, [(rot("idn", 3), "da", 0), (rot("idn", 3), e, 0), ("x", ("zh", 0, 64)), ("x", ("zl", 0, 64))])
+        step(3, "pc", "w1", ix, "na", "wt", ALU.is_gt, ALU.is_lt, S, Z)
+        if S < V:
+            win, i = pick("w1", ix, S, V)
+            mov("f", ("na", S, V), win, idx=i)
+        for h, (lo, hi) in enumerate(HS):
+            passes(2 + h, lo, hi, [(("bo", 0, 128), "wt", 0)])
+            act(("wr", lo, hi), bk(2 + h), AF.Sign, bias=WB)
+        return ix
 
-    def walk(u4, u9, wm):
-        for h in (0, 1):
-            passes(h, [(("m85", 0, 128, 1, 1), ("ones", 0, H, 1, 1)), (("bo", 0, 128), ch("lt", h, 3 * V))])
-            tt(ch("sa1", h), bk(h), ch("wr", h), ALU.mult)
-        for (t, s, s2) in ((3, "sa1", "sa2"), (2, "sa2", "sa1"), (1, "sa1", None)):
-            for h, (lo, hi) in enumerate(OPT["wch"]):
-                b0, l0 = V * (t - 1), 128 * (t - 1)
-                a0, a1 = ("g0", b0 + lo, b0 + hi), ("g1", b0 + lo, b0 + hi)
-                md = wm[3 - t][h]
-                ib = ("lv", l0 + 64 + lo // 16, l0 + 64 + hi // 16)
-                bb = bk((0, 1, 3)[h], hi - lo)
-                act(a0, (s, 0, V), AF.Relu, scale=-1.0, idx=("lv", l0 + lo // 16, l0 + hi // 16))
-                if md == "s":
-                    act(a1, (s, 0, V), AF.Relu, idx=ib)
-                elif md == "p":
-                    ts(a1, (s, 0, V), 0.0, ALU.max, idx=ib)
+    def walk(outs, parts, last_=False):
+        BS = ("bs", 0, 128)
+        for h, (lo, hi) in enumerate(HS):
+            passes(4 + h, lo, hi, [(BS, "lt", 3 * V), (("mf", 0, 128), "wr", 0)][::-1 if len(outs) == 1 else 1])
+            sign("f", ("ms", 2 * V + lo, 2 * V + hi), bk(4 + h))
+        for t in (3, 2, 1):
+            b0 = V * (t - 1)
+            for k, (lo, hi) in enumerate(parts):
+                e = "f"
+                mov(OPT["wg"][0], ("g0", b0 + lo, b0 + hi), ("ms", b0, b0 + V), idx=lst("lv", t - 1, 0, lo, hi))
+                mov(OPT["wg"][1], ("g1", b0 + lo, b0 + hi), ("ms", b0, b0 + V), idx=lst("lv", t - 1, 1, lo, hi))
+                js = range(lo // 64, hi // 64)
+                if t > 1:
+                    b = (((4, 5, 3), (0, 1, 3))[t - 2] if not last_ else (0, 1, 3))[k]
+                    passes(b, lo, hi, [(BS, "lt", b0), (("ma", 0, 128), "g0", b0), (("mb", 0, 128), "g1", b0)])
+                    sign(e, ("ms", b0 - V + lo, b0 - V + hi), bk(b, hi - lo))
+                    mm([(bk(2, 64), ("cl", 128 - 16 * (t - 1) - j, 256 - 16 * (t - 1) - j), ("ms", b0 - V + 64 * j, b0 - V + 64 * j + 64),
+                         t == 3 and j == 0, False) for j in js])
                 else:
-                    tt(a1, (s, 0, V), a0, ALU.max, idx=ib)
-                if s2 and md == "f":
-                    mm([(bb, ("m85", 0, 128, 1, 1), ("ones", 0, hi - lo, 1, 1), True, False)])
-                    mm([(bb, ("bo", 0, 128), ("lt", V * (t - 1) + lo, V * (t - 1) + hi), False, True)])
-                    tt((s2, lo, hi), bb, a1, ALU.mult)
-                elif s2:
-                    mm([(bb, rot("idp", 0), a1, True, False)])
-                    mm([(bb, rot("idp", 0), a0, False, True)])
-                    tt((s2, lo, hi), bb, ("sw", V * (t - 2) + lo, V * (t - 2) + hi), ALU.mult)
-                nms = (s2,) if s2 else (("g1",) if md == "f" else ("g1", "g0"))
-                for nm in nms:
-                    its = []
-                    for i in range(lo // 64, hi // 64):
-                        s0 = 256 * (t - 1) + 128 - (16 * (t - 1) + i)
-                        its.append((bk(2, 64), ("ct", s0, s0 + 128), (nm, 64 * i, 64 * i + 64),
-                                    t == 3 and i == 0, t == 1 and i == 15 and nm == nms[-1]))
-                    mm(its)
-        ts(u4, bk(2, 64), 0.0, ALU.not_equal, 4.0, ALU.mult)
-        if u9:
-            ts(u9, bk(2, 64), 0.0, ALU.not_equal, 9.0, ALU.mult)
+                    for (tb, nm) in (("ca", "g0"), ("cb", "g1")):
+                        mm([(bk(2, 64), (tb, 15 - j, 143 - j), (nm, 64 * j, 64 * j + 64), False, j == 15 and nm == "g1") for j in js])
+        for (u, x) in outs:
+            ts(u, bk(2, 64), -41.0, ALU.is_gt, x, ALU.mult)
 
     pool = [[6, 7], 0]
 
@@ -453,114 +487,141 @@ def build():
 
     M8 = 1.5 * 2 ** 20
 
-    def strip(n, l, tp, f, ix2):
-        for h in (0, 1):
-            b = nb_()
-            if OPT["strip_s"]:
-                act(("rm", 0, H), ch(n, h), AF.Identity, bias=M8)
-                act(bk(b), ("rm", 0, H), AF.Identity, bias=-M8)
-            else:
-                ts(bk(b), ch(n, h), M8, ALU.add, M8, ALU.subtract)
-            tt(ch(l, h), ch(n, h), bk(b), ALU.subtract)
-            ts(ch(tp, h), ch(l, h), 8192.0, ALU.mult, 6160.0, ALU.add)
-            if f:
-                act(ch(f, h), ("hab", V * h, V * h + V), AF.Identity, idx=(ix2, 32 * h, 32 * h + 32))
-
-    first = [True, True]
-    by_dma = [0, 0]
-
-    def term(items, bias, half, lo, hi, dm):
-        b = bk(nb_(), hi - lo)
-        h = lo // H
-        for n, (tb, x) in enumerate(items):
-            mm([(b, tb, (x, lo, hi), n == 0, n == len(items) - 1)])
-        act(b, b, AF.Abs, bias=bias)
-        lb = math.log(0.5) if half else 0.0
-        ac = ("acc", lo, hi)
-        if first[h]:
-            act(ac, b, AF.Exp, bias=lb, scale=-0.125)
-            first[h] = False
-        elif dm:
-            by_dma[h] += 1
-            x = ("x%d" % (by_dma[h] % 2), lo, hi)
-            act(x, b, AF.Exp, bias=lb, scale=-0.125)
-            dma("g", lambda e, T, c: [e.dma_start(A(T, ac), A(T, x), accum_op=ALU.add)], [x, ac], [ac], 1024.0 * (hi - lo))
-        else:
-            act(b, b, AF.Exp, bias=lb, scale=-0.125)
-            tt(ac, b, ac, ALU.add)
-
-    IP, IN = rot("idp", 0), rot("idn", 0)
-
-    def gain_a():
-        strip("na", "la", "ta", "fa", "ixa")
-        for (lo, hi) in HS:
-            term([(IP, "fa"), (rot("idn", 3), "hl")], 0.0, False, lo, hi, OPT["dma_add"])
-
-    def both_ways(second):
-        for k in range(4):
-            h, b, src_k, dst_k = k // 2, bk(nb_()), ("hab", H * k, H * k + H), ("eb", H * k, H * k + H)
-            if not second:
-                passes(int(b[0][1]), [(rot("idn", 3), ch("hl", h)), (IP, src_k)])
-                act(b, b, AF.Abs)
-                act(dst_k, b, AF.Exp, bias=math.log(0.5), scale=-0.125)
-            else:
-                passes(int(b[0][1]), [(IN, src_k), (rot("ihp", 0), ch("la", h)), (IN, ch("ta", h))])
-                act(b, b, AF.Abs, bias=6175.5)
-                x = ch("x%d" % (k % 2), h)
-                act(x, b, AF.Exp, scale=-0.125)
-                dma("g", lambda e, T, c, x=x, d=dst_k: [e.dma_start(A(T, d), A(T, x), accum_op=ALU.add)], [x, dst_k], [dst_k], 52e4)
-
-    def gain_b(parts, nd, both=False):
-        strip("nb", "lb", "tb", None if both else "fb", "ixb")
+    def strip(n, l, tp, base, parts, eng):
         for (lo, hi) in parts:
-            if both:
-                h = lo // H
-                tt(("acc", lo, hi), ("eb", V * h, V * h + V), ("acc", lo, hi), ALU.add, idx=("ixb", lo // 16, hi // 16))
+            b = bk(nb_(), hi - lo)
+            if eng == "s":
+                act(("rm", 0, hi - lo), (n, lo, hi), AF.Identity, bias=M8)
+                act(b, ("rm", 0, hi - lo), AF.Identity, bias=-M8)
             else:
-                term([(IP, "fb"), (rot("idn", 3), "hl")], 0.0, True, lo, hi, nd > 0)
-                term([(rot("ihp", 0), "la"), (IN, "ta"), (IN, "fb")], 6175.5, False, lo, hi, nd > 1)
-            term([(rot("ihp", 0), "lb"), (IN, "tb"), (IN, "fa")], 6175.5, True, lo, hi, nd > 2)
-            term([(rot("id32", 0), "ta"), (rot("ihn", 0), "lb"), (IP, "tb")], -6352.5, False, lo, hi, nd > 3)
-            term([(rot("id32", 0), "tb"), (rot("ihn", 0), "la"), (IP, "ta")], -6352.5, True, lo, hi, nd > 4)
+                ts(b, (n, lo, hi), M8, ALU.add, M8, ALU.subtract)
+            tt((l, base + lo, base + hi), (n, lo, hi), b, ALU.subtract)
+            ts((tp, base + lo, base + hi), (l, base + lo, base + hi), 8192.0, ALU.mult, 6160.0, ALU.add)
+
+    def term(items, bias, half, lo, hi, out):
+        k = nb_()
+        b = bk(k, hi - lo)
+        passes(k, lo, hi, items)
+        act(b, b, AF.Abs, bias=bias)
+        act(out or b, b, AF.Exp, bias=math.log(0.5) if half else 0.0, scale=-0.125)
+        if not out:
+            tt(("acc", lo, hi), b, ("acc", lo, hi), ALU.add)
+
+    def picked(out, base, w, ix, scale=1.0):
+        for (lo, hi) in CH:
+            win, i = pick(w, ix, lo, hi)
+            mov("f", (out, base + lo, base + hi), win, scale=scale, idx=i)
+
+    nx = [0]
+
+    def xbuf():
+        nx[0] += 1
+        return V * (nx[0] % 4)
+
+    HP16, HN16, I32_ = ("ihp", 0, 128), ("ihn", 0, 128), ("id32", 0, 128)
+    for k in range(2):
+        for (lo, hi) in HS:
+            b = nb_()
+            passes(b, lo, hi, [(rot("idp", 3), ("da", "db")[k], 0)])
+            act(lane("eb", k, lo, hi), bk(b), AF.Exp, bias=math.log(0.5), scale=-0.125)
 
     for rnd in (0, 1):
-        e, e2 = ("e0", "e1", "e2")[rnd], ("e0", "e1", "e2")[rnd + 1]
+        e, a0 = ("e0", "e1")[rnd], V * rnd
         ua, ub, un = ("u4", 128 * rnd, 128 * rnd + 64), ("u4", 128 * rnd + 64, 128 * rnd + 128), ("un", 64 * rnd, 64 * rnd + 64)
-        forest(e, False)
-        walk(ua, ("u9", 0, 64), OPT["wm"])
-        send(lambda T, q, ua=ua, un=un: [((q - 1) % N, A(T, ua), A(T, un))], [ua], [un], 2e3, one=True)
-        gain_a()
-        if OPT["both"]:
-            both_ways(rnd == 1)
-        tt(MK, ("u9", 0, 64), un, ALU.add)
-        forest(e, True)
-        walk(ub, None, OPT["wl"] if rnd else OPT["wm"])
-        tt(("dl", 0, 64), ua, ub, ALU.subtract)
-        for h in (0, 1):
-            eb = h if rnd else 4 + h
-            passes(eb, [(IP, ch(e, h)), ("x", 0, ("dl", 0, 64), h)])
-            ts(ch(e2, h), bk(eb), 0.0, ALU.max, 63.0, ALU.min)
-        if rnd == 1:
-            pool[0] = [4, 5, 6, 7]
-            gain_b(PIECES, OPT["tail_dma"], OPT["both"])
+        ixa = forest(e, rnd, False, None)
+        walk([(ua, 4.0), (U9, 9.0)], (HS, PIECES)[OPT["wp"][2 * rnd]])
+        send(lambda T, q, ua=ua, un=un: [((q - 1) % N, A(T, ua), A(T, un))], [ua], [un], 2500.0, one=True)
+        boost[0] = OPT["due"][3 + rnd]
+        strip("na", "la", "ta", a0, HS, OPT["strip"][2 * rnd])
+        picked("fa", a0, "hab", ixa)
+        if rnd == 0:
+            picked("acc", 0, "eb", ixa, 2.0)
         else:
-            gain_b(HS, 5 if OPT["dma_add"] else 0)
+            x = xbuf()
+            picked("xx", x, "eb", ixa, 2.0)
+            dma_add(("acc", 0, V), ("xx", x, x + V))
+        both = rnd or OPT["both"]
+        if both:
+            for (lo, hi) in HS:
+                for k in range(2):
+                    term([(IN, "hab", k, 2), (HP16, "la", a0), (IN, "ta", a0)], 6175.5, False, lo, hi, lane("xe", k, lo, hi))
+                dma_add(("xe", 2 * lo, 2 * hi), ("eb", 2 * lo, 2 * hi))
+        boost[0] = 0.0
+        mm([(bk(3, 64, 64 * t - 64), rot("idp", t), u, u is U9, u is un) for t in (1, 2) for u in (U9, un)])
+        mov("f", ("mk", 0, 128), bk(3, 128))
+        ixb = forest(e, rnd, True, un)
+        walk([(ub, -4.0)], (HS, PIECES)[OPT["wp"][2 * rnd + 1]], rnd == 1)
+        terms = (([(HP16, "lb", 0), (IN, "tb", 0), (IN, "fa", a0)], 6175.5, True),
+                 ([(I32_, "ta", a0), (HN16, "lb", 0), (IP, "tb", 0)], -6352.5, False),
+                 ([(I32_, "tb", 0), (HN16, "la", a0), (IP, "ta", a0)], -6352.5, True))
+        if rnd == 0:
+            for h, (lo, hi) in enumerate(HS):
+                passes(4 + h, lo, hi, [(IP, e, 0), ("x", ua), ("x", ub)])
+                ts(("e1", lo, hi), bk(4 + h), 0.0, ALU.max, 63.0, ALU.min)
+            dma("y", lambda e_, T, c: [e_.dma_start(T.s_t[:], T.e1[:])], [("e1", 0, V)], [("s_t", 0, 2)], 26e4)
+            a2a("t")
+            dma("y", lambda e_, T, c: [e_.dma_start(T.en[:], T.l_t[:])], [("l_t", 0, 2)], [("en", 0, V)], 26e4)
+            boost[0] = OPT["due"][1]
+            strip("nb", "lb", "tb", 0, HS, OPT["strip"][1])
+            boost[0] = OPT["due"][2]
+            x = xbuf()
+            picked("xx", x, "xe" if both else "eb", ixb)
+            dma_add(("acc", 0, V), ("xx", x, x + V))
+            if not both:
+                picked("fb", 0, "hab", ixb)
+                terms += (([(HP16, "la", 0), (IN, "ta", 0), (IN, "fb", 0)], 6175.5, False),)
+            for (its, bias, half) in terms:
+                x = xbuf()
+                for (lo, hi) in HS:
+                    term(its, bias, half, lo, hi, ("xx", x + lo, x + hi))
+                dma_add(("acc", 0, V), ("xx", x, x + V))
+            boost[0] = 0.0
 
-    def home(e, T, q, out, s, l, base, cols):
-        r = [e.dma_start(out[16 * q:16 * q + 16, cols], T[s][base + q])]
+    tt(("dl", 0, 64), ua, ub, ALU.add)
+    send(lambda T, q: [(d, T.dl[:], T.dr[:, 64 * q:64 * q + 64]) for d in others(q)], [("dl", 0, 64)], [("dr", 0, 512)], 4000.0)
+
+    def own_layer(g, T, c):
+        ins = None
+        for k in range(N):
+            x = T.dl[:] if k == c["q"] else T.dr[:, 64 * k:64 * k + 64]
+            ins = g.tensor.matmul(A(T, bk(3, 64)), T.zq[:, 112 - 16 * k:240 - 16 * k], x, k == 0, k == N - 1)
+        return ins
+    add("p", own_layer, [("zq", 0, 240), ("dl", 0, 64), ("dr", 0, 512)], [bk(3, 64)], (0.5, 0.0, 0.0, 512))
+    cp(("dq", 0, 64), bk(3, 64))
+    for h, (lo, hi) in enumerate(HS):
+        passes(h, lo, hi, [(IP, "en", 0), ("x", ("dq", 0, 64))])
+        ts(("tf", lo, hi), bk(h), 0.0, ALU.max, 63.0, ALU.min)
+        dma("y", lambda e_, T, c, lo=lo, hi=hi: [e_.dma_start(T.tollout[:, lo:hi], T.tf[:, lo:hi])], [("tf", lo, hi)], [], 26e4)
+
+    def home(e_, T, q, s, l, cols):
+        r = [e_.dma_start(T.gain[16 * q:16 * q + 16, cols], T[s][q])]
         if q > 0:
-            r.append(e.dma_start(out[0:16 * q, cols], T[l][base:base + q]))
+            r.append(e_.dma_start(T.gain[0:16 * q, cols], T[l][0:q]))
         if q < N - 1:
-            r.append(e.dma_start(out[16 * q + 16:128, cols], T[l][base + q + 1:base + N]))
+            r.append(e_.dma_start(T.gain[16 * q + 16:128, cols], T[l][q + 1:N]))
         return r
-    dma("y", lambda e, T, c: [e.dma_start(T.s_t[:], T.e2[:])], [("e2", 0, V)], [D("s_t")], 26e4)
-    a2a("s_t", "l_t", 32e3)
-    dma("g", lambda e, T, c: home(e, T, c["q"], T.tollout, "s_t", "l_t", 0, slice(0, V)), [D("s_t"), D("l_t")], [], 52e4)
+    strip("nb", "lb", "tb", 0, PIECES, OPT["strip"][3])
+    pool[0] = OPT["pool"]
     for k, (lo, hi) in enumerate(PIECES):
+        for (a, b) in ((lo, min(hi, C)), (max(lo, C), hi)):
+            if a < b:
+                win, i = pick("xe", ixb, a, b)
+                tt(("acc", a, b), win, ("acc", a, b), ALU.add, idx=i)
+        npe = OPT["pe"][k]
+        sumb = bk(OPT["sumb"][k], hi - lo)
+        for n, (its, bias, half) in enumerate(terms):
+            if n < npe:
+                x = ("xx", V * n + lo, V * n + hi)
+                term(its, bias, half, lo, hi, x)
+                mm([(sumb, rot("idf", 0), x, n == 0, n == npe - 1)])
+                if n == npe - 1:
+                    tt(("acc", lo, hi), sumb, ("acc", lo, hi), ALU.add)
+            else:
+                term(its, bias, half, lo, hi, None)
         sg, lg, nby = "s_g%d" % k, "l_g%d" % k, 512.0 * (hi - lo)
-        dma("y", lambda e, T, c, sg=sg, lo=lo, hi=hi: [e.dma_start(T[sg][:], T.acc[:, lo:hi])], [("acc", lo, hi)], [D(sg)], nby)
-        a2a(sg, lg, nby / 8)
-        dma("y", lambda e, T, c, sg=sg, lg=lg, lo=lo, hi=hi: home(e, T, c["q"], T.gain, sg, lg, 0, slice(lo, hi)), [D(sg), D(lg)], [], nby)
+        dma("y", lambda e_, T, c, sg=sg, lo=lo, hi=hi: [e_.dma_start(T[sg][:], T.acc[:, lo:hi])], [("acc", lo, hi)], [(sg, 0, 2)], nby)
+        a2a("g%d" % k, own=False)
+        dma("y", lambda e_, T, c, sg=sg, lg=lg, lo=lo, hi=hi: home(e_, T, c["q"], sg, lg, slice(lo, hi)), [(sg, 0, 2), (lg, 0, 1)], [], nby)
     return ops
 
 
@@ -568,56 +629,91 @@ def queue_of(o):
     return "s" if o["eng"] == "a" else o["eng"]
 
 
-def schedule(ops):
+def schedule(ops, turns=0):
     n = len(ops)
-    pre = [dict(o["deps"]) for o in ops]
-    for i, o in enumerate(ops):
-        if o["kind"] == "a":
-            pre[i][o["from"]] = True
-    succ = [[] for _ in range(n)]
+    pre = [list(o["deps"].items()) + ([(o["from"], True)] if o["kind"] == "a" else []) for o in ops]
+    post = [[] for _ in ops]
     for i in range(n):
-        for j in pre[i]:
-            succ[j].append(i)
-    pr = [0.0] * n
+        for j, w in pre[i]:
+            post[j].append(i)
+    ways = [[w[0] for w in o["ways"]] if "ways" in o else [queue_of(o)] for o in ops]
+    figs = []
+    for (fix, cy, gam, pec, lat, slow) in FIGURES:
+        figs.append(([price(o["vec"], fix, cy, gam, pec) + 0.01 for o in ops],
+                     [[(j, ops[j]["lat"] * slow + lat if w else 0.0) for j, w in p] for p in pre], [o["lat"] * slow for o in ops]))
+    cost, gaps, tail = figs[0]
+    way = [ops[i]["lat"] + ops[i]["boost"] for i in range(n)]
     for i in range(n - 1, -1, -1):
-        pr[i] = ops[i]["cost"] + ops[i]["lat"] + max([pr[k] + (LAT if pre[k][i] else 0.0) for k in succ[i]] + [0.0])
-    x = OPT["seed"]
-    for i in range(n):
-        x = (x * 1103515245 + 12345) % 2147483648
-        if ops[i]["kind"] == "c":
-            pr[i] += OPT["noise"] * x / 2147483648.0
-    left = [len(p) for p in pre]
-    rdy = [0.0] * n
-    fin = [0.0] * n
-    start = [0.0] * n
-    free = {}
-    avail = [i for i in range(n) if left[i] == 0]
-    order = []
-    while avail:
-        best = None
-        for i in avail:
-            q = queue_of(ops[i])
-            s = rdy[i] if q is None else max(rdy[i], free.get(q, 0.0))
-            if best is None or s < best[0] - 1e-9 or (abs(s - best[0]) <= 1e-9 and pr[i] > pr[best[1]]):
-                best = (s, i)
-        s, i = best
-        q = queue_of(ops[i])
-        if q is not None:
-            for k in avail:
-                if queue_of(ops[k]) == q and pr[k] > pr[i] + OPT["margin"] and rdy[k] < s + OPT["look"] * ops[i]["cost"]:
-                    i = k
-            s = max(rdy[i], free.get(q, 0.0))
-            free[q] = s + ops[i]["cost"]
-        avail.remove(i)
-        start[i] = s
-        fin[i] = s + ops[i]["cost"] + ops[i]["lat"]
-        order.append(i)
-        for k in succ[i]:
-            rdy[k] = max(rdy[k], fin[i] + LAT if pre[k][i] else s)
-            left[k] -= 1
-            if left[k] == 0:
-                avail.append(k)
-    return order, start, fin
+        way[i] += cost[i]
+        for j, d in gaps[i]:
+            way[j] = max(way[j], way[i] + d)
+
+    def place(shift):
+        w = [0.0] * n
+        for i in range(n - 1, -1, -1):
+            x = way[i] + shift[i]
+            for k in post[i]:
+                if w[k] + 0.01 > x:
+                    x = w[k] + 0.01
+            w[i] = x
+        end, queue = [0.0] * n, [None] * n
+        rows = {q: ([], []) for q in "vspgy"}
+        for i in sorted(range(n), key=lambda k: -w[k]):
+            ready, c, best = 0.0, cost[i], None
+            for j, d in gaps[i]:
+                if end[j] + d > ready:
+                    ready = end[j] + d
+            for q in ways[i]:
+                s, k = ready, 0
+                if q:
+                    a, b = rows[q]
+                    k = len(a)
+                    while k and b[k - 1] > ready:
+                        k -= 1
+                    while k < len(a) and a[k] < s + c:
+                        s = b[k]
+                        k += 1
+                if best is None or s < best[0]:
+                    best = (s, k, q)
+            s, k, queue[i] = best
+            end[i] = s + c
+            if queue[i]:
+                rows[queue[i]][0].insert(k, s)
+                rows[queue[i]][1].insert(k, s + c)
+        order = sorted(range(n), key=lambda k: end[k] - cost[k])
+        total = 0.0
+        for f, (cs, gp, tl) in enumerate(figs):
+            e, free, last = [0.0] * n, dict.fromkeys("vspgy", 0.0), 0.0
+            for i in order:
+                q = queue[i]
+                s = free[q] if q else 0.0
+                for j, d in gp[i]:
+                    if e[j] + d > s:
+                        s = e[j] + d
+                e[i] = s = s + cs[i]
+                if q:
+                    free[q] = s
+                if s + tl[i] > last:
+                    last = s + tl[i]
+            total += math.log(last)
+        return total, order, queue, end
+
+    shift = [0.0] * n
+    best = place(shift)
+    x = 1
+    for _ in range(turns):
+        x = (x * 1103515245 + 12345) % 2 ** 31
+        at, width, by = (x >> 8) % n, (1, 3, 10, 30)[x >> 6 & 3], (300.0, 1500.0, 6000.0, -300.0, -1500.0, -6000.0, 700.0, -700.0)[x >> 3 & 7]
+        trial = [v + by if at <= i < at + width else v for i, v in enumerate(shift)]
+        plan = place(trial)
+        if plan[0] <= best[0]:
+            best, shift = plan, trial
+    total, order, queue, end = best
+    for i, o in enumerate(ops):
+        for eng, fn, vec in o.get("ways", ()):
+            if eng == queue[i]:
+                o["eng"], o["fn"] = eng, fn
+    return order, [end[i] - cost[i] for i in range(n)], [end[i] + tail[i] for i in range(n)]
 
 
 PLAN = {}
@@ -629,7 +725,7 @@ def rank_program(g, core, T, topo):
         return
     if not PLAN:
         PLAN["ops"] = build()
-        PLAN["order"] = schedule(PLAN["ops"])[0]
+        PLAN["order"] = schedule(PLAN["ops"], OPT["turns"])[0]
     ops, order = PLAN["ops"], PLAN["order"]
     c = dict(q=q, core=core, topo=topo)
     qs = {"v": g.vector, "s": g.scalar, "p": g.tensor, "g": g, "y": g.sync}

@@ -17,28 +17,29 @@ def slots(n, d):
 
 
 PIECES = ((0, 512), (512, 768), (768, 1024))
+TAIL = ((0, 512), (512, 896), (896, 1024))
 SCRATCH = {
-    "iot": sb(V, F32), "g16": sb(176, F32), "jj": sb(128, F32), "s2": sb(128, F32), "pci": sb(8, I32), "pcf": sb(16, F32),
+    "iot": sb(V, F32), "pci": sb(8, I32), "pcf": sb(16, F32),
     "idf": sb(256, F32), "idp": sb(256, BF), "idn": sb(256, BF), "id13": sb(256, BF), "id8": sb(256, BF), "id32": sb(128, BF),
     "ihp": sb(128, F16), "ihn": sb(128, F16), "t2f": sb(144, F32), "t2v": sb(144, BF), "ca": sb(144, BF), "cb": sb(144, BF),
-    "cl": sb(256, BF), "bo": sb(176, BF), "bs": sb(128, BF), "cv": sb(256, BF), "mf": sb(128, BF), "ma": sb(128, BF), "mb": sb(128, BF),
-    "xt": sb(16 * 128, BF), "k16": sb(128, F32), "ih1": sb(128, F16), "cx": sb(64, F16), "zq": sb(240, BF),
+    "cl": sb(256, BF), "wk": sb(13 * 128, BF), "ones": sb(H, BF),
+    "xt": sb(16 * 128, BF), "ih1": sb(128, F16), "cx": sb(64, F16),
     "oi": sb(128, I32), "ou": sb(128, U16), "ov": sb(192, I32), "li": sb(128, I32), "lf": sb(192, F32), "lu": sb(512, U16),
     "vi": sb(192, I32), "vf": sb(192, F32), "lv": sb(384, U16), "zh": sb(64, BF), "zt": sb(64, F32), "zl": sb(64, BF),
     "ix": sb(64, U16), "ixa": sb(128, U16), "ixb": sb(128, U16),
-    "hp": sb(V, BF), "hi": sb(2 * V, BF), "hab": sb(2 * V, BF), "da": sb(V, BF), "db": sb(V, BF), "dd": sb(4 * V, BF), "pz": sb(V, BF), "q16": sb(V, BF),
+    "hp": sb(V, BF), "hi": sb(2 * V, BF), "hab": sb(2 * V, BF), "da": sb(V, BF), "db": sb(V, BF), "de": sb(2 * V, BF), "dd": sb(4 * V, BF), "pz": sb(V, BF), "q16": sb(V, BF),
     "e0": sb(V, BF), "e1": sb(V, BF), "en": sb(V, BF), "tf": sb(V, F32),
     "pa": sb(V, F32), "pb": sb(V, F32), "pc": sb(V, F32), "w1": sb(2 * V, F32), "w2": sb(2 * V, F32),
     "gz": sb(V, F32), "uq": sb(V, F32), "nn": sb(V, F32), "na": sb(V, F32), "nb": sb(V, F32), "rm": sb(H, F32),
-    "lt": sb(4 * V, BF), "wt": sb(V, BF), "wr": sb(V, BF), "ms": sb(3 * V, BF), "g0": sb(3 * V, BF), "g1": sb(3 * V, BF),
-    "u4": sb(256, BF), "u9": sb(64, BF), "un": sb(128, BF), "mk": sb(128, BF), "dl": sb(64, BF), "dr": sb(N * 64, BF), "dq": sb(64, BF),
+    "lt": sb(4 * V, BF), "wt": sb(V, BF), "wr": sb(V, BF), "ms": sb(2 * V, BF), "g0": sb(4 * V, BF), "g1": sb(4 * V, BF),
+    "u4": sb(256, BF), "u9": sb(64, BF), "un": sb(128, BF), "mk": sb(128, BF), "dl": sb(64, BF), "dq": sb(64, BF),
     "la": sb(2 * V, F16), "lb": sb(V, F16), "ta": sb(2 * V, BF), "tb": sb(V, BF), "fa": sb(2 * V, BF), "fb": sb(V, BF),
     "eb": sb(2 * V, F32), "xe": sb(2 * V, F32), "xx": sb(4 * V, F32), "acc": sb(V, F32),
 }
-for _k, _n, _d in (("l", 16, I32), ("h", 128, BF), ("p", 128, BF), ("e", 128, BF), ("v", 24, I32), ("t", 128, BF)):
+for _k, _n, _d in (("l", 16, I32), ("h", 128, BF), ("p", 128, BF), ("e", 128, BF), ("v", 24, I32), ("t", 128, BF), ("d", 8, BF)):
     SCRATCH["s_" + _k] = slots(_n, _d)
     SCRATCH["l_" + _k] = slots(_n, _d)
-for _k, (_lo, _hi) in enumerate(PIECES):
+for _k, (_lo, _hi) in enumerate(TAIL):
     SCRATCH["s_g%d" % _k] = slots((_hi - _lo) // 8, F32)
     SCRATCH["l_g%d" % _k] = slots((_hi - _lo) // 8, F32)
 PS = ("bA", "bB", "bC", "bD")
@@ -49,7 +50,8 @@ SEMAPHORES = ["cv", "cs", "cp", "cg"] + ["d%d" % k for k in range(NDS)]
 
 CY, PEC, GAM, FIX, LAT = 1.0, 0.5, 1.55, 60.0, 90.0
 FIGURES = ((60.0, 0.95, 1.55, 0.48, 100.0, 1.0), (50.0, 0.85, 1.2, 0.43, 150.0, 1.3), (70.0, 1.2, 2.0, 0.6, 70.0, 0.9))
-OPT = dict(c=512, s=(768, 768, 768, 768), z=(512, 512, 1024, 1024), turns=6000, dde="v", wp=(1, 1, 1, 1), wg="sv", both=True, pe=(0, 0, 0), sumb=(4, 5, 4), pool=(6, 7, 4, 5),
+OPT = dict(c=512, s=(640, 640, 640, 640), z=(512, 1024, 1024, 1024), call=800.0, parts=TAIL, s0=640,
+           init=(((0, "s", (0, 512)), (1, "v", (512, 1024))), ((0, "s", (0, 256)), (1, "v", (256, 512)), (4, "s", (512, 768)), (5, "v", (768, 1024)))), turns=8000, dde="v", hie="svs", first=((0, 256), (256, 512), (512, 1024)), wp=(1, 1, 1, 1), wg="sv", both=True, pe=(0, 0, 0), sumb=(4, 5, 4), pool=(6, 7, 4, 5),
            lean=0.0, a0=True, early=110e3, due=(0.0, 0.0, 45e3, 0.0, 0.0), strip="vvvv")
 
 
@@ -185,8 +187,11 @@ def build():
             return g.iota(A(T, out), pattern, base, step)
         return add("g", fn, [], [out], 130.0 + 2 * CY * n_(out))
 
+    sent = []
+
     def send(pairs, rd, land, lat, one=False):
         k = len(ops)
+        sent.append(k)
 
         def fn(g, T, c):
             topo, core = c["topo"], c["core"]
@@ -202,7 +207,9 @@ def build():
                                              remote_sem=T.sem[ops[k + 1]["sem"]], src=s, dst=t))
             g.remote_dma_fused(trs, local_sem=T.sem[ops[k]["sem"]])
             return tot
-        i = add("g", fn, rd, [], 500.0, kind="r", lat=lat)
+        i = add("g", fn, rd, [], 500.0 if one else OPT["call"] * (1 + (len(sent) == 1)), kind="r", lat=lat)
+        if 1 < len(sent) < 5:
+            ops[i]["deps"][sent[-2]] = False
         j = add(None, None, [], land, 0.0, kind="a")
         ops[j]["from"] = i
         ops[j]["one"] = one
@@ -245,14 +252,10 @@ def build():
     dma("y", lambda e, T, c: [e.dma_start(T.s_e[:], T.toll[:])], [], [("s_e", 0, 2)], 60e4)
     iota(("pci", 0, 1), [[0, 1]], 0, 1)
     iota(("iot", 0, 256), [[1, 256]])
-    iota(("g16", 0, 128), [[1, 8], [0, 16]])
     for k in (1, 2, 3):
         act(("iot", 256 * k, 256 * k + 256), ("iot", 0, 256), AF.Identity, bias=256.0 * k)
     for k in "lhpe":
         a2a(k)
-    iota(("jj", 0, 128), [[8, 8], [0, 2], [1, 8]])
-    iota(("s2", 0, 128), [[0, 8], [4, 2], [0, 8]], -2)
-    iota(("k16", 0, 128), [[0, 8], [1, 16]])
 
     boost[0] = OPT["early"]
     P, PD, PM, PT, P0, PH, LA, LB, P16, RA, RB, PZ, MQ, PX, P7, WB = [("pcf", k, k + 1) for k in range(16)]
@@ -284,37 +287,72 @@ def build():
     ts(("t2v", 0, 144), I144, PT, ALU.is_equal, 1.0 / 17, ALU.mult)
     ts(PX, PM, 2.0, ALU.mult)
     ts(("cx", 0, 64), ("iot", 0, 64), 32.0, ALU.mult, PX, ALU.add)
-    ts(("bo", 0, 128), ("g16", 0, 128), PD, ALU.is_equal)
+    boost[0] = 0.0
+
+    def keep(out, x, pattern, op, base, step=1, fill=0.0):
+        add("g", lambda g, T, c: g.affine_select(A(T, out), A(T, x), pattern, op, fill, base, step), [x], [out], 170.0 + 2 * CY * n_(out))
+    iota(("ones", 0, H), [[0, H]], 1)
     for k in range(4):
-        x = ("xt", H * k, H * k + H)
-        iota(x, [[0, H]], 1)
-        add("g", lambda g, T, c, x=x, k=k: g.affine_select(A(T, x), A(T, x), [[-1, 4], [-16, 8], [0, 16]], ALU.is_equal, 0.0, -4 * k, 1),
-            [x], [x], 170.0 + 2 * CY * H)
+        keep(("xt", H * k, H * k + H), ("ones", 0, H), [[-1, 4], [-16, 8], [0, 16]], ALU.is_equal, -4 * k)
+    boost[0] = OPT["early"]
     ts(RA, PM, 7.5, ALU.is_lt)
     ts(RB, PM, 7.5, ALU.is_gt)
-    ts(("pcf", 6, 8), ("pcf", 9, 11), 16.0, ALU.mult)
-    ts(PH, P, 0.5, ALU.mult)
     ts(P16, PD, 16.0, ALU.mult)
     ts(("ca", 0, 144), I144, PT, ALU.is_equal, RA, ALU.mult)
     ts(("cb", 0, 144), I144, PT, ALU.is_equal, RB, ALU.mult)
     for k in range(2):
         ts(("cl", 128 * k, 128 * k + 128), I128, P16, ALU.is_equal)
-    ts(("mf", 0, 128), ("jj", 0, 128), PH, ALU.is_equal, 16.0, ALU.mult)
-    ts(("ma", 0, 128), ("jj", 0, 128), PH, ALU.is_equal, LA, ALU.mult)
-    ts(("mb", 0, 128), ("jj", 0, 128), PH, ALU.is_equal, LB, ALU.mult)
-    tt(("bs", 0, 128), ("bo", 0, 128), ("s2", 0, 128), ALU.mult)
     ts(P7, PM, 7.0, ALU.is_equal)
-    ts(WB, P7, 100.0, ALU.mult, -8.5, ALU.add)
-    ts(("cv", 0, 128), ("s2", 0, 128), -8.5, ALU.mult, -16.0, ALU.add)
-    ts(("cv", 128, 256), ("k16", 0, 128), 7.0, ALU.is_equal, 63.0, ALU.mult)
-    tt(("cv", 0, 128), ("cv", 0, 128), ("cv", 128, 256), ALU.add)
-    ts(("cv", 128, 256), ("bo", 0, 128), P7, ALU.mult)
-    tt(("cv", 0, 128), ("cv", 0, 128), ("cv", 128, 256), ALU.mult)
-    for nm in ("mf", "ma"):
-        tt((nm, 0, 128), (nm, 0, 128), ("cv", 0, 128), ALU.add)
-    ts(PZ, PM, 112.0, ALU.add)
-    ts(MQ, PD, [float], ALU.is_equal)
-    ts(("zq", 0, 240), ("iot", 0, 240), PZ, ALU.is_equal, MQ, ALU.mult)
+    ts(WB, P7, 100.0, ALU.mult, -17.0, ALU.add)
+    boost[0] = 0.0
+    BS, BW, BL, BO, LA2, LB2, MA, MB, MA3, MB3, NA, NB, S8 = [("wk", 128 * k, 128 * k + 128) for k in range(13)]
+
+    def by_half(tb, lo, hi):
+        iota(tb, [[0, 8], [hi - lo, 2], [0, 8]], lo)
+
+    def by_quarter(tb, even, odd):
+        iota(tb, [[0, 16], [odd - even, 2], [0, 4]], even)
+
+    def own_group(first, last):
+        x, n = ("wk", first[1], last[2]), (last[2] - first[1]) // 128
+        keep(x, x, [[0, n], [-16, 8], [0, 16]], ALU.is_ge, 0)
+        keep(x, x, [[0, n], [16, 8], [0, 16]], ALU.is_ge, 15, step=-1)
+
+    def row(tb, r):
+        keep(tb, tb, [[-16, 8], [0, 16]], ALU.is_equal, -r)
+
+    def paint(tb, r, value, part=0, parts=1):
+        keep(tb, tb, [[-16, 8], [H, parts], [0, 16 // parts]], ALU.not_equal, -r - H * part, fill=value)
+
+    by_half(BS, -2, 2)
+    by_half(BW, 2, 0)
+    by_half(BL, 0, 2)
+    own_group(BS, BL)
+    by_half(BO, 1, 1)
+    by_quarter(LA2, -2, 0)
+    by_quarter(LB2, 0, 2)
+    own_group(BO, LB2)
+    for tb in (MA, MB):
+        by_half(tb, 16, 16)
+        keep(tb, tb, [[-16, 8], [0, 2], [-2, 8]], ALU.is_equal, 0)
+    keep(MA, MA, [[16, 8], [0, 16]], ALU.is_gt, 8, step=-1)
+    keep(MB, MB, [[-16, 8], [0, 16]], ALU.is_ge, -8)
+    for tb, even, odd in ((MA3, 16, 0), (MB3, 0, 16), (NA, 16, 0), (NB, 0, 16)):
+        by_quarter(tb, even, odd)
+        row(tb, 0)
+    by_half(S8, -16, 16)
+    row(S8, 0)
+    for k in (0, 2):
+        paint(MA3, 8, -16.0, k, 4)
+        paint(MB3, 8, 16.0, k + 1, 4)
+    for tb, lo, hi in ((MA, 1.0, -33.0), (MA3, -15.0, -49.0)):
+        paint(tb, 7, lo, 0, 2)
+        paint(tb, 7, hi, 1, 2)
+    paint(NA, 7, -49.0)
+    for k in (0, 2):
+        paint(NA, 7, -15.0, k, 4)
+    for tb in (MA, MA3, NA):
+        paint(tb, 7, 128.0, 7, 16)
 
     boost[0] = 0.0
     dma("y", lambda e, T, c: [e.dma_start(T.li[:, 0:64], T.l_l[:, 0:64, :])], [("l_l", 0, 2)], [("li", 0, 64)], 32e3)
@@ -335,16 +373,22 @@ def build():
         return (nm, 2 * lo + k, 2 * hi, 2)
 
     IP, IN = rot("idp", 0), rot("idn", 0)
-    DEL = 0.125
-    for h, (lo, hi) in enumerate(HS):
-        mov("s", lane("hi", 0, lo, hi), ("hp", 0, V), idx=lst("lu", 0, 0, lo, hi))
+    DEL, MID = 0.125, -511.5 / 8192
+    for (lo, hi), (ba, bb) in zip(OPT["first"], ((0, 4), (1, 5), (2, 3))):
+        mov(OPT["hie"][lo // 256], lane("hi", 0, lo, hi), ("hp", 0, V), idx=lst("lu", 0, 0, lo, hi))
         mov("v", lane("hi", 1, lo, hi), ("hp", 0, V), idx=lst("lu", 0, 1, lo, hi))
-        passes(h, lo, hi, [(rot("idp", 1), "hp", 0), (IN, "hi", 0, 2)])
-        act(("da", lo, hi), bk(h), AF.Abs)
-        passes(4 + h, lo, hi, [(rot("idp", 1), "hp", 0), (IN, "hi", 1, 2)])
-        act(("db", lo, hi), bk(4 + h), AF.Abs)
-        passes(4 + h, lo, hi, [(IN, "da", 0), (IP, "db", 0)])
-        mov(OPT["dde"], ("dd", lo, hi), bk(4 + h), bias=DEL)
+        passes(ba, lo, hi, [(rot("idp", 1), "hp", 0), (IN, "hi", 0, 2)])
+        act(("da", lo, hi), bk(ba, hi - lo), AF.Abs)
+        passes(bb, lo, hi, [(rot("idp", 1), "hp", 0), (IN, "hi", 1, 2)])
+        act(("db", lo, hi), bk(bb, hi - lo), AF.Abs)
+        passes(bb, lo, hi, [(IN, "da", 0), (IP, "db", 0)])
+        mov(OPT["dde"], ("dd", lo, hi), bk(bb, hi - lo), bias=DEL)
+
+    def with_edges(rnd):
+        x = ("de", V * rnd, V * rnd + V)
+        dma("y", lambda e, T, c: [e.dma_start(A(T, x), T.da[:])], [("da", 0, V)], [x], 26e4)
+        dma_add(x, (("e0", "e1")[rnd], 0, V))
+    with_edges(0)
 
     def turn(out, x, t):
         (o, a, b), (i, c_, d) = out, x
@@ -393,10 +437,10 @@ def build():
         clo, chi = CH[0] if lo < C else CH[1]
         return (w, 2 * clo, 2 * chi), (ix[0], ix[1] + lo // 16, ix[1] + hi // 16)
 
-    def step(t, p, w, ix, sel, out, op, op_r, S, Z):
+    def step(t, p, w, ix, sel, out, op, op_r, S, Z, bias=0.0):
         def part(lo, hi):
             win, i = pick(w, ix, lo, hi)
-            act((sel, lo, hi), win, AF.Identity, idx=i)
+            act((sel, lo, hi), win, AF.Identity, bias=bias, idx=i)
             return [tt((out, lo, hi), (PS[0], lo, hi), (sel, lo, hi), op_r)]
         if S < V:
             mov("s", ("uq", S, V), (PS[0], S, V))
@@ -404,16 +448,19 @@ def build():
         if S < V:
             win, i = pick(w, ix, S, V)
             tt((out, S, V), win, ("uq", S, V), op, idx=i)
-            part(C, S)
+            if C < S:
+                part(C, S)
         else:
             part(C, 768)
             part(768, V)
 
     IX = ("ix", 0)
-    votes(0, "pz", "w1", IX, V)
-    for (lo, hi, e) in ((0, C, "s"), (C, 768, "s"), (768, V, "v")):
-        win, i = pick("w1", IX, lo, hi)
-        mov(e, ("q16", lo, hi), win, bias=-128.0 - DEL, idx=i)
+    for h in (1, 0):
+        passes(h, H * h, H * h + H, [(rot("id8", 1), "hp", 0), (IP, "da", 0), (IP, "e0", 0)])
+    step(0, "pz", "w2", ("ixb", 0), "nn", "pa", ALU.add, ALU.add, OPT["s0"], V)
+    for (lo, hi) in CH:
+        win, i = pick("w2", ("ixb", 0), lo, hi)
+        mov("f", ("q16", lo, hi), win, bias=-128.0 - DEL, idx=i)
 
     cp(("vf", 0, 192), ("vi", 0, 192))
     mm([(bk(7, 128, 128 * (t - 1)), rot("idf", t), ("vf", 0, 128), True, True) for t in (1, 2, 3)]
@@ -426,50 +473,55 @@ def build():
 
     def forest(e, rnd, second, un):
         Z, S = OPT["z"][2 * rnd + second], OPT["s"][2 * rnd + second]
-        for h, (lo, hi) in enumerate(HS):
-            its = [(IP, "q16", 0), (IP, e, 0)][::-1 if rnd == 0 else 1]
-            passes(h, lo, hi, [(rot("id8", 1), "hp", 0), (IP, "da", 0)] + its + ([("x", U9), ("x", un)] if second else []))
-            mov("sv"[h], ("pa", lo, hi), bk(h), bias=128.0 - 511.5 / 8192)
+        for b, en, (lo, hi) in OPT["init"][second] if rnd or second else ():
+            its = [(IP, "de", V * rnd), ("x", U9), ("x", un)] if second else [(IP, "da", 0), (IP, e, 0)]
+            passes(b, lo, hi, [(rot("id8", 1), "hp", 0), (IP, "q16", 0)] + its)
+            mov(en, ("pa", lo, hi), bk(b, hi - lo), bias=128.0)
         for (t, p, p2) in ((1, "pa", "pb"), (2, "pb", "pc")):
             for h in (1, 0):
-                passes(h, H * h, H * h + H, [(rot("idp", t), "da", 0), (rot("idp", t), e, 0)]
+                passes(h, H * h, H * h + H, ([(rot("idp", t), "de", V * rnd)] if second or t > 1 else [(rot("idp", t), "da", 0), (rot("idp", t), e, 0)])
                        + ([(rot("id13", 2), "hp", 0)] if t == 1 else []) + ([("x", ("mk", 64 * t - 64, 64 * t))] if second else []))
             step(t, p, "w1", IX, "nn", p2, ALU.add, ALU.add, S, Z)
         ix = ("ixb" if second else "ixa", 64 * rnd)
         if second:
+            for (lo, hi) in HS:
+                passes(4, lo, hi, [(BO, "lt", 2 * V)])
+                act(("wt", lo, hi), bk(4), AF.Sign, bias=-8.5)
             votes(3, "pc", "w2", ix, Z, rnd == 0)
             boost[0] = OPT["due"][0] * (1 - rnd)
-            for (lo, hi) in (PIECES if rnd else CH):
+            for (lo, hi) in CH:
                 win, i = pick("w2", ix, lo, hi)
-                mov("f", ("nb", lo, hi), win, idx=i)
+                mov("f", ("nb", lo, hi), win, bias=MID, idx=i)
             boost[0] = 0.0
             return ix
         for h in (1, 0):
-            passes(h, H * h, H * h + H, [(rot("idn", 3), "da", 0), (rot("idn", 3), e, 0), ("x", ("zh", 0, 64)), ("x", ("zl", 0, 64))])
-        step(3, "pc", "w1", ix, "na", "wt", ALU.is_gt, ALU.is_lt, S, Z)
+            passes(h, H * h, H * h + H, [(rot("idn", 3), "de", V * rnd), ("x", ("zh", 0, 64)), ("x", ("zl", 0, 64))])
+        step(3, "pc", "w1", ix, "na", "wt", ALU.is_gt, ALU.is_lt, S, Z, MID)
         if S < V:
             win, i = pick("w1", ix, S, V)
-            mov("f", ("na", S, V), win, idx=i)
-        for h, (lo, hi) in enumerate(HS):
-            passes(2 + h, lo, hi, [(("bo", 0, 128), "wt", 0)])
-            act(("wr", lo, hi), bk(2 + h), AF.Sign, bias=WB)
+            mov("f", ("na", S, V), win, bias=MID, idx=i)
+        for b, (lo, hi) in zip((4, 5, 3), PIECES):
+            passes(b, lo, hi, [(BL, "lt", 3 * V), (BW, "wt", 0)])
+            act(("wr", lo, hi), bk(b, hi - lo), AF.Sign, bias=WB)
         return ix
 
     def walk(outs, parts, last_=False):
-        BS = ("bs", 0, 128)
-        for h, (lo, hi) in enumerate(HS):
-            passes(4 + h, lo, hi, [(BS, "lt", 3 * V), (("mf", 0, 128), "wr", 0)][::-1 if len(outs) == 1 else 1])
-            sign("f", ("ms", 2 * V + lo, 2 * V + hi), bk(4 + h))
+        second = len(outs) == 1
         for t in (3, 2, 1):
             b0 = V * (t - 1)
+            win = ("ms", b0, b0 + V) if t < 3 else ("lt", 3 * V, 4 * V) if second else ("wr", 0, V)
+            g0 = b0 + V * (t == 3 and second)
             for k, (lo, hi) in enumerate(parts):
                 e = "f"
-                mov(OPT["wg"][0], ("g0", b0 + lo, b0 + hi), ("ms", b0, b0 + V), idx=lst("lv", t - 1, 0, lo, hi))
-                mov(OPT["wg"][1], ("g1", b0 + lo, b0 + hi), ("ms", b0, b0 + V), idx=lst("lv", t - 1, 1, lo, hi))
+                mov(OPT["wg"][0], ("g0", g0 + lo, g0 + hi), win, idx=lst("lv", t - 1, 0, lo, hi))
+                mov(OPT["wg"][1], ("g1", g0 + lo, g0 + hi), win, idx=lst("lv", t - 1, 1, lo, hi))
                 js = range(lo // 64, hi // 64)
                 if t > 1:
                     b = (((4, 5, 3), (0, 1, 3))[t - 2] if not last_ else (0, 1, 3))[k]
-                    passes(b, lo, hi, [(BS, "lt", b0), (("ma", 0, 128), "g0", b0), (("mb", 0, 128), "g1", b0)])
+                    if t == 3 and second:
+                        passes(b, lo, hi, [(NA, "g0", b0), (NB, "g1", b0), (S8, "wt", 0), (LA2, "g0", g0), (LB2, "g1", g0)])
+                    else:
+                        passes(b, lo, hi, [(BS, "lt", b0), ((MA, MA3)[t - 2], "g0", b0), ((MB, MB3)[t - 2], "g1", b0)])
                     sign(e, ("ms", b0 - V + lo, b0 - V + hi), bk(b, hi - lo))
                     mm([(bk(2, 64), ("cl", 128 - 16 * (t - 1) - j, 256 - 16 * (t - 1) - j), ("ms", b0 - V + 64 * j, b0 - V + 64 * j + 64),
                          t == 3 and j == 0, False) for j in js])
@@ -559,6 +611,7 @@ def build():
                 passes(4 + h, lo, hi, [(IP, e, 0), ("x", ua), ("x", ub)])
                 ts(("e1", lo, hi), bk(4 + h), 0.0, ALU.max, 63.0, ALU.min)
             dma("y", lambda e_, T, c: [e_.dma_start(T.s_t[:], T.e1[:])], [("e1", 0, V)], [("s_t", 0, 2)], 26e4)
+            with_edges(1)
             a2a("t")
             dma("y", lambda e_, T, c: [e_.dma_start(T.en[:], T.l_t[:])], [("l_t", 0, 2)], [("en", 0, V)], 26e4)
             boost[0] = OPT["due"][1]
@@ -578,20 +631,13 @@ def build():
             boost[0] = 0.0
 
     tt(("dl", 0, 64), ua, ub, ALU.add)
-    send(lambda T, q: [(d, T.dl[:], T.dr[:, 64 * q:64 * q + 64]) for d in others(q)], [("dl", 0, 64)], [("dr", 0, 512)], 4000.0)
-
-    def own_layer(g, T, c):
-        ins = None
-        for k in range(N):
-            x = T.dl[:] if k == c["q"] else T.dr[:, 64 * k:64 * k + 64]
-            ins = g.tensor.matmul(A(T, bk(3, 64)), T.zq[:, 112 - 16 * k:240 - 16 * k], x, k == 0, k == N - 1)
-        return ins
-    add("p", own_layer, [("zq", 0, 240), ("dl", 0, 64), ("dr", 0, 512)], [bk(3, 64)], (0.5, 0.0, 0.0, 512))
-    cp(("dq", 0, 64), bk(3, 64))
+    dma("y", lambda e_, T, c: [e_.dma_start(T.s_d[:], T.dl[:])], [("dl", 0, 64)], [("s_d", 0, 2)], 16e3)
+    a2a("d")
+    dma("a", lambda e_, T, c: [e_.dma_start(T.dq[:], T.l_d[:])], [("l_d", 0, 2)], [("dq", 0, 64)], 16e3)
     for h, (lo, hi) in enumerate(HS):
         passes(h, lo, hi, [(IP, "en", 0), ("x", ("dq", 0, 64))])
         ts(("tf", lo, hi), bk(h), 0.0, ALU.max, 63.0, ALU.min)
-        dma("y", lambda e_, T, c, lo=lo, hi=hi: [e_.dma_start(T.tollout[:, lo:hi], T.tf[:, lo:hi])], [("tf", lo, hi)], [], 26e4)
+        dma("a", lambda e_, T, c, lo=lo, hi=hi: [e_.dma_start(T.tollout[:, lo:hi], T.tf[:, lo:hi])], [("tf", lo, hi)], [], 26e4)
 
     def home(e_, T, q, s, l, cols):
         r = [e_.dma_start(T.gain[16 * q:16 * q + 16, cols], T[s][q])]
@@ -600,9 +646,9 @@ def build():
         if q < N - 1:
             r.append(e_.dma_start(T.gain[16 * q + 16:128, cols], T[l][q + 1:N]))
         return r
-    strip("nb", "lb", "tb", 0, PIECES, OPT["strip"][3])
+    strip("nb", "lb", "tb", 0, OPT["parts"], OPT["strip"][3])
     pool[0] = OPT["pool"]
-    for k, (lo, hi) in enumerate(PIECES):
+    for k, (lo, hi) in enumerate(OPT["parts"]):
         for (a, b) in ((lo, min(hi, C)), (max(lo, C), hi)):
             if a < b:
                 win, i = pick("xe", ixb, a, b)
@@ -618,6 +664,7 @@ def build():
                     tt(("acc", lo, hi), sumb, ("acc", lo, hi), ALU.add)
             else:
                 term(its, bias, half, lo, hi, None)
+    for k, (lo, hi) in enumerate(TAIL):
         sg, lg, nby = "s_g%d" % k, "l_g%d" % k, 512.0 * (hi - lo)
         dma("y", lambda e_, T, c, sg=sg, lo=lo, hi=hi: [e_.dma_start(T[sg][:], T.acc[:, lo:hi])], [("acc", lo, hi)], [(sg, 0, 2)], nby)
         a2a("g%d" % k, own=False)
@@ -681,7 +728,7 @@ def schedule(ops, turns=0):
                 rows[queue[i]][0].insert(k, s)
                 rows[queue[i]][1].insert(k, s + c)
         order = sorted(range(n), key=lambda k: end[k] - cost[k])
-        total = 0.0
+        total, ends = 0.0, []
         for f, (cs, gp, tl) in enumerate(figs):
             e, free, last = [0.0] * n, dict.fromkeys("vspgy", 0.0), 0.0
             for i in order:
@@ -696,19 +743,48 @@ def schedule(ops, turns=0):
                 if s + tl[i] > last:
                     last = s + tl[i]
             total += math.log(last)
-        return total, order, queue, end
+            ends.append(e)
+        return total, order, queue, end, w, ends
+
+    def held_up(plan):
+        total, order, queue, end, w, ends = plan
+        before, seen = {}, {}
+        for i in order:
+            before[i], seen[queue[i]] = seen.get(queue[i]), i
+        pairs = []
+        for (cs, gp, tl), e in zip(figs, ends):
+            i = max(range(n), key=lambda k: e[k] + tl[k])
+            while i is not None:
+                nxt = [j for j, d in gp[i] if abs(e[j] + d + cs[i] - e[i]) < 1e-3]
+                if not nxt and queue[i] and before[i] is not None:
+                    pairs.append((i, before[i]))
+                    nxt = [before[i]]
+                i = nxt[0] if nxt else None
+        return pairs
 
     shift = [0.0] * n
     best = place(shift)
+    pairs = held_up(best)
     x = 1
-    for _ in range(turns):
+    for turn in range(turns):
         x = (x * 1103515245 + 12345) % 2 ** 31
-        at, width, by = (x >> 8) % n, (1, 3, 10, 30)[x >> 6 & 3], (300.0, 1500.0, 6000.0, -300.0, -1500.0, -6000.0, 700.0, -700.0)[x >> 3 & 7]
-        trial = [v + by if at <= i < at + width else v for i, v in enumerate(shift)]
+        trial = list(shift)
+        if turn % 2 and pairs:
+            i, j = pairs[(x >> 8) % len(pairs)]
+            by = max(best[4][j] - best[4][i], 0.0) + (1.0, 300.0, 1000.0, 3000.0)[x >> 4 & 3]
+            if x >> 6 & 1:
+                trial[i] += by
+            else:
+                trial[j] -= by
+        else:
+            at, width, by = (x >> 8) % n, (1, 3, 10, 30)[x >> 6 & 3], (300.0, 1500.0, 6000.0, -300.0, -1500.0, -6000.0, 700.0, -700.0)[x >> 3 & 7]
+            for i in range(at, min(n, at + width)):
+                trial[i] += by
         plan = place(trial)
         if plan[0] <= best[0]:
             best, shift = plan, trial
-    total, order, queue, end = best
+            pairs = held_up(best)
+    total, order, queue, end = best[:4]
     for i, o in enumerate(ops):
         for eng, fn, vec in o.get("ways", ()):
             if eng == queue[i]:

import math
from concourse.bass import DstId, RemoteDMATransfer
from concourse.mybir import AluOpType as ALU, ActivationFunctionType as AF

N = 8
V = 1024
H = 512
F32, BF, F16, I32, U16 = "float32", "bfloat16", "float16", "int32", "uint16"


def sb(n, d):
    return ("sbuf", [128, n], d)


def slots(n, d):
    return ("dram", [N, 128, n], d)


PIECES = ((0, 512), (512, 768), (768, 1024))
TAIL = ((0, 512), (512, 896), (896, 1024))
SCRATCH = {
    "iot": sb(V, F32), "pci": sb(8, I32), "pcf": sb(16, F32),
    "idf": sb(256, F32), "idp": sb(256, BF), "idn": sb(256, BF), "id13": sb(256, BF), "id8": sb(256, BF), "id32": sb(128, BF),
    "ihp": sb(128, F16), "ihn": sb(128, F16), "t2f": sb(144, F32), "t2v": sb(144, BF), "ca": sb(144, BF), "cb": sb(144, BF),
    "cl": sb(256, BF), "wk": sb(13 * 128, BF), "ones": sb(H, BF),
    "xt": sb(16 * 128, BF), "ih1": sb(128, F16), "cx": sb(64, F16),
    "oi": sb(128, I32), "ou": sb(128, U16), "ov": sb(192, I32), "li": sb(128, I32), "lf": sb(192, F32), "lu": sb(512, U16),
    "vi": sb(192, I32), "vf": sb(192, F32), "lv": sb(384, U16), "zh": sb(64, BF), "zt": sb(64, F32), "zl": sb(64, BF),
    "ix": sb(64, U16), "ixa": sb(128, U16), "ixb": sb(128, U16),
    "hp": sb(V, BF), "hi": sb(2 * V, BF), "hab": sb(2 * V, BF), "da": sb(V, BF), "db": sb(V, BF), "de": sb(2 * V, BF), "dd": sb(4 * V, BF), "pz": sb(V, BF), "q16": sb(V, BF),
    "e0": sb(V, BF), "e1": sb(V, BF), "en": sb(V, BF), "tf": sb(V, F32),
    "pa": sb(V, F32), "pb": sb(V, F32), "pc": sb(V, F32), "w1": sb(2 * V, F32), "w2": sb(2 * V, F32),
    "gz": sb(V, F32), "uq": sb(V, F32), "nn": sb(V, F32), "na": sb(V, F32), "nb": sb(V, F32), "rm": sb(H, F32),
    "lt": sb(4 * V, BF), "wt": sb(V, BF), "wr": sb(V, BF), "ms": sb(2 * V, BF), "g0": sb(4 * V, BF), "g1": sb(4 * V, BF),
    "u4": sb(256, BF), "u9": sb(64, BF), "un": sb(128, BF), "mk": sb(128, BF), "dl": sb(64, BF), "dq": sb(64, BF),
    "la": sb(2 * V, F16), "lb": sb(V, F16), "ta": sb(2 * V, BF), "tb": sb(V, BF), "fa": sb(2 * V, BF), "fb": sb(V, BF),
    "eb": sb(2 * V, F32), "xe": sb(2 * V, F32), "xx": sb(4 * V, F32), "acc": sb(V, F32),
}
for _k, _n, _d in (("l", 16, I32), ("h", 128, BF), ("p", 128, BF), ("e", 128, BF), ("v", 24, I32), ("t", 128, BF), ("d", 8, BF)):
    SCRATCH["s_" + _k] = slots(_n, _d)
    SCRATCH["l_" + _k] = slots(_n, _d)
for _k, (_lo, _hi) in enumerate(TAIL):
    SCRATCH["s_g%d" % _k] = slots((_hi - _lo) // 8, F32)
    SCRATCH["l_g%d" % _k] = slots((_hi - _lo) // 8, F32)
PS = ("bA", "bB", "bC", "bD")
for _k in PS:
    SCRATCH[_k] = ("psum", [128, V], F32)
NDS = 100
SEMAPHORES = ["cv", "cs", "cp", "cg"] + ["d%d" % k for k in range(NDS)]

CY, PEC, GAM, FIX, LAT = 1.0, 0.5, 1.55, 60.0, 90.0
FIGURES = ((60.0, 0.95, 1.55, 0.48, 100.0, 1.0), (50.0, 0.85, 1.2, 0.43, 150.0, 1.3), (70.0, 1.2, 2.0, 0.6, 70.0, 0.9))
OPT = dict(c=512, s=(640, 640, 640, 640), z=(512, 1024, 1024, 1024), call=800.0, parts=TAIL, s0=640,
           init=(((0, "s", (0, 512)), (1, "v", (512, 1024))), ((0, "s", (0, 256)), (1, "v", (256, 512)), (4, "s", (512, 768)), (5, "v", (768, 1024)))), turns=8000, dde="v", hie="svs", first=((0, 256), (256, 512), (512, 1024)), wp=(1, 1, 1, 1), wg="sv", both=True, pe=(0, 0, 0), sumb=(4, 5, 4), pool=(6, 7, 4, 5),
           lean=0.0, a0=True, early=110e3, due=(0.0, 0.0, 45e3, 0.0, 0.0), strip="vvvv")


def price(v, fix=FIX, cy=CY, gam=GAM, pec=PEC):
    if isinstance(v, tuple):
        return fix * v[0] + cy * (v[1] + gam * v[2]) + pec * v[3]
    return v


def build():
    ops = []
    last = {}
    nsem = [0]
    boost = [0.0]

    def span(r):
        nm, lo, hi = r[0], r[1], r[2]
        if nm in PS:
            return nm, lo // H * H, (hi + H - 1) // H * H, None, True
        return nm, lo, hi, (lo % 2 if len(r) > 3 and r[3] == 2 else None), False

    def add(eng, fn, rd, wr, cost, kind="c", lat=0.0):
        i = len(ops)
        deps = {}
        for (rs, w) in ((rd, False), (wr, True)):
            for r in rs:
                nm, lo, hi, lane, bank = span(r)
                for (l2, h2, j, w2, lane2) in last.get(nm, ()):
                    if l2 < hi and lo < h2 and (lane is None or lane2 is None or lane == lane2):
                        same = ops[j]["eng"] == eng != "f" and kind == "c" and ops[j]["kind"] == "c"
                        if w2 and not w:
                            deps[j] = True
                        elif w or w2 or (bank and not same):
                            deps[j] = deps.get(j, False) or not (same and eng == "p")
        for (rs, w) in ((rd, False), (wr, True)):
            for r in rs:
                nm, lo, hi, lane, bank = span(r)
                lst = last.setdefault(nm, [])
                if w:
                    lst[:] = [e for e in lst if not (lo - (lane or 0) <= e[0] and e[1] <= hi and (lane is None or lane == e[4]))]
                lst.append((lo, hi, i, w, lane))
        o = dict(eng=eng, fn=fn, deps=deps, boost=boost[0], vec=cost, cost=price(cost), kind=kind, lat=lat, nm=(wr or rd)[0][0] if (wr or rd) else "")
        if kind != "c":
            o["sem"] = "d%d" % nsem[0]
            nsem[0] += 1
        ops.append(o)
        return i

    def A(T, r):
        if isinstance(r, (int, float)):
            return r
        nm, lo, hi = r[0], r[1], r[2]
        st = r[3] if len(r) > 3 else 1
        p = r[4] if len(r) > 4 else 128
        return T[nm][0:p, lo:hi:st] if st != 1 else T[nm][0:p, lo:hi]

    def n_(r):
        st = r[3] if len(r) > 3 else 1
        return (r[2] - r[1] + st - 1) // st

    def two(r):
        return SCRATCH[r[0]][2] in (BF, F16, U16)

    def src(T, x, idx):
        return A(T, x) if idx is None else A(T, x).indirect(A(T, idx))

    def aps(*xs):
        return [x for x in xs if isinstance(x, tuple)]

    def vcost(out, idx, base):
        if idx is not None:
            return (1, 0.0, n_(out), 0.0)
        return (1, max(64.0, n_(out) * base), 0.0, 0.0)

    def tt(out, x, y, op, idx=None):
        return add("v", lambda g, T, c: g.vector.tensor_tensor(A(T, out), src(T, x, idx), A(T, y), op),
                   aps(x, y, idx), [out], vcost(out, idx, 1.0 if x[0] in PS or y[0] in PS else 2.0))

    def ts(out, x, s1, op0, s2=None, op1=None, idx=None):
        def fn(g, T, c):
            a = s1[0](c["q"]) if isinstance(s1, list) else A(T, s1)
            if op1 is None:
                return g.vector.tensor_scalar(A(T, out), src(T, x, idx), a, None, op0)
            return g.vector.tensor_scalar(A(T, out), src(T, x, idx), a, A(T, s2), op0, op1)
        return add("v", fn, aps(x, s1, s2, idx), [out], vcost(out, idx, 0.5 if two(out) and two(x) else 1.0))

    def cp(out, x, idx=None):
        return add("v", lambda g, T, c: g.vector.tensor_copy(A(T, out), src(T, x, idx)),
                   aps(x, idx), [out], vcost(out, idx, 0.5 if two(out) and two(x) else 1.0))

    def act(out, x, f, bias=0.0, scale=1.0, idx=None):
        return add("s", lambda g, T, c: g.scalar.activation(A(T, out), src(T, x, idx), f, bias=A(T, bias), scale=A(T, scale)),
                   aps(x, idx, bias, scale), [out], vcost(out, idx, 1.0))

    def either(eng, on_s, on_v, rd, out, cost):
        i = add(eng, on_v if eng == "v" else on_s, rd, [out], cost)
        if eng == "f":
            ops[i]["ways"] = [("s", on_s, cost), ("v", on_v, cost)]
        return i

    def mov(eng, out, x, bias=0.0, scale=1.0, idx=None):
        return either(eng, lambda g, T, c: g.scalar.activation(A(T, out), src(T, x, idx), AF.Identity, bias=bias, scale=scale),
                      lambda g, T, c: g.vector.tensor_scalar(A(T, out), src(T, x, idx), scale, bias, ALU.mult, ALU.add),
                      aps(x, idx), out, vcost(out, idx, 1.0))

    def sign(eng, out, x):
        return either(eng, lambda g, T, c: g.scalar.activation(A(T, out), A(T, x), AF.Sign),
                      lambda g, T, c: g.vector.tensor_scalar(A(T, out), A(T, x), -1.0, 1.0, ALU.max, ALU.min), [x], out, vcost(out, None, 1.0))

    def mm(items):
        def fn(g, T, c):
            ins = None
            for (o, l, r, s0, s1) in items:
                ins = g.tensor.matmul(A(T, o), A(T, l), A(T, r), s0, s1)
            return ins
        cost = (0.5, 0.0, 0.0, sum(max(64, n_(r)) * (1 if two(r) else 4) for (o, l, r, s0, s1) in items))
        rd = []
        for (o, l, r, s0, s1) in items:
            rd += [l, r]
        return add("p", fn, rd, [items[0][0]], cost)

    def dma(q, fn, rd, wr, nbytes):
        return add(q, fn, rd, wr, 60.0 if q != "g" else 500.0, kind="d", lat=2000.0 + nbytes / 400.0)

    def dma_add(out, x):
        dma("g", lambda e, T, c: [e.dma_start(A(T, out), A(T, x), accum_op=ALU.add)], [x, out], [out], 1024.0 * n_(out))

    def iota(out, pattern, base=0, step=0):
        small = SCRATCH[out[0]][2] != I32
        def fn(g, T, c):
            if small:
                return g.iota(A(T, out), pattern, base, step, allow_small_or_imprecise_dtypes=True)
            return g.iota(A(T, out), pattern, base, step)
        return add("g", fn, [], [out], 130.0 + 2 * CY * n_(out))

    sent = []

    def send(pairs, rd, land, lat, one=False):
        k = len(ops)
        sent.append(k)

        def fn(g, T, c):
            topo, core = c["topo"], c["core"]
            trs = []
            tot = 0
            for n, (d, s, t) in enumerate(pairs(T, c["q"])):
                dc = T.cores[d]
                rid, pid = topo.addr(dc, core)
                en = topo.engines(core, dc)
                m = topo.mask(core, dc) if one else 1 << en[n]
                tot += len(en) if one else 1
                trs.append(RemoteDMATransfer(dst_ids=[DstId(rid=rid, pnc=pid)], dma_engine_mask=m,
                                             remote_sem=T.sem[ops[k + 1]["sem"]], src=s, dst=t))
            g.remote_dma_fused(trs, local_sem=T.sem[ops[k]["sem"]])
            return tot
        i = add("g", fn, rd, [], 500.0 if one else OPT["call"] * (1 + (len(sent) == 1)), kind="r", lat=lat)
        if 1 < len(sent) < 5:
            ops[i]["deps"][sent[-2]] = False
        j = add(None, None, [], land, 0.0, kind="a")
        ops[j]["from"] = i
        ops[j]["one"] = one
        return j

    def others(q):
        return [d % N for d in range(q + 1, q + N)]

    def a2a(k, own=True):
        s, l = "s_" + k, "l_" + k
        nby = 128 * SCRATCH[s][1][2] * (2 if SCRATCH[s][2] == BF else 4)
        send(lambda T, q: [(d, T[s][d], T[l][q]) for d in others(q)], [(s, 0, 2)], [(l, 0, 1)], 2200.0 + nby / 25.0)
        if own:
            dma("y", lambda e, T, c: [e.dma_start(T[l][c["q"]], T[s][c["q"]])], [(s, 0, 2)], [(l, 1, 2)], nby)

    HS = ((0, H), (H, V))

    def bk(k, n=H, lo=0):
        return (PS[k // 2], H * (k % 2) + lo, H * (k % 2) + lo + n)

    def rot(nm, t):
        return (nm, 16 * t, 16 * t + 128)

    def passes(bank, lo, hi, items):
        for n, it in enumerate(items):
            s0, s1 = n == 0, n == len(items) - 1
            if it[0] == "x":
                js = range(lo // 64, hi // 64)
                mm([(bk(bank, 64, 64 * j - lo), ("xt", 128 * j, 128 * j + 128), it[1], False, s1 and j == js[-1]) for j in js])
            else:
                st = it[3] if len(it) > 3 else 1
                mm([(bk(bank, hi - lo), it[0], (it[1], it[2] + st * lo, it[2] - it[2] % st + st * hi, st), s0, s1)])

    dma("y", lambda e, T, c: [e.dma_start(T.s_l[:, 0:64, :], T.sa[:])], [], [("s_l", 0, 1)], 4e4)
    dma("a", lambda e, T, c: [e.dma_start(T.s_l[:, 64:128, :], T.sb[:])], [], [("s_l", 1, 2)], 4e4)
    dma("y", lambda e, T, c: [e.dma_start(T.s_h[:], T.hf[:])], [], [("s_h", 0, 2)], 26e4)
    dma("a", lambda e, T, c: [e.dma_start(T.oi[:, 0:64], T.sa[:]), e.dma_start(T.oi[:, 64:128], T.sb[:])], [], [("oi", 0, 128)], 8e4)
    dma("y", lambda e, T, c: [e.dma_start(T.s_p[:], T.p0[:])], [], [("s_p", 0, 2)], 40e4)
    dma("a", lambda e, T, c: [e.dma_start(T.ov[:, 128:192], T.lim[:])], [], [("ov", 128, 192)], 4e4)
    dma("y", lambda e, T, c: [e.dma_start(T.s_e[:], T.toll[:])], [], [("s_e", 0, 2)], 60e4)
    iota(("pci", 0, 1), [[0, 1]], 0, 1)
    iota(("iot", 0, 256), [[1, 256]])
    for k in (1, 2, 3):
        act(("iot", 256 * k, 256 * k + 256), ("iot", 0, 256), AF.Identity, bias=256.0 * k)
    for k in "lhpe":
        a2a(k)

    boost[0] = OPT["early"]
    P, PD, PM, PT, P0, PH, LA, LB, P16, RA, RB, PZ, MQ, PX, P7, WB = [("pcf", k, k + 1) for k in range(16)]
    ts(("pci", 1, 2), ("pci", 0, 1), 4, ALU.arith_shift_right)
    ts(("pci", 2, 3), ("pci", 0, 1), 15, ALU.bitwise_and)
    cp(("pcf", 0, 3), ("pci", 0, 3))
    ts(PT, PD, 16.0, ALU.mult, 15.0, ALU.add)
    ts(P0, PM, 0.0, ALU.is_equal)
    cp(("ou", 0, 128), ("oi", 0, 128))
    I128, I144 = ("iot", 0, 128), ("iot", 0, 144)
    ts(("t2f", 0, 144), I144, PT, ALU.is_equal, P0, ALU.mult)
    add("v", lambda g, T, c: g.vector.tensor_copy(T.w2[:, 0:V].indirect(T.ou[:, 0:64]), T.iot[:]),
        [("iot", 0, V), ("ou", 0, 64)], [("w2", 0, V)], (1, V * 3.8, 0, 0))
    add("s", lambda g, T, c: g.scalar.activation(T.w2[:, V:2 * V].indirect(T.ou[:, 64:128]), T.iot[:], AF.Silu),
        [("iot", 0, V), ("ou", 64, 128)], [("w2", V, 2 * V)], (22, V * 3.8, 0, 0))
    for k in range(2):
        for j in range(0, 16, 4):
            mm([(bk(7, 64, 64 * k), ("t2f", 15 - i, 143 - i), ("w2", k * V + i, k * V + V, 16), i == 0, i == 15) for i in range(j, j + 4)])
    cp(("ov", 0, 128), bk(7, 128))
    dma("y", lambda e, T, c: [e.dma_start(T.s_v[:], T.ov[:])], [("ov", 0, 192)], [("s_v", 0, 2)], 1e5)
    a2a("v")
    for k in range(2):
        ts(("idf", 128 * k, 128 * k + 128), I128, P, ALU.is_equal)
    for (nm, n, s) in (("idp", 192, 1.0), ("idn", 192, -1.0), ("id13", 160, 2.0 ** -13), ("id8", 144, 2.0 ** -8), ("id32", 128, 1.0 / 32)):
        mov("f", (nm, 0, n), ("idf", 0, n), scale=s)
    ts(("ihp", 0, 128), ("idp", 0, 128), 8192.0, ALU.mult)
    ts(("ihn", 0, 128), ("idp", 0, 128), -8192.0, ALU.mult)
    ts(("ih1", 0, 128), ("idp", 0, 128), 1.0, ALU.mult)
    ts(("t2v", 0, 144), I144, PT, ALU.is_equal, 1.0 / 17, ALU.mult)
    ts(PX, PM, 2.0, ALU.mult)
    ts(("cx", 0, 64), ("iot", 0, 64), 32.0, ALU.mult, PX, ALU.add)
    boost[0] = 0.0

    def keep(out, x, pattern, op, base, step=1, fill=0.0):
        add("g", lambda g, T, c: g.affine_select(A(T, out), A(T, x), pattern, op, fill, base, step), [x], [out], 170.0 + 2 * CY * n_(out))
    iota(("ones", 0, H), [[0, H]], 1)
    for k in range(4):
        keep(("xt", H * k, H * k + H), ("ones", 0, H), [[-1, 4], [-16, 8], [0, 16]], ALU.is_equal, -4 * k)
    boost[0] = OPT["early"]
    ts(RA, PM, 7.5, ALU.is_lt)
    ts(RB, PM, 7.5, ALU.is_gt)
    ts(P16, PD, 16.0, ALU.mult)
    ts(("ca", 0, 144), I144, PT, ALU.is_equal, RA, ALU.mult)
    ts(("cb", 0, 144), I144, PT, ALU.is_equal, RB, ALU.mult)
    for k in range(2):
        ts(("cl", 128 * k, 128 * k + 128), I128, P16, ALU.is_equal)
    ts(P7, PM, 7.0, ALU.is_equal)
    ts(WB, P7, 100.0, ALU.mult, -17.0, ALU.add)
    boost[0] = 0.0
    BS, BW, BL, BO, LA2, LB2, MA, MB, MA3, MB3, NA, NB, S8 = [("wk", 128 * k, 128 * k + 128) for k in range(13)]

    def by_half(tb, lo, hi):
        iota(tb, [[0, 8], [hi - lo, 2], [0, 8]], lo)

    def by_quarter(tb, even, odd):
        iota(tb, [[0, 16], [odd - even, 2], [0, 4]], even)

    def own_group(first, last):
        x, n = ("wk", first[1], last[2]), (last[2] - first[1]) // 128
        keep(x, x, [[0, n], [-16, 8], [0, 16]], ALU.is_ge, 0)
        keep(x, x, [[0, n], [16, 8], [0, 16]], ALU.is_ge, 15, step=-1)

    def row(tb, r):
        keep(tb, tb, [[-16, 8], [0, 16]], ALU.is_equal, -r)

    def paint(tb, r, value, part=0, parts=1):
        keep(tb, tb, [[-16, 8], [H, parts], [0, 16 // parts]], ALU.not_equal, -r - H * part, fill=value)

    by_half(BS, -2, 2)
    by_half(BW, 2, 0)
    by_half(BL, 0, 2)
    own_group(BS, BL)
    by_half(BO, 1, 1)
    by_quarter(LA2, -2, 0)
    by_quarter(LB2, 0, 2)
    own_group(BO, LB2)
    for tb in (MA, MB):
        by_half(tb, 16, 16)
        keep(tb, tb, [[-16, 8], [0, 2], [-2, 8]], ALU.is_equal, 0)
    keep(MA, MA, [[16, 8], [0, 16]], ALU.is_gt, 8, step=-1)
    keep(MB, MB, [[-16, 8], [0, 16]], ALU.is_ge, -8)
    for tb, even, odd in ((MA3, 16, 0), (MB3, 0, 16), (NA, 16, 0), (NB, 0, 16)):
        by_quarter(tb, even, odd)
        row(tb, 0)
    by_half(S8, -16, 16)
    row(S8, 0)
    for k in (0, 2):
        paint(MA3, 8, -16.0, k, 4)
        paint(MB3, 8, 16.0, k + 1, 4)
    for tb, lo, hi in ((MA, 1.0, -33.0), (MA3, -15.0, -49.0)):
        paint(tb, 7, lo, 0, 2)
        paint(tb, 7, hi, 1, 2)
    paint(NA, 7, -49.0)
    for k in (0, 2):
        paint(NA, 7, -15.0, k, 4)
    for tb in (MA, MA3, NA):
        paint(tb, 7, 128.0, 7, 16)

    boost[0] = 0.0
    dma("y", lambda e, T, c: [e.dma_start(T.li[:, 0:64], T.l_l[:, 0:64, :])], [("l_l", 0, 2)], [("li", 0, 64)], 32e3)
    dma("y", lambda e, T, c: [e.dma_start(T.li[:, 64:128], T.l_l[:, 64:128, :])], [("l_l", 0, 2)], [("li", 64, 128)], 32e3)
    dma("y", lambda e, T, c: [e.dma_start(T.hp[16:128, :], T.l_h[0:7]), e.dma_start(T.hp[0:16, :], T.l_h[7])], [("l_h", 0, 2)], [("hp", 0, V)], 26e4)
    dma("y", lambda e, T, c: [e.dma_start(T.pz[:], T.l_p[:])], [("l_p", 0, 2)], [("pz", 0, V)], 26e4)
    dma("y", lambda e, T, c: [e.dma_start(T.e0[:], T.l_e[:])], [("l_e", 0, 2)], [("e0", 0, V)], 26e4)
    dma("y", lambda e, T, c: [e.dma_start(T.vi[:], T.l_v[:])], [("l_v", 0, 2)], [("vi", 0, 192)], 1e5)
    cp(("lu", 0, 128), ("li", 0, 128))
    cp(("lf", 0, 128), ("li", 0, 128))
    mm([(bk(6, 128, 128 * (t - 1)), rot("idf", t), ("lf", 0, 128), True, True) for t in (1, 2, 3)])
    cp(("lu", 128, 512), bk(6, 384))

    def lst(nm, t, k, lo, hi):
        return (nm, 128 * t + 64 * k + lo // 16, 128 * t + 64 * k + hi // 16)

    def lane(nm, k, lo, hi):
        return (nm, 2 * lo + k, 2 * hi, 2)

    IP, IN = rot("idp", 0), rot("idn", 0)
    DEL, MID = 0.125, -511.5 / 8192
    for (lo, hi), (ba, bb) in zip(OPT["first"], ((0, 4), (1, 5), (2, 3))):
        mov(OPT["hie"][lo // 256], lane("hi", 0, lo, hi), ("hp", 0, V), idx=lst("lu", 0, 0, lo, hi))
        mov("v", lane("hi", 1, lo, hi), ("hp", 0, V), idx=lst("lu", 0, 1, lo, hi))
        passes(ba, lo, hi, [(rot("idp", 1), "hp", 0), (IN, "hi", 0, 2)])
        act(("da", lo, hi), bk(ba, hi - lo), AF.Abs)
        passes(bb, lo, hi, [(rot("idp", 1), "hp", 0), (IN, "hi", 1, 2)])
        act(("db", lo, hi), bk(bb, hi - lo), AF.Abs)
        passes(bb, lo, hi, [(IN, "da", 0), (IP, "db", 0)])
        mov(OPT["dde"], ("dd", lo, hi), bk(bb, hi - lo), bias=DEL)

    def with_edges(rnd):
        x = ("de", V * rnd, V * rnd + V)
        dma("y", lambda e, T, c: [e.dma_start(A(T, x), T.da[:])], [("da", 0, V)], [x], 26e4)
        dma_add(x, (("e0", "e1")[rnd], 0, V))
    with_edges(0)

    def turn(out, x, t):
        (o, a, b), (i, c_, d) = out, x
        dma("y", lambda e, T, c: [e.dma_start(T[o][0:128 - 16 * t, a:b], T[i][16 * t:128, c_:d]),
                                  e.dma_start(T[o][128 - 16 * t:128, a:b], T[i][0:16 * t, c_:d])], [x], [out], 256.0 * (b - a))
    for t in (1, 2, 3):
        for (lo, hi) in (HS if t == 1 else ((0, V),)):
            turn(("dd", V * t + lo, V * t + hi), ("dd", lo, hi), t)
    turn(("hab", 0, 2 * V), ("hi", 0, 2 * V), 3)

    C = OPT["c"]
    CH = ((0, C), (C, V))

    def halves(lo, hi):
        return [(max(lo, a), min(hi, b)) for (a, b) in HS if max(lo, a) < min(hi, b)]

    def behind(i, js):
        for j in js:
            ops[i]["deps"].setdefault(j, False)
        return i

    def votes(t, p, w, ix, z, late=False, mid=None):
        pw = (p, 0, V)
        for (lo, hi) in halves(z, V):
            passes(4 + lo // H, lo, hi, [(rot("idp", t), "dd", 0)])
            act(("gz", lo, hi), pw, AF.Identity, idx=lst("lu", t, 1, lo, hi))
        row = []
        for k, (lo, hi) in enumerate(CH):
            act(lane(w, 0, lo, hi), pw, AF.Identity, bias=DEL, idx=lst("lu", t, 0, lo, hi))
            if lo < z:
                m = min(hi, z)
                behind(tt(lane(w, 1, lo, m), pw, ("dd", V * t + lo, V * t + m), ALU.add, idx=lst("lu", t, 1, lo, m)), row[:1])
            for (a, b) in halves(max(lo, z), hi):
                behind(tt(lane(w, 1, a, b), bk(4 + a // H, b - a, a - max(z, a // H * H)), ("gz", a, b), ALU.add), row[:1])
            row.append(behind(tt(("lt", V * t + lo, V * t + hi), pw, lane(w, 1, lo, hi), ALU.is_gt, idx=lst("lu", t, 0, lo, hi)), row[1:]))
            n = (hi - lo) // 16
            mm([(bk(2 + k, n), ("ih1", 0, 128), ("cx", 0, n), True, False)]
               + [(bk(2 + k, n), ("t2v", 15 - i, 143 - i), ("lt", V * t + lo + i, V * t + hi, 16), False, i == 15) for i in range(16)])
            js = mid() if mid and k else []
            row.append(behind(ts((ix[0], ix[1] + lo // 16, ix[1] + hi // 16), bk(2 + k, n), 1.5 * 2 ** 23, ALU.add, 1.5 * 2 ** 23, ALU.subtract),
                              js if OPT["a0"] else []))
            if late:
                row.pop()

    def pick(w, ix, lo, hi):
        clo, chi = CH[0] if lo < C else CH[1]
        return (w, 2 * clo, 2 * chi), (ix[0], ix[1] + lo // 16, ix[1] + hi // 16)

    def step(t, p, w, ix, sel, out, op, op_r, S, Z, bias=0.0):
        def part(lo, hi):
            win, i = pick(w, ix, lo, hi)
            act((sel, lo, hi), win, AF.Identity, bias=bias, idx=i)
            return [tt((out, lo, hi), (PS[0], lo, hi), (sel, lo, hi), op_r)]
        if S < V:
            mov("s", ("uq", S, V), (PS[0], S, V))
        votes(t, p, w, ix, Z, mid=lambda: part(0, C))
        if S < V:
            win, i = pick(w, ix, S, V)
            tt((out, S, V), win, ("uq", S, V), op, idx=i)
            if C < S:
                part(C, S)
        else:
            part(C, 768)
            part(768, V)

    IX = ("ix", 0)
    for h in (1, 0):
        passes(h, H * h, H * h + H, [(rot("id8", 1), "hp", 0), (IP, "da", 0), (IP, "e0", 0)])
    step(0, "pz", "w2", ("ixb", 0), "nn", "pa", ALU.add, ALU.add, OPT["s0"], V)
    for (lo, hi) in CH:
        win, i = pick("w2", ("ixb", 0), lo, hi)
        mov("f", ("q16", lo, hi), win, bias=-128.0 - DEL, idx=i)

    cp(("vf", 0, 192), ("vi", 0, 192))
    mm([(bk(7, 128, 128 * (t - 1)), rot("idf", t), ("vf", 0, 128), True, True) for t in (1, 2, 3)]
       + [(bk(7, 64, 384), rot("idf", 3), ("vf", 128, 192), True, True)])
    cp(("zh", 0, 64), bk(7, 64, 384))
    tt(("zt", 0, 64), bk(7, 64, 384), ("zh", 0, 64), ALU.subtract)
    ts(("zl", 0, 64), ("zt", 0, 64), 0.9375, ALU.add)
    cp(("lv", 0, 384), bk(7, 384))
    U9 = ("u9", 0, 64)

    def forest(e, rnd, second, un):
        Z, S = OPT["z"][2 * rnd + second], OPT["s"][2 * rnd + second]
        for b, en, (lo, hi) in OPT["init"][second] if rnd or second else ():
            its = [(IP, "de", V * rnd), ("x", U9), ("x", un)] if second else [(IP, "da", 0), (IP, e, 0)]
            passes(b, lo, hi, [(rot("id8", 1), "hp", 0), (IP, "q16", 0)] + its)
            mov(en, ("pa", lo, hi), bk(b, hi - lo), bias=128.0)
        for (t, p, p2) in ((1, "pa", "pb"), (2, "pb", "pc")):
            for h in (1, 0):
                passes(h, H * h, H * h + H, ([(rot("idp", t), "de", V * rnd)] if second or t > 1 else [(rot("idp", t), "da", 0), (rot("idp", t), e, 0)])
                       + ([(rot("id13", 2), "hp", 0)] if t == 1 else []) + ([("x", ("mk", 64 * t - 64, 64 * t))] if second else []))
            step(t, p, "w1", IX, "nn", p2, ALU.add, ALU.add, S, Z)
        ix = ("ixb" if second else "ixa", 64 * rnd)
        if second:
            for (lo, hi) in HS:
                passes(4, lo, hi, [(BO, "lt", 2 * V)])
                act(("wt", lo, hi), bk(4), AF.Sign, bias=-8.5)
            votes(3, "pc", "w2", ix, Z, rnd == 0)
            boost[0] = OPT["due"][0] * (1 - rnd)
            for (lo, hi) in CH:
                win, i = pick("w2", ix, lo, hi)
                mov("f", ("nb", lo, hi), win, bias=MID, idx=i)
            boost[0] = 0.0
            return ix
        for h in (1, 0):
            passes(h, H * h, H * h + H, [(rot("idn", 3), "de", V * rnd), ("x", ("zh", 0, 64)), ("x", ("zl", 0, 64))])
        step(3, "pc", "w1", ix, "na", "wt", ALU.is_gt, ALU.is_lt, S, Z, MID)
        if S < V:
            win, i = pick("w1", ix, S, V)
            mov("f", ("na", S, V), win, bias=MID, idx=i)
        for b, (lo, hi) in zip((4, 5, 3), PIECES):
            passes(b, lo, hi, [(BL, "lt", 3 * V), (BW, "wt", 0)])
            act(("wr", lo, hi), bk(b, hi - lo), AF.Sign, bias=WB)
        return ix

    def walk(outs, parts, last_=False):
        second = len(outs) == 1
        for t in (3, 2, 1):
            b0 = V * (t - 1)
            win = ("ms", b0, b0 + V) if t < 3 else ("lt", 3 * V, 4 * V) if second else ("wr", 0, V)
            g0 = b0 + V * (t == 3 and second)
            for k, (lo, hi) in enumerate(parts):
                e = "f"
                mov(OPT["wg"][0], ("g0", g0 + lo, g0 + hi), win, idx=lst("lv", t - 1, 0, lo, hi))
                mov(OPT["wg"][1], ("g1", g0 + lo, g0 + hi), win, idx=lst("lv", t - 1, 1, lo, hi))
                js = range(lo // 64, hi // 64)
                if t > 1:
                    b = (((4, 5, 3), (0, 1, 3))[t - 2] if not last_ else (0, 1, 3))[k]
                    if t == 3 and second:
                        passes(b, lo, hi, [(NA, "g0", b0), (NB, "g1", b0), (S8, "wt", 0), (LA2, "g0", g0), (LB2, "g1", g0)])
                    else:
                        passes(b, lo, hi, [(BS, "lt", b0), ((MA, MA3)[t - 2], "g0", b0), ((MB, MB3)[t - 2], "g1", b0)])
                    sign(e, ("ms", b0 - V + lo, b0 - V + hi), bk(b, hi - lo))
                    mm([(bk(2, 64), ("cl", 128 - 16 * (t - 1) - j, 256 - 16 * (t - 1) - j), ("ms", b0 - V + 64 * j, b0 - V + 64 * j + 64),
                         t == 3 and j == 0, False) for j in js])
                else:
                    for (tb, nm) in (("ca", "g0"), ("cb", "g1")):
                        mm([(bk(2, 64), (tb, 15 - j, 143 - j), (nm, 64 * j, 64 * j + 64), False, j == 15 and nm == "g1") for j in js])
        for (u, x) in outs:
            ts(u, bk(2, 64), -41.0, ALU.is_gt, x, ALU.mult)

    pool = [[6, 7], 0]

    def nb_():
        pool[1] += 1
        return pool[0][pool[1] % len(pool[0])]

    M8 = 1.5 * 2 ** 20

    def strip(n, l, tp, base, parts, eng):
        for (lo, hi) in parts:
            b = bk(nb_(), hi - lo)
            if eng == "s":
                act(("rm", 0, hi - lo), (n, lo, hi), AF.Identity, bias=M8)
                act(b, ("rm", 0, hi - lo), AF.Identity, bias=-M8)
            else:
                ts(b, (n, lo, hi), M8, ALU.add, M8, ALU.subtract)
            tt((l, base + lo, base + hi), (n, lo, hi), b, ALU.subtract)
            ts((tp, base + lo, base + hi), (l, base + lo, base + hi), 8192.0, ALU.mult, 6160.0, ALU.add)

    def term(items, bias, half, lo, hi, out):
        k = nb_()
        b = bk(k, hi - lo)
        passes(k, lo, hi, items)
        act(b, b, AF.Abs, bias=bias)
        act(out or b, b, AF.Exp, bias=math.log(0.5) if half else 0.0, scale=-0.125)
        if not out:
            tt(("acc", lo, hi), b, ("acc", lo, hi), ALU.add)

    def picked(out, base, w, ix, scale=1.0):
        for (lo, hi) in CH:
            win, i = pick(w, ix, lo, hi)
            mov("f", (out, base + lo, base + hi), win, scale=scale, idx=i)

    nx = [0]

    def xbuf():
        nx[0] += 1
        return V * (nx[0] % 4)

    HP16, HN16, I32_ = ("ihp", 0, 128), ("ihn", 0, 128), ("id32", 0, 128)
    for k in range(2):
        for (lo, hi) in HS:
            b = nb_()
            passes(b, lo, hi, [(rot("idp", 3), ("da", "db")[k], 0)])
            act(lane("eb", k, lo, hi), bk(b), AF.Exp, bias=math.log(0.5), scale=-0.125)

    for rnd in (0, 1):
        e, a0 = ("e0", "e1")[rnd], V * rnd
        ua, ub, un = ("u4", 128 * rnd, 128 * rnd + 64), ("u4", 128 * rnd + 64, 128 * rnd + 128), ("un", 64 * rnd, 64 * rnd + 64)
        ixa = forest(e, rnd, False, None)
        walk([(ua, 4.0), (U9, 9.0)], (HS, PIECES)[OPT["wp"][2 * rnd]])
        send(lambda T, q, ua=ua, un=un: [((q - 1) % N, A(T, ua), A(T, un))], [ua], [un], 2500.0, one=True)
        boost[0] = OPT["due"][3 + rnd]
        strip("na", "la", "ta", a0, HS, OPT["strip"][2 * rnd])
        picked("fa", a0, "hab", ixa)
        if rnd == 0:
            picked("acc", 0, "eb", ixa, 2.0)
        else:
            x = xbuf()
            picked("xx", x, "eb", ixa, 2.0)
            dma_add(("acc", 0, V), ("xx", x, x + V))
        both = rnd or OPT["both"]
        if both:
            for (lo, hi) in HS:
                for k in range(2):
                    term([(IN, "hab", k, 2), (HP16, "la", a0), (IN, "ta", a0)], 6175.5, False, lo, hi, lane("xe", k, lo, hi))
                dma_add(("xe", 2 * lo, 2 * hi), ("eb", 2 * lo, 2 * hi))
        boost[0] = 0.0
        mm([(bk(3, 64, 64 * t - 64), rot("idp", t), u, u is U9, u is un) for t in (1, 2) for u in (U9, un)])
        mov("f", ("mk", 0, 128), bk(3, 128))
        ixb = forest(e, rnd, True, un)
        walk([(ub, -4.0)], (HS, PIECES)[OPT["wp"][2 * rnd + 1]], rnd == 1)
        terms = (([(HP16, "lb", 0), (IN, "tb", 0), (IN, "fa", a0)], 6175.5, True),
                 ([(I32_, "ta", a0), (HN16, "lb", 0), (IP, "tb", 0)], -6352.5, False),
                 ([(I32_, "tb", 0), (HN16, "la", a0), (IP, "ta", a0)], -6352.5, True))
        if rnd == 0:
            for h, (lo, hi) in enumerate(HS):
                passes(4 + h, lo, hi, [(IP, e, 0), ("x", ua), ("x", ub)])
                ts(("e1", lo, hi), bk(4 + h), 0.0, ALU.max, 63.0, ALU.min)
            dma("y", lambda e_, T, c: [e_.dma_start(T.s_t[:], T.e1[:])], [("e1", 0, V)], [("s_t", 0, 2)], 26e4)
            with_edges(1)
            a2a("t")
            dma("y", lambda e_, T, c: [e_.dma_start(T.en[:], T.l_t[:])], [("l_t", 0, 2)], [("en", 0, V)], 26e4)
            boost[0] = OPT["due"][1]
            strip("nb", "lb", "tb", 0, HS, OPT["strip"][1])
            boost[0] = OPT["due"][2]
            x = xbuf()
            picked("xx", x, "xe" if both else "eb", ixb)
            dma_add(("acc", 0, V), ("xx", x, x + V))
            if not both:
                picked("fb", 0, "hab", ixb)
                terms += (([(HP16, "la", 0), (IN, "ta", 0), (IN, "fb", 0)], 6175.5, False),)
            for (its, bias, half) in terms:
                x = xbuf()
                for (lo, hi) in HS:
                    term(its, bias, half, lo, hi, ("xx", x + lo, x + hi))
                dma_add(("acc", 0, V), ("xx", x, x + V))
            boost[0] = 0.0

    tt(("dl", 0, 64), ua, ub, ALU.add)
    dma("y", lambda e_, T, c: [e_.dma_start(T.s_d[:], T.dl[:])], [("dl", 0, 64)], [("s_d", 0, 2)], 16e3)
    a2a("d")
    dma("a", lambda e_, T, c: [e_.dma_start(T.dq[:], T.l_d[:])], [("l_d", 0, 2)], [("dq", 0, 64)], 16e3)
    for h, (lo, hi) in enumerate(HS):
        passes(h, lo, hi, [(IP, "en", 0), ("x", ("dq", 0, 64))])
        ts(("tf", lo, hi), bk(h), 0.0, ALU.max, 63.0, ALU.min)
        dma("a", lambda e_, T, c, lo=lo, hi=hi: [e_.dma_start(T.tollout[:, lo:hi], T.tf[:, lo:hi])], [("tf", lo, hi)], [], 26e4)

    def home(e_, T, q, s, l, cols):
        r = [e_.dma_start(T.gain[16 * q:16 * q + 16, cols], T[s][q])]
        if q > 0:
            r.append(e_.dma_start(T.gain[0:16 * q, cols], T[l][0:q]))
        if q < N - 1:
            r.append(e_.dma_start(T.gain[16 * q + 16:128, cols], T[l][q + 1:N]))
        return r
    strip("nb", "lb", "tb", 0, OPT["parts"], OPT["strip"][3])
    pool[0] = OPT["pool"]
    for k, (lo, hi) in enumerate(OPT["parts"]):
        for (a, b) in ((lo, min(hi, C)), (max(lo, C), hi)):
            if a < b:
                win, i = pick("xe", ixb, a, b)
                tt(("acc", a, b), win, ("acc", a, b), ALU.add, idx=i)
        npe = OPT["pe"][k]
        sumb = bk(OPT["sumb"][k], hi - lo)
        for n, (its, bias, half) in enumerate(terms):
            if n < npe:
                x = ("xx", V * n + lo, V * n + hi)
                term(its, bias, half, lo, hi, x)
                mm([(sumb, rot("idf", 0), x, n == 0, n == npe - 1)])
                if n == npe - 1:
                    tt(("acc", lo, hi), sumb, ("acc", lo, hi), ALU.add)
            else:
                term(its, bias, half, lo, hi, None)
    for k, (lo, hi) in enumerate(TAIL):
        sg, lg, nby = "s_g%d" % k, "l_g%d" % k, 512.0 * (hi - lo)
        dma("y", lambda e_, T, c, sg=sg, lo=lo, hi=hi: [e_.dma_start(T[sg][:], T.acc[:, lo:hi])], [("acc", lo, hi)], [(sg, 0, 2)], nby)
        a2a("g%d" % k, own=False)
        dma("y", lambda e_, T, c, sg=sg, lg=lg, lo=lo, hi=hi: home(e_, T, c["q"], sg, lg, slice(lo, hi)), [(sg, 0, 2), (lg, 0, 1)], [], nby)
    return ops


def queue_of(o):
    return "s" if o["eng"] == "a" else o["eng"]


def schedule(ops, turns=0):
    n = len(ops)
    pre = [list(o["deps"].items()) + ([(o["from"], True)] if o["kind"] == "a" else []) for o in ops]
    post = [[] for _ in ops]
    for i in range(n):
        for j, w in pre[i]:
            post[j].append(i)
    ways = [[w[0] for w in o["ways"]] if "ways" in o else [queue_of(o)] for o in ops]
    figs = []
    for (fix, cy, gam, pec, lat, slow) in FIGURES:
        figs.append(([price(o["vec"], fix, cy, gam, pec) + 0.01 for o in ops],
                     [[(j, ops[j]["lat"] * slow + lat if w else 0.0) for j, w in p] for p in pre], [o["lat"] * slow for o in ops]))
    cost, gaps, tail = figs[0]
    way = [ops[i]["lat"] + ops[i]["boost"] for i in range(n)]
    for i in range(n - 1, -1, -1):
        way[i] += cost[i]
        for j, d in gaps[i]:
            way[j] = max(way[j], way[i] + d)

    def place(shift):
        w = [0.0] * n
        for i in range(n - 1, -1, -1):
            x = way[i] + shift[i]
            for k in post[i]:
                if w[k] + 0.01 > x:
                    x = w[k] + 0.01
            w[i] = x
        end, queue = [0.0] * n, [None] * n
        rows = {q: ([], []) for q in "vspgy"}
        for i in sorted(range(n), key=lambda k: -w[k]):
            ready, c, best = 0.0, cost[i], None
            for j, d in gaps[i]:
                if end[j] + d > ready:
                    ready = end[j] + d
            for q in ways[i]:
                s, k = ready, 0
                if q:
                    a, b = rows[q]
                    k = len(a)
                    while k and b[k - 1] > ready:
                        k -= 1
                    while k < len(a) and a[k] < s + c:
                        s = b[k]
                        k += 1
                if best is None or s < best[0]:
                    best = (s, k, q)
            s, k, queue[i] = best
            end[i] = s + c
            if queue[i]:
                rows[queue[i]][0].insert(k, s)
                rows[queue[i]][1].insert(k, s + c)
        order = sorted(range(n), key=lambda k: end[k] - cost[k])
        total, ends = 0.0, []
        for f, (cs, gp, tl) in enumerate(figs):
            e, free, last = [0.0] * n, dict.fromkeys("vspgy", 0.0), 0.0
            for i in order:
                q = queue[i]
                s = free[q] if q else 0.0
                for j, d in gp[i]:
                    if e[j] + d > s:
                        s = e[j] + d
                e[i] = s = s + cs[i]
                if q:
                    free[q] = s
                if s + tl[i] > last:
                    last = s + tl[i]
            total += math.log(last)
            ends.append(e)
        return total, order, queue, end, w, ends

    def held_up(plan):
        total, order, queue, end, w, ends = plan
        before, seen = {}, {}
        for i in order:
            before[i], seen[queue[i]] = seen.get(queue[i]), i
        pairs = []
        for (cs, gp, tl), e in zip(figs, ends):
            i = max(range(n), key=lambda k: e[k] + tl[k])
            while i is not None:
                nxt = [j for j, d in gp[i] if abs(e[j] + d + cs[i] - e[i]) < 1e-3]
                if not nxt and queue[i] and before[i] is not None:
                    pairs.append((i, before[i]))
                    nxt = [before[i]]
                i = nxt[0] if nxt else None
        return pairs

    shift = [0.0] * n
    best = place(shift)
    pairs = held_up(best)
    x = 1
    for turn in range(turns):
        x = (x * 1103515245 + 12345) % 2 ** 31
        trial = list(shift)
        if turn % 2 and pairs:
            i, j = pairs[(x >> 8) % len(pairs)]
            by = max(best[4][j] - best[4][i], 0.0) + (1.0, 300.0, 1000.0, 3000.0)[x >> 4 & 3]
            if x >> 6 & 1:
                trial[i] += by
            else:
                trial[j] -= by
        else:
            at, width, by = (x >> 8) % n, (1, 3, 10, 30)[x >> 6 & 3], (300.0, 1500.0, 6000.0, -300.0, -1500.0, -6000.0, 700.0, -700.0)[x >> 3 & 7]
            for i in range(at, min(n, at + width)):
                trial[i] += by
        plan = place(trial)
        if plan[0] <= best[0]:
            best, shift = plan, trial
            pairs = held_up(best)
    total, order, queue, end = best[:4]
    for i, o in enumerate(ops):
        for eng, fn, vec in o.get("ways", ()):
            if eng == queue[i]:
                o["eng"], o["fn"] = eng, fn
    return order, [end[i] - cost[i] for i in range(n)], [end[i] + tail[i] for i in range(n)]


PLAN = {}


def rank_program(g, core, T, topo):
    q = T.rank_of(core)
    if q is None:
        return
    if not PLAN:
        PLAN["ops"] = build()
        PLAN["order"] = schedule(PLAN["ops"], OPT["turns"])[0]
    ops, order = PLAN["ops"], PLAN["order"]
    c = dict(q=q, core=core, topo=topo)
    qs = {"v": g.vector, "s": g.scalar, "p": g.tensor, "g": g, "y": g.sync}
    csem = {"v": "cv", "s": "cs", "p": "cp", "g": "cg"}
    cnt = {}
    tok = {}
    seen = {k: {} for k in qs}
    know = {}

    def wait(qn, j):
        s, v = tok[j]
        if seen[qn].get(s, 0) < v:
            qs[qn].wait_ge(T.sem[s], v)
            seen[qn][s] = v
            for (s2, v2) in know[j].items():
                if seen[qn].get(s2, 0) < v2:
                    seen[qn][s2] = v2

    for i in order:
        o = ops[i]
        if o["kind"] == "a":
            nb = T.cores[(q + 1) % N]
            tok[i] = (o["sem"], len(topo.engines(nb, core)) if o["one"] else N - 1)
            know[i] = {}
            continue
        qn = queue_of(o)
        for j in sorted((j for j, w in o["deps"].items() if w), reverse=True):
            wait(qn, j)
        know[i] = dict(seen[qn])
        if o["kind"] == "c":
            s = csem[qn]
            cnt[s] = cnt.get(s, 0) + 1
            o["fn"](g, T, c).then_inc(T.sem[s], 1)
            tok[i] = (s, cnt[s])
        elif o["kind"] == "d":
            ins = o["fn"](qs[qn], T, c)
            for x in ins:
                x.then_inc(T.sem[o["sem"]], 16)
            tok[i] = (o["sem"], 16 * len(ins))
        else:
            tok[i] = (o["sem"], o["fn"](g, T, c))
    fin = {}
    for i in order:
        s, v = tok[i]
        if v >= fin.get(s, (0, 0))[0]:
            fin[s] = (v, i)
    for i in order:
        s, v = tok[i]
        if fin[s][1] == i and all(seen[k].get(s, 0) < v for k in seen):
            wait("g", i)
